import numpy as np
import ml_dtypes


def mxq(x, axis, fmt="e4m3"):
    dtype, down = {"e4m3": (ml_dtypes.float8_e4m3fn, 7), "e5m2": (ml_dtypes.float8_e5m2, 14)}[fmt]
    v = np.moveaxis(np.asarray(x, np.float32).astype(ml_dtypes.bfloat16).astype(np.float64), axis, -1)
    blocks = v.reshape(v.shape[:-1] + (-1, 32))
    amax = np.abs(blocks).max(-1, keepdims=True)
    byte = np.maximum(np.where(amax > 0, np.frexp(amax)[1] - 1 + 127, 0) - down, 1)
    scale = np.exp2(byte - 127.0)
    codes = (blocks / scale).astype(np.float32).astype(dtype).astype(np.float64)
    return np.moveaxis((codes * scale).reshape(v.shape), -1, axis)


WIDE = False


def mx_kscale(k):
    if not WIDE:
        return np.ones(k)
    levels = np.array([10, -10, 5, -5, 0])
    if k % 512:
        return np.exp2(np.random.permutation(np.resize(levels, k // 32))).repeat(32)
    a = np.empty((k // 512, 16))
    for p in range(k // 512):
        a[p, :8] = np.random.permutation(np.resize(levels, 8))
        for g in range(8):
            far = levels[np.abs(levels - a[p, g]) >= 10]
            a[p, g + 8] = far[np.random.randint(len(far))]
    return np.exp2(a.ravel()).repeat(32)


def f64(x):
    return np.asarray(x).astype(np.float64)


def striped(idx):
    return np.tile(idx.reshape(-1, 16).T, (8, 1)).astype(np.uint16)


def unstriped(offs):
    return offs[:16].T.reshape(-1).astype(np.int64)


E2M1 = np.array([0.0, 0.5, 1.0, 1.5, 2.0, 3.0, 4.0, 6.0, -0.0, -0.5, -1.0, -1.5, -2.0, -3.0, -4.0, -6.0])


def pack_weight(w, fmt):
    k, n = w.shape
    w = f64(np.asarray(w, np.float32).astype(ml_dtypes.bfloat16)).reshape(k // 32, 32, n)
    amax = np.abs(w).max(1)
    if fmt == "e4m3":
        byte = np.frexp(amax)[1] - 1 + 127 - 7
    else:
        mant, ex = np.frexp(amax / 6.0)
        byte = np.where(mant > 0.5, ex, ex - 1) + 127
    byte = np.clip(np.where(amax > 0, byte, 1), 1, 254)
    scaled = (w * np.exp2(127.0 - byte)[:, None, :]).reshape(k, n).astype(np.float32)
    by_word = np.ascontiguousarray(scaled.reshape(k // 512, 128, 4, n).transpose(0, 1, 3, 2))
    if fmt == "e4m3":
        words = by_word.astype(ml_dtypes.float8_e4m3fn).view(np.uint8)
    else:
        c = by_word.astype(ml_dtypes.float4_e2m1fn).view(np.uint8) & 0xF
        words = (c[..., 0::2] | (c[..., 1::2] << 4)).reshape(k // 512, 128, 2 * n)
    return np.ascontiguousarray(words), np.ascontiguousarray(byte.astype(np.uint8).reshape(k // 512, 16, n))


def unpack_weight(words, scales, fmt):
    g, _, n = scales.shape
    words = np.ascontiguousarray(words).reshape(g, 128, n, -1)
    if fmt == "e4m3":
        vals = words.view(ml_dtypes.float8_e4m3fn).astype(np.float64)
    else:
        nib = np.empty((g, 128, n, 4), np.uint8)
        nib[..., 0::2] = words & 0xF
        nib[..., 1::2] = words >> 4
        vals = E2M1[nib]
    vals = vals * np.repeat(np.exp2(scales.astype(np.float64) - 127.0), 8, axis=1)[..., None]
    return vals.transpose(0, 1, 3, 2).reshape(g * 512, n)


def gelu(v):
    return 0.5 * v * (1.0 + np.tanh(np.sqrt(2.0 / np.pi) * (v + 0.044715 * v**3)))


K, T, E, C, N = 2048, 640, 10, 128, 128


def by_expert(wq, xq):
    return np.concatenate([wq[e].T @ xq[:, e * C:(e + 1) * C] for e in range(E)], axis=1)


def setup_inputs():
    n = np.random.standard_normal
    s = mx_kscale(K)[:, None]
    first = np.random.permutation(np.repeat(np.arange(E), T // E))
    second = (first + 1 + np.random.permutation(np.repeat(np.arange(E - 1), -(-T // (E - 1)))[:T])) % E
    while np.bincount(second, minlength=E).max() != T // E:
        load = np.bincount(second, minlength=E); hi, lo = int(load.argmax()), int(load.argmin())
        t = np.flatnonzero((second == hi) & (first != lo))[0]; second[t] = lo
    slot_token = np.empty(E * C, np.int64); pos = np.empty((2, T), np.int64); fill = np.zeros(E, np.int64)
    place = np.stack([np.random.permutation(C) for _ in range(E)])
    for r, deal in enumerate((first, second)):
        for t in np.random.permutation(T):
            e = deal[t]; j = e * C + place[e, fill[e]]; fill[e] += 1; slot_token[j] = t; pos[r, t] = j
    g = np.random.uniform(0.2, 0.8, T)
    w = [pack_weight(m, "e2m1") for m in n((E + 1, K, N)) / np.sqrt(K) / s[None]]
    return {
        "xT": (n((K, T)) * s).astype(np.float32),
        "w_words": np.stack([m[0] for m in w]),
        "w_scales": np.stack([m[1] for m in w]),
        "b": (0.3 * n((N, E + 1))).astype(np.float32),
        "gate": np.stack([np.tile(g, (N, 1)), np.tile(1.0 - g, (N, 1))]).astype(np.float32),
        "offs": striped(slot_token),
        "pos1": striped(pos[0]),
        "pos2": striped(pos[1]),
    }


def reference(xT, w_words, w_scales, b, gate, offs, pos1, pos2):
    idx = unstriped(offs)
    w = np.stack([unpack_weight(w_words[e], w_scales[e], "e2m1") for e in range(E + 1)])
    wq = w
    xs = mxq(f64(xT), 0, "e4m3")
    ys = gelu((wq[E].T @ xs) + f64(b)[:, E:])
    xq = mxq(f64(xT)[:, idx], 0, "e4m3")
    y = by_expert(w, xq)
    y = gelu(y + np.repeat(f64(b)[:, :E], C, axis=1))
    return ys + f64(gate[0]) * y[:, unstriped(pos1)] + f64(gate[1]) * y[:, unstriped(pos2)]

@@ -1,0 +1,226 @@
+from contextlib import ExitStack
+
+import concourse.mybir as mybir
+
+K, T, E, C, N = 2048, 640, 10, 128, 128
+S = E * C
+P = 128
+PASSES = 4
+FLOPS = 2 * K * N * (S + T)
+
+F32 = mybir.dt.float32
+BF16 = mybir.dt.bfloat16
+U32 = mybir.dt.uint32
+I32 = mybir.dt.int32
+U16 = mybir.dt.uint16
+U8 = mybir.dt.uint8
+FP8X4 = mybir.dt.float8_e4m3fn_x4
+FP4X4 = mybir.dt.float4_e2m1fn_x4
+GELU = mybir.ActivationFunctionType.Gelu_apprx_tanh
+MULT = mybir.AluOpType.mult
+
+NARROW = [((0, 480), [(0, 256)]), ((480, 480), [(256, 512)]), ((960, 320), [(768, 512)])]
+WIDE = [((0, 640), [(0, 512)]), ((640, 640), [(512, 512), (1024, 256)])]
+LAST = [((0, 480), [(0, 256)]), ((480, 480), [(256, 512)]), ((960, 192), [(768, 256), (1024, 128)]), ((1152, 128), [(1152, 128)])]
+PIECES = [NARROW, WIDE, WIDE, LAST]
+
+
+def tile_moe_shr_lin_gelu_kernel(tc, xT, w_words, w_scales, b, gate, offs, pos1, pos2, out):
+    nc = tc.nc
+    with ExitStack() as ctx:
+        keep = ctx.enter_context(tc.tile_pool(name="keep", bufs=1))
+        ring = ctx.enter_context(tc.tile_pool(name="ring", bufs=2))
+        psum = ctx.enter_context(tc.psum_pool(name="psum", bufs=1))
+
+        offs_t = keep.tile([P, S // 16], U16, name="offs_t")
+        pos1_t = keep.tile([P, T // 16], U16, name="pos1_t")
+        pos2_t = keep.tile([P, T // 16], U16, name="pos2_t")
+        bias = keep.tile([P, E + 1], F32, name="bias")
+        gates = keep.tile([P, 2 * T], F32, name="gates")
+        wsc = keep.tile([P, (E + 1) * PASSES * N], U8, name="wsc", align_bytes=64)
+        warm = keep.tile([P, 8], F32, name="warm")
+        y = keep.tile([P, S], F32, name="y")
+        ys = keep.tile([P, T], F32, name="ys")
+        words, gath, slots, shq, cs, ss, csh, ssh = [], [], [], [], [], [], [], []
+        for a in range(PASSES):
+            words.append(keep.tile([P, (E + 1) * 2 * N], U8, name=f"words{a}", align_bytes=64))
+            gath.append(keep.tile([P, 4 * S], BF16, name=f"gath{a}", align_bytes=64))
+            slots.append(keep.tile([P, 4 * S], BF16, name=f"slots{a}", align_bytes=64))
+            shq.append(keep.tile([P, 4 * 512], BF16, name=f"shq{a}", align_bytes=64))
+            cs.append(keep.tile([P, S], U32, name=f"cs{a}", align_bytes=64))
+            ss.append(keep.tile([P, S], U8, name=f"ss{a}", align_bytes=64))
+            csh.append(keep.tile([P, 512], U32, name=f"csh{a}", align_bytes=64))
+            ssh.append(keep.tile([P, 512], U8, name=f"ssh{a}", align_bytes=64))
+        rest = keep.tile([P, PASSES * 4 * C], BF16, name="rest", align_bytes=64)
+        crest = keep.tile([P, PASSES * C], U32, name="crest", align_bytes=64)
+        srest = keep.tile([P, PASSES * C], U8, name="srest", align_bytes=64)
+
+        pairs_all = keep.tile([P, PASSES * 4 * T], BF16, name="pairs_all", align_bytes=64)
+        pairs = [pairs_all[:, 4 * T * (PASSES - 1 - a) : 4 * T * (PASSES - a)] for a in range(PASSES)]
+
+        xv = xT.rearrange("(a p j) t -> a p j t", p=P, j=4)
+        wv = w_words.bitcast(I32)
+        sv = w_scales.bitcast(I32)
+
+        nc.vector.memset(warm[:], 0.0)
+        nc.scalar.activation(out=warm[:], in_=warm[:], func=GELU)
+        nc.vector.memset(wsc[:].bitcast(I32), 0)
+
+        raw = {}
+
+        def load_x(a, h):
+            raw[a, h] = ring.tile([P, 2, T], F32, name=f"raw{h}")
+            nc.sync.dma_start(raw[a, h][:], xv[a][:, 2 * h : 2 * h + 2, :])
+
+        def load_w(a):
+            nc.sync.dma_start(
+                words[a][:].bitcast(I32).rearrange("p (e n) -> p e n", e=E + 1),
+                wv[:, a, :, :].rearrange("e p n -> p e n"),
+            )
+
+        load_x(0, 0)
+        nc.sync.dma_start(offs_t[:], offs)
+        load_x(0, 1)
+        load_x(1, 0)
+        load_x(1, 1)
+
+        def load_rest():
+            load_x(2, 0)
+            load_x(2, 1)
+            for q in range(4):
+                nc.sync.dma_start(
+                    wsc[32 * q : 32 * q + 4, :].bitcast(I32).rearrange("q (i n) -> q i n", n=N // 4),
+                    sv[:, :, 4 * q : 4 * q + 4, :].rearrange("e a q n -> q (e a) n"),
+                )
+            load_w(0)
+            load_x(3, 0)
+            load_x(3, 1)
+            load_w(1)
+            load_w(2)
+            load_w(3)
+            nc.sync.dma_start(bias[:], b)
+            nc.sync.dma_start(pos1_t[:], pos1)
+            nc.sync.dma_start(pos2_t[:], pos2)
+            nc.sync.dma_start(gates[:].rearrange("p (g t) -> p g t", g=2), gate.rearrange("g p t -> p g t"))
+
+        def cast(a, h, c0=0, c1=T, copy=nc.scalar.copy):
+            copy(
+                out=pairs[a][:, 2 * T * h : 2 * T * (h + 1)].rearrange("p (t e) -> p t e", e=2)[:, c0:c1, :],
+                in_=raw[a, h][:, :, c0:c1].rearrange("p e t -> p t e"),
+            )
+
+        def gather(a, h, start, size):
+            window = 2 * T * (PASSES - 1 - a) + T * h
+            nc.vector.tensor_copy(
+                gath[a][:].bitcast(U32)[:, S * h + start : S * h + start + size],
+                pairs_all[:].bitcast(U32)[:, window : window + (T if size < T else 2 * T)].indirect(offs_t[:, start // 16 : (start + size) // 16]),
+            )
+
+        def weave(a, start, size):
+            nc.scalar.copy(
+                out=slots[a][:].bitcast(U32).rearrange("p (n u) -> p n u", u=2)[:, start : start + size, :],
+                in_=gath[a][:].bitcast(U32).rearrange("p (u n) -> p n u", u=2)[:, start : start + size, :],
+            )
+
+        def weave_shared(a):
+            src = pairs[a].bitcast(U32).rearrange("p (u n) -> p n u", u=2)
+            nc.scalar.copy(out=shq[a][:].bitcast(U32).rearrange("p (n u) -> p n u", u=2), in_=src[:, :512, :])
+            nc.scalar.copy(
+                out=rest[:].bitcast(U32)[:, 2 * C * a : 2 * C * (a + 1)].rearrange("p (n u) -> p n u", u=2), in_=src[:, 512:, :]
+            )
+
+        def quant(a, cuts):
+            for s0, w in cuts:
+                nc.vector.quantize_mx(
+                    out=cs[a][:, s0 : s0 + w].bitcast(FP8X4),
+                    scales=ss[a][:, s0 : s0 + w],
+                    in_=slots[a][:, 4 * s0 : 4 * (s0 + w)],
+                )
+
+        def quant_shared(a):
+            nc.vector.quantize_mx(out=csh[a][:].bitcast(FP8X4), scales=ssh[a][:], in_=shq[a][:])
+
+        def quant_rest():
+            nc.vector.quantize_mx(out=crest[:].bitcast(FP8X4), scales=srest[:], in_=rest[:])
+
+        def multiply(bank, e, codes, scales, s0, w):
+            for a in range(PASSES):
+                i = e * PASSES + a
+                nc.tensor.matmul_mx(
+                    out=bank,
+                    lhsT=words[a][:, e * 2 * N : (e + 1) * 2 * N].bitcast(FP4X4),
+                    lhsT_scale=wsc[:, i * N : (i + 1) * N],
+                    rhs=codes(a)[:, s0(a) : s0(a) + w].bitcast(FP8X4),
+                    rhs_scale=scales(a)[:, s0(a) : s0(a) + w],
+                    start=(a == 0),
+                    stop=(a == PASSES - 1),
+                )
+
+        banks = {}
+
+        def bank_of(e):
+            key = e if e > 5 else e // 2
+            if key not in banks:
+                banks[key] = psum.tile([P, 3 * C if key == 0 else 2 * C if key < 3 else C], F32, name=f"bank{key}")
+            at = e % 2 * C if key < 3 else 0
+            return banks[key][:, at : at + C]
+
+        def experts(group):
+            for e in group:
+                multiply(bank_of(e), e, lambda a: cs[a], lambda a: ss[a], lambda a: e * C, C)
+            for e in group:
+                nc.scalar.activation(out=y[:, e * C : (e + 1) * C], in_=bank_of(e), func=GELU, bias=bias[:, e : e + 1])
+
+        def shared():
+            bank = psum.tile([P, 512], F32, name="bank_shared")
+            multiply(bank[:], E, lambda a: csh[a], lambda a: ssh[a], lambda a: 0, 512)
+            nc.scalar.activation(out=ys[:, :512], in_=bank[:], func=GELU, bias=bias[:, E : E + 1])
+            bank_rest = banks[0][:, 2 * C :]
+            multiply(bank_rest, E, lambda a: crest, lambda a: srest, lambda a: a * C, C)
+            nc.scalar.activation(out=ys[:, 512:], in_=bank_rest, func=GELU, bias=bias[:, E : E + 1])
+
+        cast(0, 0, 0, 384, nc.vector.tensor_copy)
+        cast(0, 0, 384, T)
+        cast(0, 1)
+        cast(1, 0)
+        cast(1, 1)
+        load_rest()
+        pending = []
+
+        def finish(a, cuts):
+            quant(a, cuts)
+            if a == PASSES - 1:
+                for s0, w in cuts:
+                    experts(range(s0 // C, (s0 + w) // C))
+
+        for a in range(PASSES):
+            if 0 < a < PASSES - 1:
+                cast(a + 1, 0)
+                cast(a + 1, 1)
+            for i, ((start, size), cuts) in enumerate(PIECES[a]):
+                gather(a, 0, start, size)
+                gather(a, 1, start, size)
+                weave(a, start, size)
+                if pending:
+                    finish(*pending.pop())
+                pending.append((a, cuts))
+                if i == min(len(PIECES[a]) - 1, 2):
+                    weave_shared(a)
+        finish(*pending.pop())
+        for a in range(PASSES):
+            quant_shared(a)
+        quant_rest()
+        shared()
+
+        s1 = keep.tile([P, T], F32, name="s1")
+        s2 = keep.tile([P, T], F32, name="s2")
+        t1 = keep.tile([P, T], F32, name="t1")
+        res = keep.tile([P, T], F32, name="res")
+        nc.vector.tensor_tensor(s1[:], y[:].indirect(pos1_t[:]), gates[:, :T], MULT)
+        nc.vector.tensor_tensor(s2[:], y[:].indirect(pos2_t[:]), gates[:, T:], MULT)
+        parts = (slice(0, 384), slice(384, T))
+        for cols in parts:
+            nc.vector.tensor_add(t1[:, cols], s1[:, cols], ys[:, cols])
+        for cols in parts:
+            nc.vector.tensor_add(res[:, cols], t1[:, cols], s2[:, cols])
+            nc.sync.dma_start(out[:, cols], res[:, cols])

@@ -6,6 +6,11 @@ K, T, E, C, N = 2048, 640, 10, 128, 128
 S = E * C
 P = 128
 PASSES = 4
+ROWS = 2 * PASSES
+WINDOW = 1712
+LAST = PASSES - 1
+PIECES = ((0, 512), (512, 1024), (1024, S))
+LATE = 3
 FLOPS = 2 * K * N * (S + T)
 
 F32 = mybir.dt.float32
@@ -18,11 +23,6 @@ FP8X4 = mybir.dt.float8_e4m3fn_x4
 FP4X4 = mybir.dt.float4_e2m1fn_x4
 GELU = mybir.ActivationFunctionType.Gelu_apprx_tanh
 MULT = mybir.AluOpType.mult
-
-NARROW = [((0, 480), [(0, 256)]), ((480, 480), [(256, 512)]), ((960, 320), [(768, 512)])]
-WIDE = [((0, 640), [(0, 512)]), ((640, 640), [(512, 512), (1024, 256)])]
-LAST = [((0, 480), [(0, 256)]), ((480, 480), [(256, 512)]), ((960, 192), [(768, 256), (1024, 128)]), ((1152, 128), [(1152, 128)])]
-PIECES = [NARROW, WIDE, WIDE, LAST]
 
 
 def tile_moe_shr_lin_gelu_kernel(tc, xT, w_words, w_scales, b, gate, offs, pos1, pos2, out):
@@ -41,22 +41,20 @@ def tile_moe_shr_lin_gelu_kernel(tc, xT, w_words, w_scales, b, gate, offs, pos1,
         warm = keep.tile([P, 8], F32, name="warm")
         y = keep.tile([P, S], F32, name="y")
         ys = keep.tile([P, T], F32, name="ys")
-        words, gath, slots, shq, cs, ss, csh, ssh = [], [], [], [], [], [], [], []
+        words = []
         for a in range(PASSES):
             words.append(keep.tile([P, (E + 1) * 2 * N], U8, name=f"words{a}", align_bytes=64))
-            gath.append(keep.tile([P, 4 * S], BF16, name=f"gath{a}", align_bytes=64))
-            slots.append(keep.tile([P, 4 * S], BF16, name=f"slots{a}", align_bytes=64))
-            shq.append(keep.tile([P, 4 * 512], BF16, name=f"shq{a}", align_bytes=64))
-            cs.append(keep.tile([P, S], U32, name=f"cs{a}", align_bytes=64))
-            ss.append(keep.tile([P, S], U8, name=f"ss{a}", align_bytes=64))
-            csh.append(keep.tile([P, 512], U32, name=f"csh{a}", align_bytes=64))
-            ssh.append(keep.tile([P, 512], U8, name=f"ssh{a}", align_bytes=64))
-        rest = keep.tile([P, PASSES * 4 * C], BF16, name="rest", align_bytes=64)
-        crest = keep.tile([P, PASSES * C], U32, name="crest", align_bytes=64)
-        srest = keep.tile([P, PASSES * C], U8, name="srest", align_bytes=64)
+        slots = keep.tile([P, PASSES * 4 * S], BF16, name="slots", align_bytes=64)
+        cs = keep.tile([P, PASSES * S], U32, name="cs", align_bytes=64)
+        ss = keep.tile([P, PASSES * S], U8, name="ss", align_bytes=64)
+        shq = keep.tile([P, PASSES * 4 * T], BF16, name="shq", align_bytes=64)
+        csh = {}
+        ssh = keep.tile([P, PASSES * T], U8, name="ssh", align_bytes=64)
 
-        pairs_all = keep.tile([P, PASSES * 4 * T], BF16, name="pairs_all", align_bytes=64)
-        pairs = [pairs_all[:, 4 * T * (PASSES - 1 - a) : 4 * T * (PASSES - a)] for a in range(PASSES)]
+        pairs = keep.tile([P, 2 * ((ROWS - 1) * T + WINDOW)], BF16, name="pairs", align_bytes=64)
+
+        def row_at(a, h):
+            return T * (2 * (PASSES - 1 - a) + h)
 
         xv = xT.rearrange("(a p j) t -> a p j t", p=P, j=4)
         wv = w_words.bitcast(I32)
@@ -64,6 +62,7 @@ def tile_moe_shr_lin_gelu_kernel(tc, xT, w_words, w_scales, b, gate, offs, pos1,
 
         nc.vector.memset(warm[:], 0.0)
         nc.scalar.activation(out=warm[:], in_=warm[:], func=GELU)
+        nc.vector.memset(pairs[:].bitcast(I32)[:, ROWS * T :], 0)
         nc.vector.memset(wsc[:].bitcast(I32), 0)
 
         raw = {}
@@ -72,145 +71,158 @@ def tile_moe_shr_lin_gelu_kernel(tc, xT, w_words, w_scales, b, gate, offs, pos1,
             raw[a, h] = ring.tile([P, 2, T], F32, name=f"raw{h}")
             nc.sync.dma_start(raw[a, h][:], xv[a][:, 2 * h : 2 * h + 2, :])
 
-        def load_w(a):
-            nc.sync.dma_start(
-                words[a][:].bitcast(I32).rearrange("p (e n) -> p e n", e=E + 1),
-                wv[:, a, :, :].rearrange("e p n -> p e n"),
-            )
-
-        load_x(0, 0)
-        nc.sync.dma_start(offs_t[:], offs)
-        load_x(0, 1)
-        load_x(1, 0)
-        load_x(1, 1)
-
         def load_rest():
-            load_x(2, 0)
-            load_x(2, 1)
             for q in range(4):
                 nc.sync.dma_start(
                     wsc[32 * q : 32 * q + 4, :].bitcast(I32).rearrange("q (i n) -> q i n", n=N // 4),
                     sv[:, :, 4 * q : 4 * q + 4, :].rearrange("e a q n -> q (e a) n"),
                 )
-            load_w(0)
-            load_x(3, 0)
-            load_x(3, 1)
-            load_w(1)
-            load_w(2)
-            load_w(3)
+            for a in range(PASSES):
+                nc.sync.dma_start(
+                    words[a][:].bitcast(I32).rearrange("p (e n) -> p e n", e=E + 1),
+                    wv[:, a, :, :].rearrange("e p n -> p e n"),
+                )
             nc.sync.dma_start(bias[:], b)
             nc.sync.dma_start(pos1_t[:], pos1)
             nc.sync.dma_start(pos2_t[:], pos2)
             nc.sync.dma_start(gates[:].rearrange("p (g t) -> p g t", g=2), gate.rearrange("g p t -> p g t"))
 
         def cast(a, h, c0=0, c1=T, copy=nc.scalar.copy):
+            at = 2 * row_at(a, h)
             copy(
-                out=pairs[a][:, 2 * T * h : 2 * T * (h + 1)].rearrange("p (t e) -> p t e", e=2)[:, c0:c1, :],
+                out=pairs[:, at : at + 2 * T].rearrange("p (t e) -> p t e", e=2)[:, c0:c1, :],
                 in_=raw[a, h][:, :, c0:c1].rearrange("p e t -> p t e"),
             )
 
-        def gather(a, h, start, size):
-            window = 2 * T * (PASSES - 1 - a) + T * h
+        gath = {}
+
+        def gather(a, h, s0=0, s1=S):
+            if (a, s0) not in gath:
+                gath[a, s0] = keep.tile([P, 2 * S], U32, name=f"gath{a}_{s0}", align_bytes=64) if a < LAST else keep.tile([P, 2 * T], U32, name=f"gath{a}_{s0}", align_bytes=64)
+            at = row_at(a, h)
+            w = s1 - s0
             nc.vector.tensor_copy(
-                gath[a][:].bitcast(U32)[:, S * h + start : S * h + start + size],
-                pairs_all[:].bitcast(U32)[:, window : window + (T if size < T else 2 * T)].indirect(offs_t[:, start // 16 : (start + size) // 16]),
+                gath[a, s0][:, w * h : w * (h + 1)],
+                pairs[:].bitcast(U32)[:, at : at + WINDOW].indirect(offs_t[:, s0 // 16 : s1 // 16]),
             )
 
-        def weave(a, start, size):
+        def weave(a, s0=0, s1=S):
             nc.scalar.copy(
-                out=slots[a][:].bitcast(U32).rearrange("p (n u) -> p n u", u=2)[:, start : start + size, :],
-                in_=gath[a][:].bitcast(U32).rearrange("p (u n) -> p n u", u=2)[:, start : start + size, :],
+                out=slots[:].bitcast(U32)[:, 2 * (S * a + s0) : 2 * (S * a + s1)].rearrange("p (n u) -> p n u", u=2),
+                in_=gath[a, s0][:, : 2 * (s1 - s0)].rearrange("p (u n) -> p n u", u=2),
             )
 
         def weave_shared(a):
-            src = pairs[a].bitcast(U32).rearrange("p (u n) -> p n u", u=2)
-            nc.scalar.copy(out=shq[a][:].bitcast(U32).rearrange("p (n u) -> p n u", u=2), in_=src[:, :512, :])
+            at = row_at(a, 0)
             nc.scalar.copy(
-                out=rest[:].bitcast(U32)[:, 2 * C * a : 2 * C * (a + 1)].rearrange("p (n u) -> p n u", u=2), in_=src[:, 512:, :]
+                out=shq[:].bitcast(U32)[:, 2 * T * a : 2 * T * (a + 1)].rearrange("p (n u) -> p n u", u=2),
+                in_=pairs[:].bitcast(U32)[:, at : at + 2 * T].rearrange("p (u n) -> p n u", u=2),
             )
 
-        def quant(a, cuts):
-            for s0, w in cuts:
+        def quant(c0, c1):
+            nc.vector.quantize_mx(out=cs[:, c0:c1].bitcast(FP8X4), scales=ss[:, c0:c1], in_=slots[:, 4 * c0 : 4 * c1])
+
+        def quant_shared(half, s0):
+            csh[half] = keep.tile([P, 2 * T], U32, name=f"gath{LAST}_{s0}", align_bytes=64)
+            first = 2 * T * half
+            for c0, c1 in ((0, 1024), (1024, 2 * T)):
                 nc.vector.quantize_mx(
-                    out=cs[a][:, s0 : s0 + w].bitcast(FP8X4),
-                    scales=ss[a][:, s0 : s0 + w],
-                    in_=slots[a][:, 4 * s0 : 4 * (s0 + w)],
+                    out=csh[half][:, c0:c1].bitcast(FP8X4),
+                    scales=ssh[:, first + c0 : first + c1],
+                    in_=shq[:, 4 * (first + c0) : 4 * (first + c1)],
                 )
 
-        def quant_shared(a):
-            nc.vector.quantize_mx(out=csh[a][:].bitcast(FP8X4), scales=ssh[a][:], in_=shq[a][:])
+        def multiply(bank, e, a, codes, scales):
+            i = e * PASSES + a
+            nc.tensor.matmul_mx(
+                out=bank,
+                lhsT=words[a][:, e * 2 * N : (e + 1) * 2 * N].bitcast(FP4X4),
+                lhsT_scale=wsc[:, i * N : (i + 1) * N],
+                rhs=codes.bitcast(FP8X4),
+                rhs_scale=scales,
+                start=(a == 0),
+                stop=(a == LAST),
+            )
 
-        def quant_rest():
-            nc.vector.quantize_mx(out=crest[:].bitcast(FP8X4), scales=srest[:], in_=rest[:])
+        late_bank = psum.tile([P, 512], F32, name="bank0")
+        banks = [late_bank[:, e * C : (e + 1) * C] for e in range(LATE)]
+        for e in range(LATE, E):
+            bank = psum.tile([P, C], F32, name=f"bank{e}")
+            banks.append(bank[:])
 
-        def multiply(bank, e, codes, scales, s0, w):
+        def expert_pass(e, a):
+            cols = slice(a * S + e * C, a * S + (e + 1) * C)
+            multiply(banks[e], e, a, cs[:, cols], ss[:, cols])
+
+        def early_pass(a):
+            for e in range(LATE, E):
+                expert_pass(e, a)
+
+        def close(s0, s1):
+            group = range(s0 // C, s1 // C)
+            for e in group:
+                for a in range(PASSES) if e < LATE else (LAST,):
+                    expert_pass(e, a)
+            for e in group:
+                nc.scalar.activation(out=y[:, e * C : (e + 1) * C], in_=banks[e], func=GELU, bias=bias[:, e : e + 1])
+
+        def shared(c0, c1, name):
+            bank = psum.tile([P, c1 - c0], F32, name=name)
             for a in range(PASSES):
-                i = e * PASSES + a
-                nc.tensor.matmul_mx(
-                    out=bank,
-                    lhsT=words[a][:, e * 2 * N : (e + 1) * 2 * N].bitcast(FP4X4),
-                    lhsT_scale=wsc[:, i * N : (i + 1) * N],
-                    rhs=codes(a)[:, s0(a) : s0(a) + w].bitcast(FP8X4),
-                    rhs_scale=scales(a)[:, s0(a) : s0(a) + w],
-                    start=(a == 0),
-                    stop=(a == PASSES - 1),
-                )
+                at = a % 2 * T
+                multiply(bank[:], E, a, csh[a // 2][:, at + c0 : at + c1], ssh[:, a * T + c0 : a * T + c1])
+            nc.scalar.activation(out=ys[:, c0:c1], in_=bank[:], func=GELU, bias=bias[:, E : E + 1])
 
-        banks = {}
-
-        def bank_of(e):
-            key = e if e > 5 else e // 2
-            if key not in banks:
-                banks[key] = psum.tile([P, 3 * C if key == 0 else 2 * C if key < 3 else C], F32, name=f"bank{key}")
-            at = e % 2 * C if key < 3 else 0
-            return banks[key][:, at : at + C]
-
-        def experts(group):
-            for e in group:
-                multiply(bank_of(e), e, lambda a: cs[a], lambda a: ss[a], lambda a: e * C, C)
-            for e in group:
-                nc.scalar.activation(out=y[:, e * C : (e + 1) * C], in_=bank_of(e), func=GELU, bias=bias[:, e : e + 1])
-
-        def shared():
-            bank = psum.tile([P, 512], F32, name="bank_shared")
-            multiply(bank[:], E, lambda a: csh[a], lambda a: ssh[a], lambda a: 0, 512)
-            nc.scalar.activation(out=ys[:, :512], in_=bank[:], func=GELU, bias=bias[:, E : E + 1])
-            bank_rest = banks[0][:, 2 * C :]
-            multiply(bank_rest, E, lambda a: crest, lambda a: srest, lambda a: a * C, C)
-            nc.scalar.activation(out=ys[:, 512:], in_=bank_rest, func=GELU, bias=bias[:, E : E + 1])
-
-        cast(0, 0, 0, 384, nc.vector.tensor_copy)
-        cast(0, 0, 384, T)
-        cast(0, 1)
-        cast(1, 0)
+        load_x(0, 1)
+        nc.sync.dma_start(offs_t[:], offs)
+        load_x(0, 0)
+        load_x(1, 1)
+        load_x(1, 0)
+        cast(0, 1, 0, 384, nc.vector.tensor_copy)
+        cast(0, 1, 384, T)
+        load_x(2, 1)
+        gather(0, 1)
+        cast(0, 0)
+        load_x(2, 0)
+        gather(0, 0)
         cast(1, 1)
+        load_x(3, 1)
+        gather(1, 1)
+        cast(1, 0)
+        load_x(3, 0)
         load_rest()
-        pending = []
-
-        def finish(a, cuts):
-            quant(a, cuts)
-            if a == PASSES - 1:
-                for s0, w in cuts:
-                    experts(range(s0 // C, (s0 + w) // C))
-
+        gather(1, 0)
+        cast(2, 1)
+        gather(2, 1)
+        weave(0)
+        quant(0, 1024)
+        cast(2, 0)
+        gather(2, 0)
+        cast(3, 1)
+        for s0, s1 in PIECES:
+            gather(3, 1, s0, s1)
+        cast(3, 0)
+        for s0, s1 in PIECES:
+            gather(3, 0, s0, s1)
+        weave(1)
+        quant(1024, 2048)
+        quant(2048, 2 * S)
+        early_pass(0)
+        early_pass(1)
         for a in range(PASSES):
-            if 0 < a < PASSES - 1:
-                cast(a + 1, 0)
-                cast(a + 1, 1)
-            for i, ((start, size), cuts) in enumerate(PIECES[a]):
-                gather(a, 0, start, size)
-                gather(a, 1, start, size)
-                weave(a, start, size)
-                if pending:
-                    finish(*pending.pop())
-                pending.append((a, cuts))
-                if i == min(len(PIECES[a]) - 1, 2):
-                    weave_shared(a)
-        finish(*pending.pop())
-        for a in range(PASSES):
-            quant_shared(a)
-        quant_rest()
-        shared()
+            weave_shared(a)
+        weave(2)
+        quant(2 * S, 2 * S + 1024)
+        quant(2 * S + 1024, 3 * S)
+        early_pass(2)
+        for i, (s0, s1) in enumerate(PIECES):
+            weave(LAST, s0, s1)
+            quant(LAST * S + s0, LAST * S + s1)
+            close(s0, s1)
+            if i != 1:
+                quant_shared(i // 2, s0)
+        shared(0, 512, "bank0")
+        shared(512, T, f"bank{LATE}")
 
         s1 = keep.tile([P, T], F32, name="s1")
         s2 = keep.tile([P, T], F32, name="s2")
@@ -220,7 +232,7 @@ def tile_moe_shr_lin_gelu_kernel(tc, xT, w_words, w_scales, b, gate, offs, pos1,
         nc.vector.tensor_tensor(s2[:], y[:].indirect(pos2_t[:]), gates[:, T:], MULT)
         parts = (slice(0, 384), slice(384, T))
         for cols in parts:
-            nc.vector.tensor_add(t1[:, cols], s1[:, cols], ys[:, cols])
+            nc.vector.tensor_add(t1[:, cols], s1[:, cols], s2[:, cols])
         for cols in parts:
-            nc.vector.tensor_add(res[:, cols], t1[:, cols], s2[:, cols])
+            nc.vector.tensor_add(res[:, cols], t1[:, cols], ys[:, cols])
             nc.sync.dma_start(out[:, cols], res[:, cols])

@@ -11,6 +11,8 @@ WINDOW = 1712
 LAST = PASSES - 1
 PIECES = ((0, 512), (512, 1024), (1024, S))
 LATE = 3
+DIRECT = 640
+PLANE_WINDOW = 896
 FLOPS = 2 * K * N * (S + T)
 
 F32 = mybir.dt.float32
@@ -22,6 +24,7 @@ U8 = mybir.dt.uint8
 FP8X4 = mybir.dt.float8_e4m3fn_x4
 FP4X4 = mybir.dt.float4_e2m1fn_x4
 GELU = mybir.ActivationFunctionType.Gelu_apprx_tanh
+COPY = mybir.ActivationFunctionType.Copy
 MULT = mybir.AluOpType.mult
 
 
@@ -29,7 +32,6 @@ def tile_moe_shr_lin_gelu_kernel(tc, xT, w_words, w_scales, b, gate, offs, pos1,
     nc = tc.nc
     with ExitStack() as ctx:
         keep = ctx.enter_context(tc.tile_pool(name="keep", bufs=1))
-        ring = ctx.enter_context(tc.tile_pool(name="ring", bufs=2))
         psum = ctx.enter_context(tc.psum_pool(name="psum", bufs=1))
 
         offs_t = keep.tile([P, S // 16], U16, name="offs_t")
@@ -45,9 +47,10 @@ def tile_moe_shr_lin_gelu_kernel(tc, xT, w_words, w_scales, b, gate, offs, pos1,
         for a in range(PASSES):
             words.append(keep.tile([P, (E + 1) * 2 * N], U8, name=f"words{a}", align_bytes=64))
         slots = keep.tile([P, PASSES * 4 * S], BF16, name="slots", align_bytes=64)
-        cs = keep.tile([P, PASSES * S], U32, name="cs", align_bytes=64)
+        cs = {1: keep.tile([P, 2 * S], U32, name="cs", align_bytes=64)}
+        planes = keep.tile([P, 3 * T + PLANE_WINDOW], BF16, name="planes", align_bytes=64)
         ss = keep.tile([P, PASSES * S], U8, name="ss", align_bytes=64)
-        shq = keep.tile([P, PASSES * 4 * T], BF16, name="shq", align_bytes=64)
+        shq = [keep.tile([P, 2 * 4 * T], BF16, name=f"shq{half}", align_bytes=64) for half in range(2)]
         csh = {}
         ssh = keep.tile([P, PASSES * T], U8, name="ssh", align_bytes=64)
 
@@ -63,13 +66,19 @@ def tile_moe_shr_lin_gelu_kernel(tc, xT, w_words, w_scales, b, gate, offs, pos1,
         nc.vector.memset(warm[:], 0.0)
         nc.scalar.activation(out=warm[:], in_=warm[:], func=GELU)
         nc.vector.memset(pairs[:].bitcast(I32)[:, ROWS * T :], 0)
+        nc.vector.memset(planes[:].bitcast(I32)[:, 2 * T : (3 * T + PLANE_WINDOW) // 2], 0)
         nc.vector.memset(wsc[:].bitcast(I32), 0)
 
         raw = {}
 
         def load_x(a, h):
-            raw[a, h] = ring.tile([P, 2, T], F32, name=f"raw{h}")
-            nc.sync.dma_start(raw[a, h][:], xv[a][:, 2 * h : 2 * h + 2, :])
+            if (a, h) == (LAST, 0):
+                raw[a, h] = keep.tile([P, 2, T], F32, name="raw_last", align_bytes=64)
+            elif (a, h) == (2, 1):
+                raw[a, h] = slots[:, : 4 * T].bitcast(F32).rearrange("p (e t) -> p e t", e=2)
+            else:
+                raw[a, h] = keep.tile([P, 2, T], F32, name=f"raw{a}_{h}")
+            nc.sync.dma_start(raw[a, h][:, :, :], xv[a][:, 2 * h : 2 * h + 2, :])
 
         def load_rest():
             for q in range(4):
@@ -94,6 +103,20 @@ def tile_moe_shr_lin_gelu_kernel(tc, xT, w_words, w_scales, b, gate, offs, pos1,
                 in_=raw[a, h][:, :, c0:c1].rearrange("p e t -> p t e"),
             )
 
+        def split():
+            at = 2 * row_at(1, 0)
+            nc.gpsimd.tensor_copy(
+                out=planes[:, : 4 * T].rearrange("p (h e t) -> p h e t", h=2, e=2),
+                in_=pairs[:, at : at + 4 * T].rearrange("p (h t e) -> p h e t", h=2, e=2),
+            )
+
+        def gather_direct(j):
+            nc.scalar.activation(
+                out=slots[:, 4 * S : 4 * (S + DIRECT)].rearrange("p (n j) -> p n j", j=4)[:, :, j],
+                in_=planes[:, T * j : T * j + PLANE_WINDOW].indirect(offs_t[:, : DIRECT // 16]),
+                func=COPY,
+            )
+
         gath = {}
 
         def gather(a, h, s0=0, s1=S):
@@ -114,13 +137,14 @@ def tile_moe_shr_lin_gelu_kernel(tc, xT, w_words, w_scales, b, gate, offs, pos1,
 
         def weave_shared(a):
             at = row_at(a, 0)
-            nc.scalar.copy(
-                out=shq[:].bitcast(U32)[:, 2 * T * a : 2 * T * (a + 1)].rearrange("p (n u) -> p n u", u=2),
+            nc.gpsimd.tensor_copy(
+                out=shq[a // 2][:].bitcast(U32)[:, 2 * T * (a % 2) : 2 * T * (a % 2 + 1)].rearrange("p (n u) -> p n u", u=2),
                 in_=pairs[:].bitcast(U32)[:, at : at + 2 * T].rearrange("p (u n) -> p n u", u=2),
             )
 
         def quant(c0, c1):
-            nc.vector.quantize_mx(out=cs[:, c0:c1].bitcast(FP8X4), scales=ss[:, c0:c1], in_=slots[:, 4 * c0 : 4 * c1])
+            half, at = divmod(c0, 2 * S)
+            nc.vector.quantize_mx(out=cs[half][:, at : at + c1 - c0].bitcast(FP8X4), scales=ss[:, c0:c1], in_=slots[:, 4 * c0 : 4 * c1])
 
         def quant_shared(half, s0):
             csh[half] = keep.tile([P, 2 * T], U32, name=f"gath{LAST}_{s0}", align_bytes=64)
@@ -129,7 +153,7 @@ def tile_moe_shr_lin_gelu_kernel(tc, xT, w_words, w_scales, b, gate, offs, pos1,
                 nc.vector.quantize_mx(
                     out=csh[half][:, c0:c1].bitcast(FP8X4),
                     scales=ssh[:, first + c0 : first + c1],
-                    in_=shq[:, 4 * (first + c0) : 4 * (first + c1)],
+                    in_=shq[half][:, 4 * c0 : 4 * c1],
                 )
 
         def multiply(bank, e, a, codes, scales):
@@ -152,7 +176,8 @@ def tile_moe_shr_lin_gelu_kernel(tc, xT, w_words, w_scales, b, gate, offs, pos1,
 
         def expert_pass(e, a):
             cols = slice(a * S + e * C, a * S + (e + 1) * C)
-            multiply(banks[e], e, a, cs[:, cols], ss[:, cols])
+            at = a % 2 * S + e * C
+            multiply(banks[e], e, a, cs[a // 2][:, at : at + C], ss[:, cols])
 
         def early_pass(a):
             for e in range(LATE, E):
@@ -185,32 +210,38 @@ def tile_moe_shr_lin_gelu_kernel(tc, xT, w_words, w_scales, b, gate, offs, pos1,
         cast(0, 0)
         load_x(2, 0)
         gather(0, 0)
+        weave_shared(0)
         cast(1, 1)
         load_x(3, 1)
-        gather(1, 1)
+        gather(1, 1, DIRECT, S)
         cast(1, 0)
         load_x(3, 0)
         load_rest()
-        gather(1, 0)
+        gather(1, 0, DIRECT, S)
+        split()
         cast(2, 1)
         gather(2, 1)
         weave(0)
-        quant(0, 1024)
-        cast(2, 0)
+        for j in range(4):
+            gather_direct(j)
+        cast(2, 0, copy=nc.gpsimd.tensor_copy)
         gather(2, 0)
-        cast(3, 1)
+        cast(3, 1, copy=nc.gpsimd.tensor_copy)
         for s0, s1 in PIECES:
             gather(3, 1, s0, s1)
-        cast(3, 0)
+        weave_shared(1)
+        weave_shared(2)
+        cast(3, 0, copy=nc.gpsimd.tensor_copy)
+        weave_shared(3)
         for s0, s1 in PIECES:
             gather(3, 0, s0, s1)
-        weave(1)
+        weave(1, DIRECT, S)
+        cs[0] = keep.tile([P, 2 * S], U32, name="raw_last", align_bytes=64)
+        quant(0, 1024)
         quant(1024, 2048)
         quant(2048, 2 * S)
         early_pass(0)
         early_pass(1)
-        for a in range(PASSES):
-            weave_shared(a)
         weave(2)
         quant(2 * S, 2 * S + 1024)
         quant(2 * S + 1024, 3 * S)
@@ -224,10 +255,10 @@ def tile_moe_shr_lin_gelu_kernel(tc, xT, w_words, w_scales, b, gate, offs, pos1,
         shared(0, 512, "bank0")
         shared(512, T, f"bank{LATE}")
 
-        s1 = keep.tile([P, T], F32, name="s1")
-        s2 = keep.tile([P, T], F32, name="s2")
-        t1 = keep.tile([P, T], F32, name="t1")
-        res = keep.tile([P, T], F32, name="res")
+        s1 = keep.tile([P, T], F32, name="raw0_1")
+        s2 = keep.tile([P, T], F32, name="raw0_0")
+        t1 = keep.tile([P, T], F32, name="raw1_1")
+        res = keep.tile([P, T], F32, name="raw1_0")
         nc.vector.tensor_tensor(s1[:], y[:].indirect(pos1_t[:]), gates[:, :T], MULT)
         nc.vector.tensor_tensor(s2[:], y[:].indirect(pos2_t[:]), gates[:, T:], MULT)
         parts = (slice(0, 384), slice(384, T))

@@ -10,9 +10,10 @@ ROWS = 2 * PASSES
 WINDOW = 1712
 LAST = PASSES - 1
 PIECES = ((0, 512), (512, 1024), (1024, S))
-LATE = 3
-DIRECT = 640
-PLANE_WINDOW = 896
+BANKS = 8
+MADE = [(0, 1), (1, 1), (0, 0), (2, 1), (2, 0), (1, 0), (3, 1), (3, 0)]
+DIRECT = 1024
+PLANE_WINDOW = 1376
 FLOPS = 2 * K * N * (S + T)
 
 F32 = mybir.dt.float32
@@ -47,17 +48,16 @@ def tile_moe_shr_lin_gelu_kernel(tc, xT, w_words, w_scales, b, gate, offs, pos1,
         for a in range(PASSES):
             words.append(keep.tile([P, (E + 1) * 2 * N], U8, name=f"words{a}", align_bytes=64))
         slots = keep.tile([P, PASSES * 4 * S], BF16, name="slots", align_bytes=64)
-        cs = {1: keep.tile([P, 2 * S], U32, name="cs", align_bytes=64)}
+        cs = keep.tile([P, PASSES * S], U32, name="cs", align_bytes=64)
+        direct = keep.tile([P, 4 * DIRECT], BF16, name="direct", align_bytes=64)
         planes = keep.tile([P, 3 * T + PLANE_WINDOW], BF16, name="planes", align_bytes=64)
-        ss = keep.tile([P, PASSES * S], U8, name="ss", align_bytes=64)
-        shq = [keep.tile([P, 2 * 4 * T], BF16, name=f"shq{half}", align_bytes=64) for half in range(2)]
         csh = {}
         ssh = keep.tile([P, PASSES * T], U8, name="ssh", align_bytes=64)
 
         pairs = keep.tile([P, 2 * ((ROWS - 1) * T + WINDOW)], BF16, name="pairs", align_bytes=64)
 
         def row_at(a, h):
-            return T * (2 * (PASSES - 1 - a) + h)
+            return T * (ROWS - 1 - MADE.index((a, h)))
 
         xv = xT.rearrange("(a p j) t -> a p j t", p=P, j=4)
         wv = w_words.bitcast(I32)
@@ -67,7 +67,7 @@ def tile_moe_shr_lin_gelu_kernel(tc, xT, w_words, w_scales, b, gate, offs, pos1,
         nc.scalar.activation(out=warm[:], in_=warm[:], func=GELU)
         nc.vector.memset(pairs[:].bitcast(I32)[:, ROWS * T :], 0)
         nc.vector.memset(planes[:].bitcast(I32)[:, 2 * T : (3 * T + PLANE_WINDOW) // 2], 0)
-        nc.vector.memset(wsc[:].bitcast(I32), 0)
+        nc.gpsimd.memset(wsc[:].bitcast(I32), 0)
 
         raw = {}
 
@@ -77,7 +77,7 @@ def tile_moe_shr_lin_gelu_kernel(tc, xT, w_words, w_scales, b, gate, offs, pos1,
             elif (a, h) == (2, 1):
                 raw[a, h] = slots[:, : 4 * T].bitcast(F32).rearrange("p (e t) -> p e t", e=2)
             else:
-                raw[a, h] = keep.tile([P, 2, T], F32, name=f"raw{a}_{h}")
+                raw[a, h] = keep.tile([P, 2, T], F32, name=f"raw{a}_{h}", align_bytes=64)
             nc.sync.dma_start(raw[a, h][:, :, :], xv[a][:, 2 * h : 2 * h + 2, :])
 
         def load_rest():
@@ -103,16 +103,12 @@ def tile_moe_shr_lin_gelu_kernel(tc, xT, w_words, w_scales, b, gate, offs, pos1,
                 in_=raw[a, h][:, :, c0:c1].rearrange("p e t -> p t e"),
             )
 
-        def split():
-            at = 2 * row_at(1, 0)
-            nc.gpsimd.tensor_copy(
-                out=planes[:, : 4 * T].rearrange("p (h e t) -> p h e t", h=2, e=2),
-                in_=pairs[:, at : at + 4 * T].rearrange("p (h t e) -> p h e t", h=2, e=2),
-            )
+        def split(h):
+            nc.gpsimd.tensor_copy(out=planes[:, 2 * T * h : 2 * T * (h + 1)], in_=raw[1, h][:].rearrange("p e t -> p (e t)"))
 
         def gather_direct(j):
             nc.scalar.activation(
-                out=slots[:, 4 * S : 4 * (S + DIRECT)].rearrange("p (n j) -> p n j", j=4)[:, :, j],
+                out=direct[:].rearrange("p (n j) -> p n j", j=4)[:, :, j],
                 in_=planes[:, T * j : T * j + PLANE_WINDOW].indirect(offs_t[:, : DIRECT // 16]),
                 func=COPY,
             )
@@ -137,14 +133,14 @@ def tile_moe_shr_lin_gelu_kernel(tc, xT, w_words, w_scales, b, gate, offs, pos1,
 
         def weave_shared(a):
             at = row_at(a, 0)
+            apart = (row_at(a, 1) - at) // T
             nc.gpsimd.tensor_copy(
-                out=shq[a // 2][:].bitcast(U32)[:, 2 * T * (a % 2) : 2 * T * (a % 2 + 1)].rearrange("p (n u) -> p n u", u=2),
-                in_=pairs[:].bitcast(U32)[:, at : at + 2 * T].rearrange("p (u n) -> p n u", u=2),
+                out=shq[:].bitcast(U32)[:, 2 * T * a : 2 * T * (a + 1)].rearrange("p (n u) -> p n u", u=2),
+                in_=pairs[:].bitcast(U32)[:, at : at + (apart + 1) * T].rearrange("p (u n) -> p n u", n=T)[:, :, ::apart],
             )
 
         def quant(c0, c1):
-            half, at = divmod(c0, 2 * S)
-            nc.vector.quantize_mx(out=cs[half][:, at : at + c1 - c0].bitcast(FP8X4), scales=ss[:, c0:c1], in_=slots[:, 4 * c0 : 4 * c1])
+            nc.vector.quantize_mx(out=cs[:, c0:c1].bitcast(FP8X4), scales=ss[:, c0:c1], in_=slots[:, 4 * c0 : 4 * c1])
 
         def quant_shared(half, s0):
             csh[half] = keep.tile([P, 2 * T], U32, name=f"gath{LAST}_{s0}", align_bytes=64)
@@ -153,7 +149,7 @@ def tile_moe_shr_lin_gelu_kernel(tc, xT, w_words, w_scales, b, gate, offs, pos1,
                 nc.vector.quantize_mx(
                     out=csh[half][:, c0:c1].bitcast(FP8X4),
                     scales=ssh[:, first + c0 : first + c1],
-                    in_=shq[half][:, 4 * c0 : 4 * c1],
+                    in_=shq[:, 4 * (first + c0) : 4 * (first + c1)],
                 )
 
         def multiply(bank, e, a, codes, scales):
@@ -168,97 +164,98 @@ def tile_moe_shr_lin_gelu_kernel(tc, xT, w_words, w_scales, b, gate, offs, pos1,
                 stop=(a == LAST),
             )
 
-        late_bank = psum.tile([P, 512], F32, name="bank0")
-        banks = [late_bank[:, e * C : (e + 1) * C] for e in range(LATE)]
-        for e in range(LATE, E):
-            bank = psum.tile([P, C], F32, name=f"bank{e}")
-            banks.append(bank[:])
+        banks = {}
 
         def expert_pass(e, a):
+            if a == 0:
+                banks[e] = psum.tile([P, 512], F32, name=f"bank{e % BANKS}")
             cols = slice(a * S + e * C, a * S + (e + 1) * C)
-            at = a % 2 * S + e * C
-            multiply(banks[e], e, a, cs[a // 2][:, at : at + C], ss[:, cols])
+            multiply(banks[e][:, :C], e, a, cs[:, cols], ss[:, cols])
 
         def early_pass(a):
-            for e in range(LATE, E):
+            for e in range(BANKS):
                 expert_pass(e, a)
 
         def close(s0, s1):
             group = range(s0 // C, s1 // C)
             for e in group:
-                for a in range(PASSES) if e < LATE else (LAST,):
-                    expert_pass(e, a)
+                expert_pass(e, LAST)
             for e in group:
-                nc.scalar.activation(out=y[:, e * C : (e + 1) * C], in_=banks[e], func=GELU, bias=bias[:, e : e + 1])
+                nc.scalar.activation(out=y[:, e * C : (e + 1) * C], in_=banks[e][:, :C], func=GELU, bias=bias[:, e : e + 1])
+                if e + BANKS < E:
+                    for a in range(LAST):
+                        expert_pass(e + BANKS, a)
 
         def shared(c0, c1, name):
-            bank = psum.tile([P, c1 - c0], F32, name=name)
+            bank = psum.tile([P, 512], F32, name=name)
             for a in range(PASSES):
                 at = a % 2 * T
-                multiply(bank[:], E, a, csh[a // 2][:, at + c0 : at + c1], ssh[:, a * T + c0 : a * T + c1])
-            nc.scalar.activation(out=ys[:, c0:c1], in_=bank[:], func=GELU, bias=bias[:, E : E + 1])
+                multiply(bank[:, : c1 - c0], E, a, csh[a // 2][:, at + c0 : at + c1], ssh[:, a * T + c0 : a * T + c1])
+            nc.scalar.activation(out=ys[:, c0:c1], in_=bank[:, : c1 - c0], func=GELU, bias=bias[:, E : E + 1])
 
         load_x(0, 1)
         nc.sync.dma_start(offs_t[:], offs)
-        load_x(0, 0)
         load_x(1, 1)
-        load_x(1, 0)
+        load_x(0, 0)
         cast(0, 1, 0, 384, nc.vector.tensor_copy)
         cast(0, 1, 384, T)
         load_x(2, 1)
-        gather(0, 1)
-        cast(0, 0)
+        load_x(1, 0)
         load_x(2, 0)
-        gather(0, 0)
-        weave_shared(0)
-        cast(1, 1)
         load_x(3, 1)
-        gather(1, 1, DIRECT, S)
-        cast(1, 0)
         load_x(3, 0)
         load_rest()
-        gather(1, 0, DIRECT, S)
-        split()
-        cast(2, 1)
+        gather(0, 1)
+        split(1)
+        cast(1, 1)
+        gather(1, 1, DIRECT, S)
+        cast(0, 0, copy=nc.gpsimd.tensor_copy)
+        gather(0, 0)
+        gather_direct(2)
+        gather_direct(3)
+        cast(2, 1, copy=nc.gpsimd.tensor_copy)
         gather(2, 1)
-        weave(0)
-        for j in range(4):
-            gather_direct(j)
+        split(0)
+        gather_direct(0)
+        gather_direct(1)
         cast(2, 0, copy=nc.gpsimd.tensor_copy)
         gather(2, 0)
+        cast(1, 0, copy=nc.gpsimd.tensor_copy)
+        gather(1, 0, DIRECT, S)
         cast(3, 1, copy=nc.gpsimd.tensor_copy)
         for s0, s1 in PIECES:
             gather(3, 1, s0, s1)
-        weave_shared(1)
-        weave_shared(2)
         cast(3, 0, copy=nc.gpsimd.tensor_copy)
-        weave_shared(3)
         for s0, s1 in PIECES:
             gather(3, 0, s0, s1)
+        shq = keep.tile([P, PASSES * 4 * T], BF16, name="raw3_1", align_bytes=64)
+        ss = keep.tile([P, PASSES * S], U8, name="raw_last", align_bytes=64)
+        for a in range(PASSES):
+            weave_shared(a)
+        weave(0)
         weave(1, DIRECT, S)
-        cs[0] = keep.tile([P, 2 * S], U32, name="raw_last", align_bytes=64)
         quant(0, 1024)
-        quant(1024, 2048)
-        quant(2048, 2 * S)
+        quant(1024, S)
         early_pass(0)
+        nc.vector.quantize_mx(out=cs[:, S : S + DIRECT].bitcast(FP8X4), scales=ss[:, S : S + DIRECT], in_=direct[:])
         early_pass(1)
         weave(2)
-        quant(2 * S, 2 * S + 1024)
-        quant(2 * S + 1024, 3 * S)
+        quant(S + DIRECT, S + DIRECT + 1024)
+        quant(S + DIRECT + 1024, 3 * S)
         early_pass(2)
-        for i, (s0, s1) in enumerate(PIECES):
+        for s0, s1 in PIECES:
             weave(LAST, s0, s1)
             quant(LAST * S + s0, LAST * S + s1)
             close(s0, s1)
-            if i != 1:
-                quant_shared(i // 2, s0)
-        shared(0, 512, "bank0")
-        shared(512, T, f"bank{LATE}")
+        quant_shared(0, PIECES[2][0])
+        quant_shared(1, PIECES[1][0])
+        shared(0, 512, f"bank{(E - 1) % BANKS}")
+        shared(512, T, f"bank{(E - 2) % BANKS}")
 
-        s1 = keep.tile([P, T], F32, name="raw0_1")
-        s2 = keep.tile([P, T], F32, name="raw0_0")
-        t1 = keep.tile([P, T], F32, name="raw1_1")
-        res = keep.tile([P, T], F32, name="raw1_0")
+        s1 = keep.tile([P, T], F32, name="raw0_1", align_bytes=64)
+        s2 = keep.tile([P, T], F32, name="raw0_0", align_bytes=64)
+        t1 = keep.tile([P, T], F32, name="raw1_1", align_bytes=64)
+        res = keep.tile([P, T], F32, name="raw1_0", align_bytes=64)
         nc.vector.tensor_tensor(s1[:], y[:].indirect(pos1_t[:]), gates[:, :T], MULT)
         nc.vector.tensor_tensor(s2[:], y[:].indirect(pos2_t[:]), gates[:, T:], MULT)
         parts = (slice(0, 384), slice(384, T))

@@ -6,15 +6,20 @@ K, T, E, C, N = 2048, 640, 10, 128, 128
 S = E * C
 P = 128
 PASSES = 4
-ROWS = 2 * PASSES
-WINDOW = 1712
 LAST = PASSES - 1
+FLOPS = 2 * K * N * (S + T)
+
+ROWS = [(0, 1), (1, 1), (0, 0), (2, 1), (2, 0), (1, 0), (3, 1), (3, 0)]
+SPLIT_PASS = 1
+DIRECT = 1024
+ROW_WINDOW = 1712
+PLANE_WINDOW = 1376
+FIRST_ON_VECTOR = 384
+WIDE = 1024
 PIECES = ((0, 512), (512, 1024), (1024, S))
 BANKS = 8
-MADE = [(0, 1), (1, 1), (0, 0), (2, 1), (2, 0), (1, 0), (3, 1), (3, 0)]
-DIRECT = 1024
-PLANE_WINDOW = 1376
-FLOPS = 2 * K * N * (S + T)
+BANK = 512
+FIRST_STORE = 384
 
 F32 = mybir.dt.float32
 BF16 = mybir.dt.bfloat16
@@ -35,129 +40,126 @@ def tile_moe_shr_lin_gelu_kernel(tc, xT, w_words, w_scales, b, gate, offs, pos1,
         keep = ctx.enter_context(tc.tile_pool(name="keep", bufs=1))
         psum = ctx.enter_context(tc.psum_pool(name="psum", bufs=1))
 
+        def aligned(shape, dtype, name):
+            return keep.tile(shape, dtype, name=name, align_bytes=64)
+
         offs_t = keep.tile([P, S // 16], U16, name="offs_t")
         pos1_t = keep.tile([P, T // 16], U16, name="pos1_t")
         pos2_t = keep.tile([P, T // 16], U16, name="pos2_t")
         bias = keep.tile([P, E + 1], F32, name="bias")
         gates = keep.tile([P, 2 * T], F32, name="gates")
-        wsc = keep.tile([P, (E + 1) * PASSES * N], U8, name="wsc", align_bytes=64)
-        warm = keep.tile([P, 8], F32, name="warm")
+        w_scale = aligned([P, (E + 1) * PASSES * N], U8, "w_scale")
         y = keep.tile([P, S], F32, name="y")
         ys = keep.tile([P, T], F32, name="ys")
-        words = []
-        for a in range(PASSES):
-            words.append(keep.tile([P, (E + 1) * 2 * N], U8, name=f"words{a}", align_bytes=64))
-        slots = keep.tile([P, PASSES * 4 * S], BF16, name="slots", align_bytes=64)
-        cs = keep.tile([P, PASSES * S], U32, name="cs", align_bytes=64)
-        direct = keep.tile([P, 4 * DIRECT], BF16, name="direct", align_bytes=64)
-        planes = keep.tile([P, 3 * T + PLANE_WINDOW], BF16, name="planes", align_bytes=64)
-        csh = {}
-        ssh = keep.tile([P, PASSES * T], U8, name="ssh", align_bytes=64)
-
-        pairs = keep.tile([P, 2 * ((ROWS - 1) * T + WINDOW)], BF16, name="pairs", align_bytes=64)
+        w_codes = [aligned([P, (E + 1) * 2 * N], U8, f"w_codes{a}") for a in range(PASSES)]
+        woven_quads = aligned([P, PASSES * 4 * S], BF16, "woven_quads")
+        slot_codes = aligned([P, PASSES * S], U32, "slot_codes")
+        direct_quads = aligned([P, 4 * DIRECT], BF16, "direct_quads")
+        planes = aligned([P, 3 * T + PLANE_WINDOW], BF16, "planes")
+        shared_scale = aligned([P, PASSES * T], U8, "shared_scale")
+        rows = aligned([P, 2 * ((len(ROWS) - 1) * T + ROW_WINDOW)], BF16, "rows")
 
         def row_at(a, h):
-            return T * (ROWS - 1 - MADE.index((a, h)))
+            return T * (len(ROWS) - 1 - ROWS.index((a, h)))
 
-        xv = xT.rearrange("(a p j) t -> a p j t", p=P, j=4)
-        wv = w_words.bitcast(I32)
-        sv = w_scales.bitcast(I32)
-
-        nc.vector.memset(warm[:], 0.0)
-        nc.scalar.activation(out=warm[:], in_=warm[:], func=GELU)
-        nc.vector.memset(pairs[:].bitcast(I32)[:, ROWS * T :], 0)
+        nc.vector.memset(rows[:].bitcast(I32)[:, len(ROWS) * T :], 0)
         nc.vector.memset(planes[:].bitcast(I32)[:, 2 * T : (3 * T + PLANE_WINDOW) // 2], 0)
-        nc.gpsimd.memset(wsc[:].bitcast(I32), 0)
+        nc.gpsimd.memset(w_scale[:].bitcast(I32), 0)
 
         raw = {}
 
-        def load_x(a, h):
-            if (a, h) == (LAST, 0):
-                raw[a, h] = keep.tile([P, 2, T], F32, name="raw_last", align_bytes=64)
-            elif (a, h) == (2, 1):
-                raw[a, h] = slots[:, : 4 * T].bitcast(F32).rearrange("p (e t) -> p e t", e=2)
+        def load_row(a, h):
+            if (a, h) == (2, 1):
+                raw[a, h] = woven_quads[:, : 4 * T].bitcast(F32).rearrange("p (e t) -> p e t", e=2)
             else:
-                raw[a, h] = keep.tile([P, 2, T], F32, name=f"raw{a}_{h}", align_bytes=64)
-            nc.sync.dma_start(raw[a, h][:, :, :], xv[a][:, 2 * h : 2 * h + 2, :])
+                raw[a, h] = aligned([P, 2, T], F32, f"raw{a}_{h}")
+            nc.sync.dma_start(raw[a, h][:, :, :], xT.rearrange("(a p j) t -> a p j t", p=P, j=4)[a][:, 2 * h : 2 * h + 2, :])
 
-        def load_rest():
+        def preload_weights_and_combine_inputs():
             for q in range(4):
                 nc.sync.dma_start(
-                    wsc[32 * q : 32 * q + 4, :].bitcast(I32).rearrange("q (i n) -> q i n", n=N // 4),
-                    sv[:, :, 4 * q : 4 * q + 4, :].rearrange("e a q n -> q (e a) n"),
+                    w_scale[32 * q : 32 * q + 4, :].bitcast(I32).rearrange("r (i n) -> r i n", n=N // 4),
+                    w_scales.bitcast(I32)[:, :, 4 * q : 4 * q + 4, :].rearrange("e a r n -> r (e a) n"),
                 )
             for a in range(PASSES):
                 nc.sync.dma_start(
-                    words[a][:].bitcast(I32).rearrange("p (e n) -> p e n", e=E + 1),
-                    wv[:, a, :, :].rearrange("e p n -> p e n"),
+                    w_codes[a][:].bitcast(I32).rearrange("p (e n) -> p e n", e=E + 1),
+                    w_words.bitcast(I32)[:, a, :, :].rearrange("e p n -> p e n"),
                 )
             nc.sync.dma_start(bias[:], b)
             nc.sync.dma_start(pos1_t[:], pos1)
             nc.sync.dma_start(pos2_t[:], pos2)
             nc.sync.dma_start(gates[:].rearrange("p (g t) -> p g t", g=2), gate.rearrange("g p t -> p g t"))
 
-        def cast(a, h, c0=0, c1=T, copy=nc.scalar.copy):
+        def round_row(a, h, copy, t0=0, t1=T):
             at = 2 * row_at(a, h)
             copy(
-                out=pairs[:, at : at + 2 * T].rearrange("p (t e) -> p t e", e=2)[:, c0:c1, :],
-                in_=raw[a, h][:, :, c0:c1].rearrange("p e t -> p t e"),
+                out=rows[:, at : at + 2 * T].rearrange("p (t e) -> p t e", e=2)[:, t0:t1, :],
+                in_=raw[a, h][:, :, t0:t1].rearrange("p e t -> p t e"),
             )
 
-        def split(h):
-            nc.gpsimd.tensor_copy(out=planes[:, 2 * T * h : 2 * T * (h + 1)], in_=raw[1, h][:].rearrange("p e t -> p (e t)"))
+        def round_planes(h):
+            nc.gpsimd.tensor_copy(
+                out=planes[:, 2 * T * h : 2 * T * (h + 1)], in_=raw[SPLIT_PASS, h][:].rearrange("p e t -> p (e t)")
+            )
 
-        def gather_direct(j):
+        def gather_plane(j):
             nc.scalar.activation(
-                out=direct[:].rearrange("p (n j) -> p n j", j=4)[:, :, j],
+                out=direct_quads[:].rearrange("p (n j) -> p n j", j=4)[:, :, j],
                 in_=planes[:, T * j : T * j + PLANE_WINDOW].indirect(offs_t[:, : DIRECT // 16]),
                 func=COPY,
             )
 
-        gath = {}
+        gathered = {}
 
-        def gather(a, h, s0=0, s1=S):
-            if (a, s0) not in gath:
-                gath[a, s0] = keep.tile([P, 2 * S], U32, name=f"gath{a}_{s0}", align_bytes=64) if a < LAST else keep.tile([P, 2 * T], U32, name=f"gath{a}_{s0}", align_bytes=64)
-            at = row_at(a, h)
-            w = s1 - s0
+        def gather_row(a, h, s0=0, s1=S):
+            if (a, s0) not in gathered:
+                gathered[a, s0] = aligned([P, 2 * T if a == LAST else 2 * S], U32, f"gathered{a}_{s0}")
+            at, width = row_at(a, h), s1 - s0
             nc.vector.tensor_copy(
-                gath[a, s0][:, w * h : w * (h + 1)],
-                pairs[:].bitcast(U32)[:, at : at + WINDOW].indirect(offs_t[:, s0 // 16 : s1 // 16]),
+                gathered[a, s0][:, width * h : width * (h + 1)],
+                rows[:].bitcast(U32)[:, at : at + ROW_WINDOW].indirect(offs_t[:, s0 // 16 : s1 // 16]),
             )
 
         def weave(a, s0=0, s1=S):
             nc.scalar.copy(
-                out=slots[:].bitcast(U32)[:, 2 * (S * a + s0) : 2 * (S * a + s1)].rearrange("p (n u) -> p n u", u=2),
-                in_=gath[a, s0][:, : 2 * (s1 - s0)].rearrange("p (u n) -> p n u", u=2),
+                out=woven_quads[:].bitcast(U32)[:, 2 * (S * a + s0) : 2 * (S * a + s1)].rearrange("p (n h) -> p n h", h=2),
+                in_=gathered[a, s0][:, : 2 * (s1 - s0)].rearrange("p (h n) -> p n h", h=2),
             )
 
         def weave_shared(a):
             at = row_at(a, 0)
             apart = (row_at(a, 1) - at) // T
             nc.gpsimd.tensor_copy(
-                out=shq[:].bitcast(U32)[:, 2 * T * a : 2 * T * (a + 1)].rearrange("p (n u) -> p n u", u=2),
-                in_=pairs[:].bitcast(U32)[:, at : at + (apart + 1) * T].rearrange("p (u n) -> p n u", n=T)[:, :, ::apart],
+                out=shared_quads[:].bitcast(U32)[:, 2 * T * a : 2 * T * (a + 1)].rearrange("p (n h) -> p n h", h=2),
+                in_=rows[:].bitcast(U32)[:, at : at + (apart + 1) * T].rearrange("p (h n) -> p n h", n=T)[:, :, ::apart],
             )
 
-        def quant(c0, c1):
-            nc.vector.quantize_mx(out=cs[:, c0:c1].bitcast(FP8X4), scales=ss[:, c0:c1], in_=slots[:, 4 * c0 : 4 * c1])
+        def quantise(quads, first, count):
+            cols = slice(first, first + count)
+            nc.vector.quantize_mx(out=slot_codes[:, cols].bitcast(FP8X4), scales=slot_scale[:, cols], in_=quads)
 
-        def quant_shared(half, s0):
-            csh[half] = keep.tile([P, 2 * T], U32, name=f"gath{LAST}_{s0}", align_bytes=64)
+        def quantise_woven(first, last):
+            quantise(woven_quads[:, 4 * first : 4 * last], first, last - first)
+
+        shared_codes = {}
+
+        def quantise_shared(half, piece):
+            shared_codes[half] = aligned([P, 2 * T], U32, f"gathered{LAST}_{piece[0]}")
             first = 2 * T * half
-            for c0, c1 in ((0, 1024), (1024, 2 * T)):
+            for c0, c1 in ((0, WIDE), (WIDE, 2 * T)):
                 nc.vector.quantize_mx(
-                    out=csh[half][:, c0:c1].bitcast(FP8X4),
-                    scales=ssh[:, first + c0 : first + c1],
-                    in_=shq[:, 4 * (first + c0) : 4 * (first + c1)],
+                    out=shared_codes[half][:, c0:c1].bitcast(FP8X4),
+                    scales=shared_scale[:, first + c0 : first + c1],
+                    in_=shared_quads[:, 4 * (first + c0) : 4 * (first + c1)],
                 )
 
-        def multiply(bank, e, a, codes, scales):
+        def multiply(sums, e, a, codes, scales):
             i = e * PASSES + a
             nc.tensor.matmul_mx(
-                out=bank,
-                lhsT=words[a][:, e * 2 * N : (e + 1) * 2 * N].bitcast(FP4X4),
-                lhsT_scale=wsc[:, i * N : (i + 1) * N],
+                out=sums,
+                lhsT=w_codes[a][:, e * 2 * N : (e + 1) * 2 * N].bitcast(FP4X4),
+                lhsT_scale=w_scale[:, i * N : (i + 1) * N],
                 rhs=codes.bitcast(FP8X4),
                 rhs_scale=scales,
                 start=(a == 0),
@@ -168,9 +170,9 @@ def tile_moe_shr_lin_gelu_kernel(tc, xT, w_words, w_scales, b, gate, offs, pos1,
 
         def expert_pass(e, a):
             if a == 0:
-                banks[e] = psum.tile([P, 512], F32, name=f"bank{e % BANKS}")
+                banks[e] = psum.tile([P, BANK], F32, name=f"bank{e % BANKS}")
             cols = slice(a * S + e * C, a * S + (e + 1) * C)
-            multiply(banks[e][:, :C], e, a, cs[:, cols], ss[:, cols])
+            multiply(banks[e][:, :C], e, a, slot_codes[:, cols], slot_scale[:, cols])
 
         def early_pass(a):
             for e in range(BANKS):
@@ -186,81 +188,80 @@ def tile_moe_shr_lin_gelu_kernel(tc, xT, w_words, w_scales, b, gate, offs, pos1,
                     for a in range(LAST):
                         expert_pass(e + BANKS, a)
 
-        def shared(c0, c1, name):
-            bank = psum.tile([P, 512], F32, name=name)
+        def shared_expert(t0, t1, after):
+            bank = psum.tile([P, BANK], F32, name=f"bank{after % BANKS}")
             for a in range(PASSES):
                 at = a % 2 * T
-                multiply(bank[:, : c1 - c0], E, a, csh[a // 2][:, at + c0 : at + c1], ssh[:, a * T + c0 : a * T + c1])
-            nc.scalar.activation(out=ys[:, c0:c1], in_=bank[:, : c1 - c0], func=GELU, bias=bias[:, E : E + 1])
+                multiply(
+                    bank[:, : t1 - t0], E, a, shared_codes[a // 2][:, at + t0 : at + t1], shared_scale[:, a * T + t0 : a * T + t1]
+                )
+            nc.scalar.activation(out=ys[:, t0:t1], in_=bank[:, : t1 - t0], func=GELU, bias=bias[:, E : E + 1])
 
-        load_x(0, 1)
+        load_row(0, 1)
         nc.sync.dma_start(offs_t[:], offs)
-        load_x(1, 1)
-        load_x(0, 0)
-        cast(0, 1, 0, 384, nc.vector.tensor_copy)
-        cast(0, 1, 384, T)
-        load_x(2, 1)
-        load_x(1, 0)
-        load_x(2, 0)
-        load_x(3, 1)
-        load_x(3, 0)
-        load_rest()
-        gather(0, 1)
-        split(1)
-        cast(1, 1)
-        gather(1, 1, DIRECT, S)
-        cast(0, 0, copy=nc.gpsimd.tensor_copy)
-        gather(0, 0)
-        gather_direct(2)
-        gather_direct(3)
-        cast(2, 1, copy=nc.gpsimd.tensor_copy)
-        gather(2, 1)
-        split(0)
-        gather_direct(0)
-        gather_direct(1)
-        cast(2, 0, copy=nc.gpsimd.tensor_copy)
-        gather(2, 0)
-        cast(1, 0, copy=nc.gpsimd.tensor_copy)
-        gather(1, 0, DIRECT, S)
-        cast(3, 1, copy=nc.gpsimd.tensor_copy)
-        for s0, s1 in PIECES:
-            gather(3, 1, s0, s1)
-        cast(3, 0, copy=nc.gpsimd.tensor_copy)
-        for s0, s1 in PIECES:
-            gather(3, 0, s0, s1)
-        shq = keep.tile([P, PASSES * 4 * T], BF16, name="raw3_1", align_bytes=64)
-        ss = keep.tile([P, PASSES * S], U8, name="raw_last", align_bytes=64)
+        load_row(1, 1)
+        load_row(0, 0)
+        round_row(0, 1, nc.vector.tensor_copy, 0, FIRST_ON_VECTOR)
+        round_row(0, 1, nc.scalar.copy, FIRST_ON_VECTOR, T)
+        for a, h in ((2, 1), (1, 0), (2, 0), (3, 1), (3, 0)):
+            load_row(a, h)
+        preload_weights_and_combine_inputs()
+
+        gather_row(0, 1)
+        round_planes(1)
+        round_row(1, 1, nc.scalar.copy)
+        gather_row(1, 1, DIRECT, S)
+        round_row(0, 0, nc.gpsimd.tensor_copy)
+        gather_row(0, 0)
+        gather_plane(2)
+        gather_plane(3)
+        round_row(2, 1, nc.gpsimd.tensor_copy)
+        gather_row(2, 1)
+        round_planes(0)
+        gather_plane(0)
+        gather_plane(1)
+        round_row(2, 0, nc.gpsimd.tensor_copy)
+        gather_row(2, 0)
+        round_row(1, 0, nc.gpsimd.tensor_copy)
+        gather_row(1, 0, DIRECT, S)
+        for h in (1, 0):
+            round_row(LAST, h, nc.gpsimd.tensor_copy)
+            for s0, s1 in PIECES:
+                gather_row(LAST, h, s0, s1)
+
+        shared_quads = aligned([P, PASSES * 4 * T], BF16, "raw3_1")
+        slot_scale = aligned([P, PASSES * S], U8, "raw3_0")
         for a in range(PASSES):
             weave_shared(a)
         weave(0)
-        weave(1, DIRECT, S)
-        quant(0, 1024)
-        quant(1024, S)
+        weave(SPLIT_PASS, DIRECT, S)
+        quantise_woven(0, WIDE)
+        quantise_woven(WIDE, S)
         early_pass(0)
-        nc.vector.quantize_mx(out=cs[:, S : S + DIRECT].bitcast(FP8X4), scales=ss[:, S : S + DIRECT], in_=direct[:])
+        quantise(direct_quads[:], S, DIRECT)
         early_pass(1)
         weave(2)
-        quant(S + DIRECT, S + DIRECT + 1024)
-        quant(S + DIRECT + 1024, 3 * S)
+        quantise_woven(S + DIRECT, S + DIRECT + WIDE)
+        quantise_woven(S + DIRECT + WIDE, 3 * S)
         early_pass(2)
         for s0, s1 in PIECES:
             weave(LAST, s0, s1)
-            quant(LAST * S + s0, LAST * S + s1)
+            quantise_woven(LAST * S + s0, LAST * S + s1)
             close(s0, s1)
-        quant_shared(0, PIECES[2][0])
-        quant_shared(1, PIECES[1][0])
-        shared(0, 512, f"bank{(E - 1) % BANKS}")
-        shared(512, T, f"bank{(E - 2) % BANKS}")
+        quantise_shared(0, PIECES[2])
+        quantise_shared(1, PIECES[1])
+        shared_expert(0, BANK, E - 1)
+        shared_expert(BANK, T, E - 2)
 
-        s1 = keep.tile([P, T], F32, name="raw0_1", align_bytes=64)
-        s2 = keep.tile([P, T], F32, name="raw0_0", align_bytes=64)
-        t1 = keep.tile([P, T], F32, name="raw1_1", align_bytes=64)
-        res = keep.tile([P, T], F32, name="raw1_0", align_bytes=64)
-        nc.vector.tensor_tensor(s1[:], y[:].indirect(pos1_t[:]), gates[:, :T], MULT)
-        nc.vector.tensor_tensor(s2[:], y[:].indirect(pos2_t[:]), gates[:, T:], MULT)
-        parts = (slice(0, 384), slice(384, T))
+        first_choice = aligned([P, T], F32, "raw0_1")
+        second_choice = aligned([P, T], F32, "raw0_0")
+        routed = aligned([P, T], F32, "raw1_1")
+        total = aligned([P, T], F32, "raw1_0")
+        nc.vector.tensor_tensor(first_choice[:], y[:].indirect(pos1_t[:]), gates[:, :T], MULT)
+        nc.vector.tensor_tensor(second_choice[:], y[:].indirect(pos2_t[:]), gates[:, T:], MULT)
+        parts = (slice(0, FIRST_STORE), slice(FIRST_STORE, T))
         for cols in parts:
-            nc.vector.tensor_add(t1[:, cols], s1[:, cols], s2[:, cols])
+            nc.vector.tensor_add(routed[:, cols], first_choice[:, cols], second_choice[:, cols])
         for cols in parts:
-            nc.vector.tensor_add(res[:, cols], t1[:, cols], ys[:, cols])
-            nc.sync.dma_start(out[:, cols], res[:, cols])
+            nc.vector.tensor_add(total[:, cols], routed[:, cols], ys[:, cols])
+            nc.sync.dma_start(out[:, cols], total[:, cols])

@@ -9,11 +9,10 @@ PASSES = 4
 LAST = PASSES - 1
 FLOPS = 2 * K * N * (S + T)
 
-ROWS = [(0, 1), (1, 1), (0, 0), (2, 1), (2, 0), (1, 0), (3, 1), (3, 0)]
-SPLIT_PASS = 1
-DIRECT = 1024
-ROW_WINDOW = 1712
-PLANE_WINDOW = 1376
+PLANE_PASS = 1
+ROWS = [(0, 1), (0, 0), (2, 1), (2, 0), (3, 1), (3, 0)]
+PLANES = [3, 2, 1, 0]
+WINDOW = 1712
 FIRST_ON_VECTOR = 384
 WIDE = 1024
 PIECES = ((0, 512), (512, 1024), (1024, S))
@@ -52,28 +51,38 @@ def tile_moe_shr_lin_gelu_kernel(tc, xT, w_words, w_scales, b, gate, offs, pos1,
         y = keep.tile([P, S], F32, name="y")
         ys = keep.tile([P, T], F32, name="ys")
         w_codes = [aligned([P, (E + 1) * 2 * N], U8, f"w_codes{a}") for a in range(PASSES)]
-        woven_quads = aligned([P, PASSES * 4 * S], BF16, "woven_quads")
+        slot_quads = aligned([P, PASSES * 4 * S], BF16, "slot_quads")
         slot_codes = aligned([P, PASSES * S], U32, "slot_codes")
-        direct_quads = aligned([P, 4 * DIRECT], BF16, "direct_quads")
-        planes = aligned([P, 3 * T + PLANE_WINDOW], BF16, "planes")
-        shared_scale = aligned([P, PASSES * T], U8, "shared_scale")
-        rows = aligned([P, 2 * ((len(ROWS) - 1) * T + ROW_WINDOW)], BF16, "rows")
+        shared_codes = [aligned([P, 2 * T], U32, "shared_codes")]
+        planes = aligned([P, 3 * T + WINDOW], BF16, "planes")
+        rows = aligned([P, 2 * ((len(ROWS) - 1) * T + WINDOW)], BF16, "rows")
+        raw_planes = aligned([P, 4 * T], F32, "raw_planes")
+        gathered = [aligned([P, 2 * S], U32, f"gathered{a}") for a in range(PASSES)]
 
         def row_at(a, h):
             return T * (len(ROWS) - 1 - ROWS.index((a, h)))
 
+        def plane_at(j):
+            return T * (len(PLANES) - 1 - PLANES.index(j))
+
         nc.vector.memset(rows[:].bitcast(I32)[:, len(ROWS) * T :], 0)
-        nc.vector.memset(planes[:].bitcast(I32)[:, 2 * T : (3 * T + PLANE_WINDOW) // 2], 0)
+        nc.vector.memset(planes[:].bitcast(I32)[:, 2 * T :], 0)
         nc.gpsimd.memset(w_scale[:].bitcast(I32), 0)
 
+        x_by_pass = xT.rearrange("(a p j) t -> a p j t", p=P, j=4)
         raw = {}
 
         def load_row(a, h):
             if (a, h) == (2, 1):
-                raw[a, h] = woven_quads[:, : 4 * T].bitcast(F32).rearrange("p (e t) -> p e t", e=2)
+                raw[a, h] = slot_quads[:, : 4 * T].bitcast(F32).rearrange("p (e t) -> p e t", e=2)
             else:
                 raw[a, h] = aligned([P, 2, T], F32, f"raw{a}_{h}")
-            nc.sync.dma_start(raw[a, h][:, :, :], xT.rearrange("(a p j) t -> a p j t", p=P, j=4)[a][:, 2 * h : 2 * h + 2, :])
+            nc.sync.dma_start(raw[a, h][:, :, :], x_by_pass[a][:, 2 * h : 2 * h + 2, :])
+
+        def load_planes(j0, j1):
+            nc.sync.dma_start(
+                raw_planes[:, T * j0 : T * j1], x_by_pass[PLANE_PASS][:, j0:j1, :].rearrange("p j t -> p (j t)")
+            )
 
         def preload_weights_and_combine_inputs():
             for q in range(4):
@@ -98,70 +107,63 @@ def tile_moe_shr_lin_gelu_kernel(tc, xT, w_words, w_scales, b, gate, offs, pos1,
                 in_=raw[a, h][:, :, t0:t1].rearrange("p e t -> p t e"),
             )
 
-        def round_planes(h):
-            nc.gpsimd.tensor_copy(
-                out=planes[:, 2 * T * h : 2 * T * (h + 1)], in_=raw[SPLIT_PASS, h][:].rearrange("p e t -> p (e t)")
-            )
+        def round_plane(j, copy):
+            copy(out=planes[:, plane_at(j) : plane_at(j) + T], in_=raw_planes[:, T * j : T * (j + 1)])
 
         def gather_plane(j):
+            h, e = divmod(j, 2)
             nc.scalar.activation(
-                out=direct_quads[:].rearrange("p (n j) -> p n j", j=4)[:, :, j],
-                in_=planes[:, T * j : T * j + PLANE_WINDOW].indirect(offs_t[:, : DIRECT // 16]),
+                out=gathered[PLANE_PASS][:].bitcast(BF16)[:, 2 * S * h : 2 * S * (h + 1)].rearrange("p (n e) -> p n e", e=2)[:, :, e],
+                in_=planes[:, plane_at(j) : plane_at(j) + WINDOW].indirect(offs_t[:]),
                 func=COPY,
             )
 
-        gathered = {}
-
-        def gather_row(a, h, s0=0, s1=S):
-            if (a, s0) not in gathered:
-                gathered[a, s0] = aligned([P, 2 * T if a == LAST else 2 * S], U32, f"gathered{a}_{s0}")
-            at, width = row_at(a, h), s1 - s0
+        def gather_row(a, h):
+            at = row_at(a, h)
             nc.vector.tensor_copy(
-                gathered[a, s0][:, width * h : width * (h + 1)],
-                rows[:].bitcast(U32)[:, at : at + ROW_WINDOW].indirect(offs_t[:, s0 // 16 : s1 // 16]),
+                gathered[a][:, S * h : S * (h + 1)], rows[:].bitcast(U32)[:, at : at + WINDOW].indirect(offs_t[:])
             )
 
         def weave(a, s0=0, s1=S):
             nc.scalar.copy(
-                out=woven_quads[:].bitcast(U32)[:, 2 * (S * a + s0) : 2 * (S * a + s1)].rearrange("p (n h) -> p n h", h=2),
-                in_=gathered[a, s0][:, : 2 * (s1 - s0)].rearrange("p (h n) -> p n h", h=2),
+                out=slot_quads[:].bitcast(U32)[:, 2 * (S * a + s0) : 2 * (S * a + s1)].rearrange("p (n h) -> p n h", h=2),
+                in_=gathered[a][:].rearrange("p (h n) -> p n h", h=2)[:, s0:s1, :],
             )
 
-        def weave_shared(a):
+        def weave_shared(a, copy):
             at = row_at(a, 0)
-            apart = (row_at(a, 1) - at) // T
-            nc.gpsimd.tensor_copy(
-                out=shared_quads[:].bitcast(U32)[:, 2 * T * a : 2 * T * (a + 1)].rearrange("p (n h) -> p n h", h=2),
-                in_=rows[:].bitcast(U32)[:, at : at + (apart + 1) * T].rearrange("p (h n) -> p n h", n=T)[:, :, ::apart],
+            copy(
+                out=shared_quads[:].bitcast(I32)[:, 2 * T * a : 2 * T * (a + 1)].rearrange("p (n h) -> p n h", h=2),
+                in_=rows[:].bitcast(I32)[:, at : at + 2 * T].rearrange("p (h n) -> p n h", h=2),
             )
 
-        def quantise(quads, first, count):
-            cols = slice(first, first + count)
-            nc.vector.quantize_mx(out=slot_codes[:, cols].bitcast(FP8X4), scales=slot_scale[:, cols], in_=quads)
+        def round_shared_quads():
+            a = PLANE_PASS
+            nc.gpsimd.tensor_copy(
+                out=shared_quads[:, 4 * T * a : 4 * T * (a + 1)].rearrange("p (n j) -> p n j", j=4),
+                in_=raw_planes[:].rearrange("p (j n) -> p n j", j=4),
+            )
 
-        def quantise_woven(first, last):
-            quantise(woven_quads[:, 4 * first : 4 * last], first, last - first)
+        def quantise_slots(first, last):
+            nc.vector.quantize_mx(
+                out=slot_codes[:, first:last].bitcast(FP8X4), scales=scales[:, first:last], in_=slot_quads[:, 4 * first : 4 * last]
+            )
 
-        shared_codes = {}
+        def quantise_shared(first, last):
+            nc.vector.quantize_mx(
+                out=shared_codes[first // (2 * T)][:, first % (2 * T) : (last - 1) % (2 * T) + 1].bitcast(FP8X4),
+                scales=scales[:, PASSES * S + first : PASSES * S + last],
+                in_=shared_quads[:, 4 * first : 4 * last],
+            )
 
-        def quantise_shared(half, piece):
-            shared_codes[half] = aligned([P, 2 * T], U32, f"gathered{LAST}_{piece[0]}")
-            first = 2 * T * half
-            for c0, c1 in ((0, WIDE), (WIDE, 2 * T)):
-                nc.vector.quantize_mx(
-                    out=shared_codes[half][:, c0:c1].bitcast(FP8X4),
-                    scales=shared_scale[:, first + c0 : first + c1],
-                    in_=shared_quads[:, 4 * (first + c0) : 4 * (first + c1)],
-                )
-
-        def multiply(sums, e, a, codes, scales):
+        def multiply(sums, e, a, codes, scale_at, width):
             i = e * PASSES + a
             nc.tensor.matmul_mx(
                 out=sums,
                 lhsT=w_codes[a][:, e * 2 * N : (e + 1) * 2 * N].bitcast(FP4X4),
                 lhsT_scale=w_scale[:, i * N : (i + 1) * N],
                 rhs=codes.bitcast(FP8X4),
-                rhs_scale=scales,
+                rhs_scale=scales[:, scale_at : scale_at + width],
                 start=(a == 0),
                 stop=(a == LAST),
             )
@@ -171,8 +173,8 @@ def tile_moe_shr_lin_gelu_kernel(tc, xT, w_words, w_scales, b, gate, offs, pos1,
         def expert_pass(e, a):
             if a == 0:
                 banks[e] = psum.tile([P, BANK], F32, name=f"bank{e % BANKS}")
-            cols = slice(a * S + e * C, a * S + (e + 1) * C)
-            multiply(banks[e][:, :C], e, a, slot_codes[:, cols], slot_scale[:, cols])
+            at = a * S + e * C
+            multiply(banks[e][:, :C], e, a, slot_codes[:, at : at + C], at, C)
 
         def early_pass(a):
             for e in range(BANKS):
@@ -191,72 +193,68 @@ def tile_moe_shr_lin_gelu_kernel(tc, xT, w_words, w_scales, b, gate, offs, pos1,
         def shared_expert(t0, t1, after):
             bank = psum.tile([P, BANK], F32, name=f"bank{after % BANKS}")
             for a in range(PASSES):
-                at = a % 2 * T
-                multiply(
-                    bank[:, : t1 - t0], E, a, shared_codes[a // 2][:, at + t0 : at + t1], shared_scale[:, a * T + t0 : a * T + t1]
-                )
+                at = a * T + t0
+                multiply(bank[:, : t1 - t0], E, a, shared_codes[a // 2][:, at % (2 * T) : at % (2 * T) + t1 - t0], PASSES * S + at, t1 - t0)
             nc.scalar.activation(out=ys[:, t0:t1], in_=bank[:, : t1 - t0], func=GELU, bias=bias[:, E : E + 1])
 
         load_row(0, 1)
         nc.sync.dma_start(offs_t[:], offs)
-        load_row(1, 1)
+        load_planes(3, 4)
         load_row(0, 0)
         round_row(0, 1, nc.vector.tensor_copy, 0, FIRST_ON_VECTOR)
         round_row(0, 1, nc.scalar.copy, FIRST_ON_VECTOR, T)
-        for a, h in ((2, 1), (1, 0), (2, 0), (3, 1), (3, 0)):
+        load_planes(2, 3)
+        load_row(2, 1)
+        load_planes(0, 2)
+        for a, h in ROWS[3:]:
             load_row(a, h)
         preload_weights_and_combine_inputs()
 
         gather_row(0, 1)
-        round_planes(1)
-        round_row(1, 1, nc.scalar.copy)
-        gather_row(1, 1, DIRECT, S)
+        round_plane(3, nc.scalar.copy)
+        gather_plane(3)
         round_row(0, 0, nc.gpsimd.tensor_copy)
         gather_row(0, 0)
+        round_plane(2, nc.gpsimd.tensor_copy)
         gather_plane(2)
-        gather_plane(3)
         round_row(2, 1, nc.gpsimd.tensor_copy)
         gather_row(2, 1)
-        round_planes(0)
-        gather_plane(0)
-        gather_plane(1)
-        round_row(2, 0, nc.gpsimd.tensor_copy)
-        gather_row(2, 0)
-        round_row(1, 0, nc.gpsimd.tensor_copy)
-        gather_row(1, 0, DIRECT, S)
-        for h in (1, 0):
-            round_row(LAST, h, nc.gpsimd.tensor_copy)
-            for s0, s1 in PIECES:
-                gather_row(LAST, h, s0, s1)
+        weave(0)
+        for j in (1, 0):
+            round_plane(j, nc.gpsimd.tensor_copy)
+            gather_plane(j)
+        for a, h in ROWS[3:]:
+            round_row(a, h, nc.gpsimd.tensor_copy)
+            gather_row(a, h)
 
         shared_quads = aligned([P, PASSES * 4 * T], BF16, "raw3_1")
-        slot_scale = aligned([P, PASSES * S], U8, "raw3_0")
-        for a in range(PASSES):
-            weave_shared(a)
-        weave(0)
-        weave(SPLIT_PASS, DIRECT, S)
-        quantise_woven(0, WIDE)
-        quantise_woven(WIDE, S)
-        early_pass(0)
-        quantise(direct_quads[:], S, DIRECT)
-        early_pass(1)
+        for a in (0, 2):
+            weave_shared(a, nc.gpsimd.tensor_copy)
+        round_shared_quads()
+        weave_shared(LAST, nc.vector.tensor_copy)
+        scales = aligned([P, PASSES * (S + T)], U8, "raw_planes")
         weave(2)
-        quantise_woven(S + DIRECT, S + DIRECT + WIDE)
-        quantise_woven(S + DIRECT + WIDE, 3 * S)
-        early_pass(2)
+        weave(1)
+        for a in (0, 2, 1):
+            quantise_slots(a * S, a * S + WIDE)
+            early_pass(a)
+            quantise_slots(a * S + WIDE, (a + 1) * S)
+        quantise_shared(0, WIDE)
+        quantise_shared(WIDE, 2 * T)
         for s0, s1 in PIECES:
             weave(LAST, s0, s1)
-            quantise_woven(LAST * S + s0, LAST * S + s1)
+            quantise_slots(LAST * S + s0, LAST * S + s1)
             close(s0, s1)
-        quantise_shared(0, PIECES[2])
-        quantise_shared(1, PIECES[1])
+        shared_codes.append(aligned([P, 2 * T], U32, f"gathered{LAST}"))
+        quantise_shared(2 * T, 2 * T + WIDE)
+        quantise_shared(2 * T + WIDE, 4 * T)
         shared_expert(0, BANK, E - 1)
         shared_expert(BANK, T, E - 2)
 
         first_choice = aligned([P, T], F32, "raw0_1")
         second_choice = aligned([P, T], F32, "raw0_0")
-        routed = aligned([P, T], F32, "raw1_1")
-        total = aligned([P, T], F32, "raw1_0")
+        routed = aligned([P, T], F32, "raw2_0")
+        total = aligned([P, T], F32, "raw3_0")
         nc.vector.tensor_tensor(first_choice[:], y[:].indirect(pos1_t[:]), gates[:, :T], MULT)
         nc.vector.tensor_tensor(second_choice[:], y[:].indirect(pos2_t[:]), gates[:, T:], MULT)
         parts = (slice(0, FIRST_STORE), slice(FIRST_STORE, T))

@@ -1,6 +1,7 @@
 from contextlib import ExitStack
 
 import concourse.mybir as mybir
+from concourse.masks import make_identity
 
 K, T, E, C, N = 2048, 640, 10, 128, 128
 S = E * C
@@ -12,10 +13,13 @@ FLOPS = 2 * K * N * (S + T)
 PLANE_PASS = 1
 ROWS = [(0, 1), (0, 0), (2, 1), (2, 0), (3, 1), (3, 0)]
 PLANES = [3, 2, 1, 0]
+EARLY_ORDER = (0, 2, 1, 3)
 WINDOW = 1712
 FIRST_ON_VECTOR = 384
 WIDE = 1024
 PIECES = ((0, 512), (512, 1024), (1024, S))
+EARLY = 512
+LATE = T - EARLY
 BANKS = 8
 BANK = 512
 FIRST_STORE = 384
@@ -47,17 +51,21 @@ def tile_moe_shr_lin_gelu_kernel(tc, xT, w_words, w_scales, b, gate, offs, pos1,
         pos2_t = keep.tile([P, T // 16], U16, name="pos2_t")
         bias = keep.tile([P, E + 1], F32, name="bias")
         gates = keep.tile([P, 2 * T], F32, name="gates")
+        identity = keep.tile([P, P], F32, name="identity")
+        turned = keep.tile([P, T], F32, name="turned")
         w_scale = aligned([P, (E + 1) * PASSES * N], U8, "w_scale")
         y = keep.tile([P, S], F32, name="y")
         ys = keep.tile([P, T], F32, name="ys")
         w_codes = [aligned([P, (E + 1) * 2 * N], U8, f"w_codes{a}") for a in range(PASSES)]
         slot_quads = aligned([P, PASSES * 4 * S], BF16, "slot_quads")
         slot_codes = aligned([P, PASSES * S], U32, "slot_codes")
-        shared_codes = [aligned([P, 2 * T], U32, "shared_codes")]
+        early_codes = aligned([P, PASSES * EARLY], U32, "early_codes")
         planes = aligned([P, 3 * T + WINDOW], BF16, "planes")
         rows = aligned([P, 2 * ((len(ROWS) - 1) * T + WINDOW)], BF16, "rows")
         raw_planes = aligned([P, 4 * T], F32, "raw_planes")
-        gathered = [aligned([P, 2 * S], U32, f"gathered{a}") for a in range(PASSES)]
+        gathered = [aligned([P, 2 * S + (2 * LATE if a == LAST else 0)], U32, f"gathered{a}") for a in range(PASSES)]
+        late_quads = gathered[LAST][:, 2 * S - 6 * LATE :]
+        late_codes = aligned([P, PASSES * LATE], U32, "late_codes")
 
         def row_at(a, h):
             return T * (len(ROWS) - 1 - ROWS.index((a, h)))
@@ -68,6 +76,11 @@ def tile_moe_shr_lin_gelu_kernel(tc, xT, w_words, w_scales, b, gate, offs, pos1,
         nc.vector.memset(rows[:].bitcast(I32)[:, len(ROWS) * T :], 0)
         nc.vector.memset(planes[:].bitcast(I32)[:, 2 * T :], 0)
         nc.gpsimd.memset(w_scale[:].bitcast(I32), 0)
+
+        make_identity(nc, identity[:])
+        warm = keep.tile([P, 8], F32, name="warm")
+        nc.vector.memset(warm[:], 0.0)
+        nc.scalar.activation(out=ys[:, :8], in_=warm[:], func=GELU)
 
         x_by_pass = xT.rearrange("(a p j) t -> a p j t", p=P, j=4)
         raw = {}
@@ -90,7 +103,7 @@ def tile_moe_shr_lin_gelu_kernel(tc, xT, w_words, w_scales, b, gate, offs, pos1,
                     w_scale[32 * q : 32 * q + 4, :].bitcast(I32).rearrange("r (i n) -> r i n", n=N // 4),
                     w_scales.bitcast(I32)[:, :, 4 * q : 4 * q + 4, :].rearrange("e a r n -> r (e a) n"),
                 )
-            for a in range(PASSES):
+            for a in (0, 2, 1, 3):
                 nc.sync.dma_start(
                     w_codes[a][:].bitcast(I32).rearrange("p (e n) -> p e n", e=E + 1),
                     w_words.bitcast(I32)[:, a, :, :].rearrange("e p n -> p e n"),
@@ -127,21 +140,25 @@ def tile_moe_shr_lin_gelu_kernel(tc, xT, w_words, w_scales, b, gate, offs, pos1,
         def weave(a, s0=0, s1=S):
             nc.scalar.copy(
                 out=slot_quads[:].bitcast(U32)[:, 2 * (S * a + s0) : 2 * (S * a + s1)].rearrange("p (n h) -> p n h", h=2),
-                in_=gathered[a][:].rearrange("p (h n) -> p n h", h=2)[:, s0:s1, :],
+                in_=gathered[a][:, : 2 * S].rearrange("p (h n) -> p n h", h=2)[:, s0:s1, :],
             )
 
-        def weave_shared(a, copy):
-            at = row_at(a, 0)
+        def weave_early(a, copy):
+            at, i = row_at(a, 0), EARLY_ORDER.index(a)
             copy(
-                out=shared_quads[:].bitcast(I32)[:, 2 * T * a : 2 * T * (a + 1)].rearrange("p (n h) -> p n h", h=2),
-                in_=rows[:].bitcast(I32)[:, at : at + 2 * T].rearrange("p (h n) -> p n h", h=2),
+                out=early_quads[:].bitcast(U32)[:, 2 * EARLY * i : 2 * EARLY * (i + 1)].rearrange("p (n h) -> p n h", h=2),
+                in_=rows[:].bitcast(U32)[:, at : at + 2 * T].rearrange("p (h n) -> p n h", h=2)[:, :EARLY, :],
             )
 
-        def round_shared_quads():
-            a = PLANE_PASS
+        def weave_late():
+            nc.vector.tensor_copy(
+                out=late_quads[:, : 6 * LATE].bitcast(I32).rearrange("p (a u n h) -> p u a n h", a=3, u=2, h=2),
+                in_=rows[:].bitcast(I32)[:, : 6 * T].rearrange("p (a h t) -> p a t h", a=3, h=2)[:, :, EARLY:, :].rearrange("p a (u n) h -> p u a n h", u=2),
+            )
+
+        def round_shared_quads(quads, t0, t1):
             nc.gpsimd.tensor_copy(
-                out=shared_quads[:, 4 * T * a : 4 * T * (a + 1)].rearrange("p (n j) -> p n j", j=4),
-                in_=raw_planes[:].rearrange("p (j n) -> p n j", j=4),
+                out=quads.rearrange("p (n j) -> p n j", j=4), in_=raw_planes[:].rearrange("p (j n) -> p n j", j=4)[:, t0:t1, :]
             )
 
         def quantise_slots(first, last):
@@ -149,14 +166,14 @@ def tile_moe_shr_lin_gelu_kernel(tc, xT, w_words, w_scales, b, gate, offs, pos1,
                 out=slot_codes[:, first:last].bitcast(FP8X4), scales=scales[:, first:last], in_=slot_quads[:, 4 * first : 4 * last]
             )
 
-        def quantise_shared(first, last):
+        def quantise_shared(codes, quads, scale_at, first, last):
             nc.vector.quantize_mx(
-                out=shared_codes[first // (2 * T)][:, first % (2 * T) : (last - 1) % (2 * T) + 1].bitcast(FP8X4),
-                scales=scales[:, PASSES * S + first : PASSES * S + last],
-                in_=shared_quads[:, 4 * first : 4 * last],
+                out=codes[:, first:last].bitcast(FP8X4),
+                scales=scales[:, scale_at + first : scale_at + last],
+                in_=quads[:, 4 * first : 4 * last],
             )
 
-        def multiply(sums, e, a, codes, scale_at, width):
+        def multiply(sums, e, a, codes, scale_at, width, start, stop):
             i = e * PASSES + a
             nc.tensor.matmul_mx(
                 out=sums,
@@ -164,8 +181,8 @@ def tile_moe_shr_lin_gelu_kernel(tc, xT, w_words, w_scales, b, gate, offs, pos1,
                 lhsT_scale=w_scale[:, i * N : (i + 1) * N],
                 rhs=codes.bitcast(FP8X4),
                 rhs_scale=scales[:, scale_at : scale_at + width],
-                start=(a == 0),
-                stop=(a == LAST),
+                start=start,
+                stop=stop,
             )
 
         banks = {}
@@ -174,7 +191,7 @@ def tile_moe_shr_lin_gelu_kernel(tc, xT, w_words, w_scales, b, gate, offs, pos1,
             if a == 0:
                 banks[e] = psum.tile([P, BANK], F32, name=f"bank{e % BANKS}")
             at = a * S + e * C
-            multiply(banks[e][:, :C], e, a, slot_codes[:, at : at + C], at, C)
+            multiply(banks[e][:, :C], e, a, slot_codes[:, at : at + C], at, C, a == 0, a == LAST)
 
         def early_pass(a):
             for e in range(BANKS):
@@ -190,12 +207,12 @@ def tile_moe_shr_lin_gelu_kernel(tc, xT, w_words, w_scales, b, gate, offs, pos1,
                     for a in range(LAST):
                         expert_pass(e + BANKS, a)
 
-        def shared_expert(t0, t1, after):
+        def shared_expert(codes, scale_at, passes, t0, t1, after):
+            width = t1 - t0
             bank = psum.tile([P, BANK], F32, name=f"bank{after % BANKS}")
-            for a in range(PASSES):
-                at = a * T + t0
-                multiply(bank[:, : t1 - t0], E, a, shared_codes[a // 2][:, at % (2 * T) : at % (2 * T) + t1 - t0], PASSES * S + at, t1 - t0)
-            nc.scalar.activation(out=ys[:, t0:t1], in_=bank[:, : t1 - t0], func=GELU, bias=bias[:, E : E + 1])
+            for i, a in enumerate(passes):
+                multiply(bank[:, :width], E, a, codes[:, i * width : (i + 1) * width], scale_at + i * width, width, i == 0, i == LAST)
+            nc.scalar.activation(out=ys[:, t0:t1], in_=bank[:, :width], func=GELU, bias=bias[:, E : E + 1])
 
         load_row(0, 1)
         nc.sync.dma_start(offs_t[:], offs)
@@ -227,39 +244,53 @@ def tile_moe_shr_lin_gelu_kernel(tc, xT, w_words, w_scales, b, gate, offs, pos1,
             round_row(a, h, nc.gpsimd.tensor_copy)
             gather_row(a, h)
 
-        shared_quads = aligned([P, PASSES * 4 * T], BF16, "raw3_1")
+        early_quads = aligned([P, PASSES * 4 * EARLY], BF16, "raw3_1")
         for a in (0, 2):
-            weave_shared(a, nc.gpsimd.tensor_copy)
-        round_shared_quads()
-        weave_shared(LAST, nc.vector.tensor_copy)
+            weave_early(a, nc.gpsimd.tensor_copy)
+        round_shared_quads(late_quads[:, 6 * LATE :].bitcast(BF16), EARLY, T)
+        round_shared_quads(early_quads[:, 4 * EARLY * 2 : 4 * EARLY * 3], 0, EARLY)
         scales = aligned([P, PASSES * (S + T)], U8, "raw_planes")
+        early_scale_at, late_scale_at = PASSES * S, PASSES * (S + EARLY)
         weave(2)
         weave(1)
         for a in (0, 2, 1):
             quantise_slots(a * S, a * S + WIDE)
             early_pass(a)
             quantise_slots(a * S + WIDE, (a + 1) * S)
-        quantise_shared(0, WIDE)
-        quantise_shared(WIDE, 2 * T)
+            if a == 2:
+                quantise_shared(early_codes, early_quads, early_scale_at, 0, 2 * EARLY)
         for s0, s1 in PIECES:
+            if s1 == S:
+                quantise_shared(early_codes, early_quads, early_scale_at, 2 * EARLY, 3 * EARLY)
             weave(LAST, s0, s1)
             quantise_slots(LAST * S + s0, LAST * S + s1)
             close(s0, s1)
-        shared_codes.append(aligned([P, 2 * T], U32, f"gathered{LAST}"))
-        quantise_shared(2 * T, 2 * T + WIDE)
-        quantise_shared(2 * T + WIDE, 4 * T)
-        shared_expert(0, BANK, E - 1)
-        shared_expert(BANK, T, E - 2)
+        weave_early(LAST, nc.scalar.copy)
+        quantise_shared(early_codes, early_quads, early_scale_at, 3 * EARLY, 4 * EARLY)
+        shared_expert(early_codes, early_scale_at, EARLY_ORDER, 0, EARLY, 2)
+        weave_late()
+        quantise_shared(late_codes, late_quads.bitcast(BF16), late_scale_at, 0, PASSES * LATE)
+        shared_expert(late_codes, late_scale_at, (3, 2, 0, 1), EARLY, T, E - 2)
 
         first_choice = aligned([P, T], F32, "raw0_1")
         second_choice = aligned([P, T], F32, "raw0_0")
-        routed = aligned([P, T], F32, "raw2_0")
         total = aligned([P, T], F32, "raw3_0")
-        nc.vector.tensor_tensor(first_choice[:], y[:].indirect(pos1_t[:]), gates[:, :T], MULT)
-        nc.vector.tensor_tensor(second_choice[:], y[:].indirect(pos2_t[:]), gates[:, T:], MULT)
-        parts = (slice(0, FIRST_STORE), slice(FIRST_STORE, T))
-        for cols in parts:
-            nc.vector.tensor_add(routed[:, cols], first_choice[:, cols], second_choice[:, cols])
-        for cols in parts:
-            nc.vector.tensor_add(total[:, cols], routed[:, cols], ys[:, cols])
-            nc.sync.dma_start(out[:, cols], total[:, cols])
+        parts = ((0, FIRST_STORE), (FIRST_STORE, T))
+        sums = []
+        for i, (t0, t1) in enumerate(((0, 256), (256, EARLY), (EARLY, T))):
+            nc.vector.tensor_tensor(first_choice[:, t0:t1], y[:].indirect(pos1_t[:, t0 // 16 : t1 // 16]), gates[:, t0:t1], MULT)
+            bank = psum.tile([P, BANK], F32, name=f"bank{3 + i}")
+            for t in range(t0, t1, P):
+                cols = slice(t - t0, t - t0 + P)
+                nc.tensor.matmul(bank[:, cols], ys[:, t : t + P], identity[:], start=True, stop=False, is_transpose=True)
+                nc.tensor.matmul(bank[:, cols], first_choice[:, t : t + P], identity[:], start=False, stop=True, is_transpose=True)
+            nc.scalar.copy(out=turned[:, t0:t1], in_=bank[:, : t1 - t0])
+        for i, (t0, t1) in enumerate(parts):
+            sums.append(psum.tile([P, BANK], F32, name=f"bank{6 + i}"))
+            for t in range(t0, t1, P):
+                nc.tensor.transpose(sums[i][:, t - t0 : t - t0 + P], turned[:, t : t + P], identity[:])
+        for t0, t1 in parts:
+            nc.vector.tensor_tensor(second_choice[:, t0:t1], y[:].indirect(pos2_t[:, t0 // 16 : t1 // 16]), gates[:, T + t0 : T + t1], MULT)
+        for i, (t0, t1) in enumerate(parts):
+            nc.vector.tensor_add(total[:, t0:t1], sums[i][:, : t1 - t0], second_choice[:, t0:t1])
+            nc.sync.dma_start(out[:, t0:t1], total[:, t0:t1])

@@ -150,10 +150,10 @@ def tile_moe_shr_lin_gelu_kernel(tc, xT, w_words, w_scales, b, gate, offs, pos1,
                 in_=rows[:].bitcast(U32)[:, at : at + 2 * T].rearrange("p (h n) -> p n h", h=2)[:, :EARLY, :],
             )
 
-        def weave_late():
-            nc.vector.tensor_copy(
-                out=late_quads[:, : 6 * LATE].bitcast(I32).rearrange("p (a u n h) -> p u a n h", a=3, u=2, h=2),
-                in_=rows[:].bitcast(I32)[:, : 6 * T].rearrange("p (a h t) -> p a t h", a=3, h=2)[:, :, EARLY:, :].rearrange("p a (u n) h -> p u a n h", u=2),
+        def weave_late(copy, dtype, i0, i1):
+            copy(
+                out=late_quads[:, : 6 * LATE].bitcast(dtype).rearrange("p (a n h) -> p a n h", a=3, h=2)[:, i0:i1],
+                in_=rows[:].bitcast(dtype)[:, : 6 * T].rearrange("p (a h t) -> p a t h", a=3, h=2)[:, i0:i1, EARLY:, :],
             )
 
         def round_shared_quads(quads, t0, t1):
@@ -266,9 +266,10 @@ def tile_moe_shr_lin_gelu_kernel(tc, xT, w_words, w_scales, b, gate, offs, pos1,
             quantise_slots(LAST * S + s0, LAST * S + s1)
             close(s0, s1)
         weave_early(LAST, nc.scalar.copy)
+        weave_late(nc.scalar.copy, U32, 2, 3)
+        weave_late(nc.vector.tensor_copy, I32, 0, 2)
         quantise_shared(early_codes, early_quads, early_scale_at, 3 * EARLY, 4 * EARLY)
         shared_expert(early_codes, early_scale_at, EARLY_ORDER, 0, EARLY, 2)
-        weave_late()
         quantise_shared(late_codes, late_quads.bitcast(BF16), late_scale_at, 0, PASSES * LATE)
         shared_expert(late_codes, late_scale_at, (3, 2, 0, 1), EARLY, T, E - 2)
 
@@ -286,7 +287,7 @@ def tile_moe_shr_lin_gelu_kernel(tc, xT, w_words, w_scales, b, gate, offs, pos1,
                 nc.tensor.matmul(bank[:, cols], first_choice[:, t : t + P], identity[:], start=False, stop=True, is_transpose=True)
             nc.scalar.copy(out=turned[:, t0:t1], in_=bank[:, : t1 - t0])
         for i, (t0, t1) in enumerate(parts):
-            sums.append(psum.tile([P, BANK], F32, name=f"bank{6 + i}"))
+            sums.append(psum.tile([P, BANK], F32, name=("bank0", "bank6")[i]))
             for t in range(t0, t1, P):
                 nc.tensor.transpose(sums[i][:, t - t0 : t - t0 + P], turned[:, t : t + P], identity[:])
         for t0, t1 in parts:

@@ -13,7 +13,7 @@ FLOPS = 2 * K * N * (S + T)
 PLANE_PASS = 1
 ROWS = [(0, 1), (0, 0), (2, 1), (2, 0), (3, 1), (3, 0)]
 PLANES = [3, 2, 1, 0]
-EARLY_ORDER = (0, 2, 1, 3)
+EARLY_ORDER = (2, 0, 1, 3)
 WINDOW = 1712
 FIRST_ON_VECTOR = 384
 WIDE = 1024
@@ -63,8 +63,13 @@ def tile_moe_shr_lin_gelu_kernel(tc, xT, w_words, w_scales, b, gate, offs, pos1,
         planes = aligned([P, 3 * T + WINDOW], BF16, "planes")
         rows = aligned([P, 2 * ((len(ROWS) - 1) * T + WINDOW)], BF16, "rows")
         raw_planes = aligned([P, 4 * T], F32, "raw_planes")
-        gathered = [aligned([P, 2 * S + (2 * LATE if a == LAST else 0)], U32, f"gathered{a}") for a in range(PASSES)]
-        late_quads = gathered[LAST][:, 2 * S - 6 * LATE :]
+        shared_words = aligned([P, 6 * EARLY + 2 * T + 2 * S], U32, "shared_words")
+        early_quads = shared_words[:, : 6 * EARLY].bitcast(BF16)
+        last_words = shared_words[:, 6 * EARLY :]
+        gathered = [aligned([P, 2 * S], U32, f"gathered{a}") for a in range(LAST)] + [last_words[:, 2 * T :]]
+        plane_quads = last_words[:, : 2 * T].bitcast(BF16)
+        late_quads = last_words[:, 2 * EARLY : 2 * EARLY + 8 * LATE]
+        raw_last = shared_words[:, 6 * EARLY - T : 6 * EARLY + T].bitcast(F32).rearrange("p (e t) -> p e t", e=2)
         late_codes = aligned([P, PASSES * LATE], U32, "late_codes")
 
         def row_at(a, h):
@@ -88,6 +93,8 @@ def tile_moe_shr_lin_gelu_kernel(tc, xT, w_words, w_scales, b, gate, offs, pos1,
         def load_row(a, h):
             if (a, h) == (2, 1):
                 raw[a, h] = slot_quads[:, : 4 * T].bitcast(F32).rearrange("p (e t) -> p e t", e=2)
+            elif (a, h) == (LAST, 0):
+                raw[a, h] = raw_last
             else:
                 raw[a, h] = aligned([P, 2, T], F32, f"raw{a}_{h}")
             nc.sync.dma_start(raw[a, h][:, :, :], x_by_pass[a][:, 2 * h : 2 * h + 2, :])
@@ -120,13 +127,13 @@ def tile_moe_shr_lin_gelu_kernel(tc, xT, w_words, w_scales, b, gate, offs, pos1,
                 in_=raw[a, h][:, :, t0:t1].rearrange("p e t -> p t e"),
             )
 
-        def round_plane(j, copy):
-            copy(out=planes[:, plane_at(j) : plane_at(j) + T], in_=raw_planes[:, T * j : T * (j + 1)])
+        def round_planes(j0, j1, copy):
+            copy(out=planes[:, T * j0 : T * j1], in_=raw_planes[:, T * j0 : T * j1])
 
         def gather_plane(j):
             h, e = divmod(j, 2)
             nc.scalar.activation(
-                out=gathered[PLANE_PASS][:].bitcast(BF16)[:, 2 * S * h : 2 * S * (h + 1)].rearrange("p (n e) -> p n e", e=2)[:, :, e],
+                out=gathered[PLANE_PASS][:, :].bitcast(BF16)[:, 2 * S * h : 2 * S * (h + 1)].rearrange("p (n e) -> p n e", e=2)[:, :, e],
                 in_=planes[:, plane_at(j) : plane_at(j) + WINDOW].indirect(offs_t[:]),
                 func=COPY,
             )
@@ -143,22 +150,15 @@ def tile_moe_shr_lin_gelu_kernel(tc, xT, w_words, w_scales, b, gate, offs, pos1,
                 in_=gathered[a][:, : 2 * S].rearrange("p (h n) -> p n h", h=2)[:, s0:s1, :],
             )
 
-        def weave_early(a, copy):
-            at, i = row_at(a, 0), EARLY_ORDER.index(a)
+        def weave_shared(copy, dtype, into, i0, i1, t0, t1):
             copy(
-                out=early_quads[:].bitcast(U32)[:, 2 * EARLY * i : 2 * EARLY * (i + 1)].rearrange("p (n h) -> p n h", h=2),
-                in_=rows[:].bitcast(U32)[:, at : at + 2 * T].rearrange("p (h n) -> p n h", h=2)[:, :EARLY, :],
+                out=into.bitcast(dtype).rearrange("p (a n h) -> p a n h", a=3, h=2)[:, i0:i1],
+                in_=rows[:].bitcast(dtype)[:, : 6 * T].rearrange("p (a h t) -> p a t h", a=3, h=2)[:, i0:i1, t0:t1, :],
             )
 
-        def weave_late(copy, dtype, i0, i1):
-            copy(
-                out=late_quads[:, : 6 * LATE].bitcast(dtype).rearrange("p (a n h) -> p a n h", a=3, h=2)[:, i0:i1],
-                in_=rows[:].bitcast(dtype)[:, : 6 * T].rearrange("p (a h t) -> p a t h", a=3, h=2)[:, i0:i1, EARLY:, :],
-            )
-
-        def round_shared_quads(quads, t0, t1):
+        def round_shared_quads():
             nc.gpsimd.tensor_copy(
-                out=quads.rearrange("p (n j) -> p n j", j=4), in_=raw_planes[:].rearrange("p (j n) -> p n j", j=4)[:, t0:t1, :]
+                out=plane_quads.rearrange("p (n j) -> p n j", j=4), in_=raw_planes[:].rearrange("p (j n) -> p n j", j=4)
             )
 
         def quantise_slots(first, last):
@@ -170,7 +170,7 @@ def tile_moe_shr_lin_gelu_kernel(tc, xT, w_words, w_scales, b, gate, offs, pos1,
             nc.vector.quantize_mx(
                 out=codes[:, first:last].bitcast(FP8X4),
                 scales=scales[:, scale_at + first : scale_at + last],
-                in_=quads[:, 4 * first : 4 * last],
+                in_=quads,
             )
 
         def multiply(sums, e, a, codes, scale_at, width, start, stop):
@@ -228,27 +228,26 @@ def tile_moe_shr_lin_gelu_kernel(tc, xT, w_words, w_scales, b, gate, offs, pos1,
         preload_weights_and_combine_inputs()
 
         gather_row(0, 1)
-        round_plane(3, nc.scalar.copy)
+        round_planes(3, 4, nc.scalar.copy)
         gather_plane(3)
         round_row(0, 0, nc.gpsimd.tensor_copy)
         gather_row(0, 0)
-        round_plane(2, nc.gpsimd.tensor_copy)
+        round_planes(2, 3, nc.gpsimd.tensor_copy)
         gather_plane(2)
         round_row(2, 1, nc.gpsimd.tensor_copy)
         gather_row(2, 1)
         weave(0)
-        for j in (1, 0):
-            round_plane(j, nc.gpsimd.tensor_copy)
-            gather_plane(j)
-        for a, h in ROWS[3:]:
-            round_row(a, h, nc.gpsimd.tensor_copy)
-            gather_row(a, h)
+        round_planes(0, 2, nc.gpsimd.tensor_copy)
+        gather_plane(1)
+        gather_plane(0)
+        round_row(2, 0, nc.gpsimd.tensor_copy)
+        gather_row(2, 0)
+        for h in (1, 0):
+            round_row(LAST, h, nc.gpsimd.tensor_copy)
+            gather_row(LAST, h)
 
-        early_quads = aligned([P, PASSES * 4 * EARLY], BF16, "raw3_1")
-        for a in (0, 2):
-            weave_early(a, nc.gpsimd.tensor_copy)
-        round_shared_quads(late_quads[:, 6 * LATE :].bitcast(BF16), EARLY, T)
-        round_shared_quads(early_quads[:, 4 * EARLY * 2 : 4 * EARLY * 3], 0, EARLY)
+        weave_shared(nc.gpsimd.tensor_copy, U32, early_quads, 1, 3, 0, EARLY)
+        round_shared_quads()
         scales = aligned([P, PASSES * (S + T)], U8, "raw_planes")
         early_scale_at, late_scale_at = PASSES * S, PASSES * (S + EARLY)
         weave(2)
@@ -258,24 +257,24 @@ def tile_moe_shr_lin_gelu_kernel(tc, xT, w_words, w_scales, b, gate, offs, pos1,
             early_pass(a)
             quantise_slots(a * S + WIDE, (a + 1) * S)
             if a == 2:
-                quantise_shared(early_codes, early_quads, early_scale_at, 0, 2 * EARLY)
+                quantise_shared(early_codes, early_quads[:, 4 * EARLY :], early_scale_at, 0, 2 * EARLY)
         for s0, s1 in PIECES:
             if s1 == S:
-                quantise_shared(early_codes, early_quads, early_scale_at, 2 * EARLY, 3 * EARLY)
+                quantise_shared(early_codes, plane_quads[:, : 4 * EARLY], early_scale_at, 2 * EARLY, 3 * EARLY)
             weave(LAST, s0, s1)
             quantise_slots(LAST * S + s0, LAST * S + s1)
             close(s0, s1)
-        weave_early(LAST, nc.scalar.copy)
-        weave_late(nc.scalar.copy, U32, 2, 3)
-        weave_late(nc.vector.tensor_copy, I32, 0, 2)
-        quantise_shared(early_codes, early_quads, early_scale_at, 3 * EARLY, 4 * EARLY)
+        weave_shared(nc.scalar.copy, U32, early_quads, 0, 1, 0, EARLY)
+        weave_shared(nc.scalar.copy, U32, late_quads[:, 2 * LATE :], 2, 3, EARLY, T)
+        weave_shared(nc.vector.tensor_copy, I32, late_quads[:, 2 * LATE :], 0, 2, EARLY, T)
+        quantise_shared(early_codes, early_quads[:, : 4 * EARLY], early_scale_at, 3 * EARLY, 4 * EARLY)
         shared_expert(early_codes, early_scale_at, EARLY_ORDER, 0, EARLY, 2)
         quantise_shared(late_codes, late_quads.bitcast(BF16), late_scale_at, 0, PASSES * LATE)
-        shared_expert(late_codes, late_scale_at, (3, 2, 0, 1), EARLY, T, E - 2)
+        shared_expert(late_codes, late_scale_at, (1, 3, 2, 0), EARLY, T, E - 2)
 
         first_choice = aligned([P, T], F32, "raw0_1")
         second_choice = aligned([P, T], F32, "raw0_0")
-        total = aligned([P, T], F32, "raw3_0")
+        total = aligned([P, T], F32, "raw2_0")
         parts = ((0, FIRST_STORE), (FIRST_STORE, T))
         sums = []
         for i, (t0, t1) in enumerate(((0, 256), (256, EARLY), (EARLY, T))):

@@ -78,14 +78,14 @@ def tile_moe_shr_lin_gelu_kernel(tc, xT, w_words, w_scales, b, gate, offs, pos1,
         def plane_at(j):
             return T * (len(PLANES) - 1 - PLANES.index(j))
 
+        warm = keep.tile([P, 8], F32, name="warm")
+        nc.gpsimd.memset(warm[:], 0.0)
+        nc.scalar.activation(out=ys[:, :8], in_=warm[:], func=GELU)
         nc.vector.memset(rows[:].bitcast(I32)[:, len(ROWS) * T :], 0)
         nc.vector.memset(planes[:].bitcast(I32)[:, 2 * T :], 0)
         nc.gpsimd.memset(w_scale[:].bitcast(I32), 0)
 
         make_identity(nc, identity[:])
-        warm = keep.tile([P, 8], F32, name="warm")
-        nc.vector.memset(warm[:], 0.0)
-        nc.scalar.activation(out=ys[:, :8], in_=warm[:], func=GELU)
 
         x_by_pass = xT.rearrange("(a p j) t -> a p j t", p=P, j=4)
         raw = {}

@@ -56,7 +56,8 @@ def tile_moe_shr_lin_gelu_kernel(tc, xT, w_words, w_scales, b, gate, offs, pos1,
         w_scale = aligned([P, (E + 1) * PASSES * N], U8, "w_scale")
         y = keep.tile([P, S], F32, name="y")
         ys = keep.tile([P, T], F32, name="ys")
-        w_codes = [aligned([P, (E + 1) * 2 * N], U8, f"w_codes{a}") for a in range(PASSES)]
+        w_even = [aligned([P, (E + 1) * 2 * N], U8, f"w_codes{a}") for a in (0, 2)]
+        w_odd = aligned([P, (E + 1) * 4 * N], U8, "w_odd")
         slot_quads = aligned([P, PASSES * 4 * S], BF16, "slot_quads")
         slot_codes = aligned([P, PASSES * S], U32, "slot_codes")
         early_codes = aligned([P, PASSES * EARLY], U32, "early_codes")
@@ -110,11 +111,15 @@ def tile_moe_shr_lin_gelu_kernel(tc, xT, w_words, w_scales, b, gate, offs, pos1,
                     w_scale[32 * q : 32 * q + 4, :].bitcast(I32).rearrange("r (i n) -> r i n", n=N // 4),
                     w_scales.bitcast(I32)[:, :, 4 * q : 4 * q + 4, :].rearrange("e a r n -> r (e a) n"),
                 )
-            for a in (0, 2, 1, 3):
+            for a in (0, 2):
                 nc.sync.dma_start(
-                    w_codes[a][:].bitcast(I32).rearrange("p (e n) -> p e n", e=E + 1),
+                    w_even[a // 2][:].bitcast(I32).rearrange("p (e n) -> p e n", e=E + 1),
                     w_words.bitcast(I32)[:, a, :, :].rearrange("e p n -> p e n"),
                 )
+            nc.sync.dma_start(
+                w_odd[:].bitcast(I32).rearrange("p (i n) -> p i n", n=N // 2),
+                w_words.bitcast(I32).rearrange("e (u v) p n -> v p (e u) n", v=2)[1],
+            )
             nc.sync.dma_start(bias[:], b)
             nc.sync.dma_start(pos1_t[:], pos1)
             nc.sync.dma_start(pos2_t[:], pos2)
@@ -175,9 +180,10 @@ def tile_moe_shr_lin_gelu_kernel(tc, xT, w_words, w_scales, b, gate, offs, pos1,
 
         def multiply(sums, e, a, codes, scale_at, width, start, stop):
             i = e * PASSES + a
+            weights, at = (w_odd, i // 2) if a % 2 else (w_even[a // 2], e)
             nc.tensor.matmul_mx(
                 out=sums,
-                lhsT=w_codes[a][:, e * 2 * N : (e + 1) * 2 * N].bitcast(FP4X4),
+                lhsT=weights[:, at * 2 * N : (at + 1) * 2 * N].bitcast(FP4X4),
                 lhsT_scale=w_scale[:, i * N : (i + 1) * N],
                 rhs=codes.bitcast(FP8X4),
                 rhs_scale=scales[:, scale_at : scale_at + width],
@@ -285,12 +291,13 @@ def tile_moe_shr_lin_gelu_kernel(tc, xT, w_words, w_scales, b, gate, offs, pos1,
                 nc.tensor.matmul(bank[:, cols], ys[:, t : t + P], identity[:], start=True, stop=False, is_transpose=True)
                 nc.tensor.matmul(bank[:, cols], first_choice[:, t : t + P], identity[:], start=False, stop=True, is_transpose=True)
             nc.scalar.copy(out=turned[:, t0:t1], in_=bank[:, : t1 - t0])
-        for i, (t0, t1) in enumerate(parts):
-            sums.append(psum.tile([P, BANK], F32, name=("bank0", "bank6")[i]))
+        stores = ((0, 256), (256, EARLY), (EARLY, T))
+        for i, (t0, t1) in enumerate(stores):
+            sums.append(psum.tile([P, BANK], F32, name=("bank0", "bank6", "bank7")[i]))
             for t in range(t0, t1, P):
                 nc.tensor.transpose(sums[i][:, t - t0 : t - t0 + P], turned[:, t : t + P], identity[:])
         for t0, t1 in parts:
             nc.vector.tensor_tensor(second_choice[:, t0:t1], y[:].indirect(pos2_t[:, t0 // 16 : t1 // 16]), gates[:, T + t0 : T + t1], MULT)
-        for i, (t0, t1) in enumerate(parts):
+        for i, (t0, t1) in enumerate(stores):
             nc.vector.tensor_add(total[:, t0:t1], sums[i][:, : t1 - t0], second_choice[:, t0:t1])
             nc.sync.dma_start(out[:, t0:t1], total[:, t0:t1])

@@ -20,9 +20,9 @@ WIDE = 1024
 PIECES = ((0, 512), (512, 1024), (1024, S))
 EARLY = 512
 LATE = T - EARLY
+FETCHED = 256
 BANKS = 8
 BANK = 512
-FIRST_STORE = 384
 
 F32 = mybir.dt.float32
 BF16 = mybir.dt.bfloat16
@@ -281,8 +281,10 @@ def tile_moe_shr_lin_gelu_kernel(tc, xT, w_words, w_scales, b, gate, offs, pos1,
         first_choice = aligned([P, T], F32, "raw0_1")
         second_choice = aligned([P, T], F32, "raw0_0")
         total = aligned([P, T], F32, "raw2_0")
-        parts = ((0, FIRST_STORE), (FIRST_STORE, T))
+        stores = ((0, 256), (256, EARLY), (EARLY, T))
         sums = []
+        fetched = aligned([P, FETCHED], F32, "raw3_1")
+        nc.scalar.activation(out=fetched[:], in_=y[:].indirect(pos2_t[:, : FETCHED // 16]), func=COPY)
         for i, (t0, t1) in enumerate(((0, 256), (256, EARLY), (EARLY, T))):
             nc.vector.tensor_tensor(first_choice[:, t0:t1], y[:].indirect(pos1_t[:, t0 // 16 : t1 // 16]), gates[:, t0:t1], MULT)
             bank = psum.tile([P, BANK], F32, name=f"bank{3 + i}")
@@ -291,13 +293,12 @@ def tile_moe_shr_lin_gelu_kernel(tc, xT, w_words, w_scales, b, gate, offs, pos1,
                 nc.tensor.matmul(bank[:, cols], ys[:, t : t + P], identity[:], start=True, stop=False, is_transpose=True)
                 nc.tensor.matmul(bank[:, cols], first_choice[:, t : t + P], identity[:], start=False, stop=True, is_transpose=True)
             nc.scalar.copy(out=turned[:, t0:t1], in_=bank[:, : t1 - t0])
-        stores = ((0, 256), (256, EARLY), (EARLY, T))
         for i, (t0, t1) in enumerate(stores):
             sums.append(psum.tile([P, BANK], F32, name=("bank0", "bank6", "bank7")[i]))
             for t in range(t0, t1, P):
                 nc.tensor.transpose(sums[i][:, t - t0 : t - t0 + P], turned[:, t : t + P], identity[:])
-        for t0, t1 in parts:
-            nc.vector.tensor_tensor(second_choice[:, t0:t1], y[:].indirect(pos2_t[:, t0 // 16 : t1 // 16]), gates[:, T + t0 : T + t1], MULT)
+        nc.vector.tensor_tensor(second_choice[:, :FETCHED], fetched[:], gates[:, T : T + FETCHED], MULT)
+        nc.vector.tensor_tensor(second_choice[:, FETCHED:], y[:].indirect(pos2_t[:, FETCHED // 16 :]), gates[:, T + FETCHED :], MULT)
         for i, (t0, t1) in enumerate(stores):
             nc.vector.tensor_add(total[:, t0:t1], sums[i][:, : t1 - t0], second_choice[:, t0:t1])
             nc.sync.dma_start(out[:, t0:t1], total[:, t0:t1])

@@ -51,7 +51,6 @@ def tile_moe_shr_lin_gelu_kernel(tc, xT, w_words, w_scales, b, gate, offs, pos1,
         pos2_t = keep.tile([P, T // 16], U16, name="pos2_t")
         bias = keep.tile([P, E + 1], F32, name="bias")
         gates = keep.tile([P, 2 * T], F32, name="gates")
-        identity = keep.tile([P, P], F32, name="identity")
         turned = keep.tile([P, T], F32, name="turned")
         w_scale = aligned([P, (E + 1) * PASSES * N], U8, "w_scale")
         y = keep.tile([P, S], F32, name="y")
@@ -84,9 +83,7 @@ def tile_moe_shr_lin_gelu_kernel(tc, xT, w_words, w_scales, b, gate, offs, pos1,
         nc.scalar.activation(out=ys[:, :8], in_=warm[:], func=GELU)
         nc.vector.memset(rows[:].bitcast(I32)[:, len(ROWS) * T :], 0)
         nc.vector.memset(planes[:].bitcast(I32)[:, 2 * T :], 0)
-        nc.gpsimd.memset(w_scale[:].bitcast(I32), 0)
-
-        make_identity(nc, identity[:])
+        nc.vector.memset(w_scale[:].bitcast(I32), 0)
 
         x_by_pass = xT.rearrange("(a p j) t -> a p j t", p=P, j=4)
         raw = {}
@@ -226,6 +223,8 @@ def tile_moe_shr_lin_gelu_kernel(tc, xT, w_words, w_scales, b, gate, offs, pos1,
         load_row(0, 0)
         round_row(0, 1, nc.vector.tensor_copy, 0, FIRST_ON_VECTOR)
         round_row(0, 1, nc.scalar.copy, FIRST_ON_VECTOR, T)
+        identity = aligned([P, P], F32, "raw0_1")
+        make_identity(nc, identity[:])
         load_planes(2, 3)
         load_row(2, 1)
         load_planes(0, 2)
@@ -278,7 +277,7 @@ def tile_moe_shr_lin_gelu_kernel(tc, xT, w_words, w_scales, b, gate, offs, pos1,
         quantise_shared(late_codes, late_quads.bitcast(BF16), late_scale_at, 0, PASSES * LATE)
         shared_expert(late_codes, late_scale_at, (1, 3, 2, 0), EARLY, T, E - 2)
 
-        first_choice = aligned([P, T], F32, "raw0_1")
+        first_choice = aligned([P, T], F32, "first_choice")
         second_choice = aligned([P, T], F32, "raw0_0")
         total = aligned([P, T], F32, "raw2_0")
         stores = ((0, 256), (256, EARLY), (EARLY, T))

@@ -60,7 +60,7 @@ def tile_moe_shr_lin_gelu_kernel(tc, xT, w_words, w_scales, b, gate, offs, pos1,
         slot_quads = aligned([P, PASSES * 4 * S], BF16, "slot_quads")
         slot_codes = aligned([P, PASSES * S], U32, "slot_codes")
         early_codes = aligned([P, PASSES * EARLY], U32, "early_codes")
-        planes = aligned([P, 3 * T + WINDOW], BF16, "planes")
+        planes = slot_quads[:, 2 * 4 * S - 3 * T :][:, : 3 * T + WINDOW]
         rows = aligned([P, 2 * ((len(ROWS) - 1) * T + WINDOW)], BF16, "rows")
         raw_planes = aligned([P, 4 * T], F32, "raw_planes")
         shared_words = aligned([P, 6 * EARLY + 2 * T + 2 * S], U32, "shared_words")
@@ -82,7 +82,7 @@ def tile_moe_shr_lin_gelu_kernel(tc, xT, w_words, w_scales, b, gate, offs, pos1,
         nc.gpsimd.memset(warm[:], 0.0)
         nc.scalar.activation(out=ys[:, :8], in_=warm[:], func=GELU)
         nc.vector.memset(rows[:].bitcast(I32)[:, len(ROWS) * T :], 0)
-        nc.vector.memset(planes[:].bitcast(I32)[:, 2 * T :], 0)
+        nc.vector.memset(planes.bitcast(I32)[:, 2 * T :], 0)
         nc.vector.memset(w_scale[:].bitcast(I32), 0)
 
         x_by_pass = xT.rearrange("(a p j) t -> a p j t", p=P, j=4)
@@ -227,8 +227,9 @@ def tile_moe_shr_lin_gelu_kernel(tc, xT, w_words, w_scales, b, gate, offs, pos1,
         make_identity(nc, identity[:])
         load_planes(2, 3)
         load_row(2, 1)
+        load_row(2, 0)
         load_planes(0, 2)
-        for a, h in ROWS[3:]:
+        for a, h in ROWS[4:]:
             load_row(a, h)
         preload_weights_and_combine_inputs()
 
@@ -242,11 +243,11 @@ def tile_moe_shr_lin_gelu_kernel(tc, xT, w_words, w_scales, b, gate, offs, pos1,
         round_row(2, 1, nc.gpsimd.tensor_copy)
         gather_row(2, 1)
         weave(0)
+        round_row(2, 0, nc.gpsimd.tensor_copy)
+        gather_row(2, 0)
         round_planes(0, 2, nc.gpsimd.tensor_copy)
         gather_plane(1)
         gather_plane(0)
-        round_row(2, 0, nc.gpsimd.tensor_copy)
-        gather_row(2, 0)
         for h in (1, 0):
             round_row(LAST, h, nc.gpsimd.tensor_copy)
             gather_row(LAST, h)

@@ -257,12 +257,13 @@ def tile_moe_shr_lin_gelu_kernel(tc, xT, w_words, w_scales, b, gate, offs, pos1,
         scales = aligned([P, PASSES * (S + T)], U8, "raw_planes")
         early_scale_at, late_scale_at = PASSES * S, PASSES * (S + EARLY)
         weave(2)
-        weave(1)
+        weave(1, 0, WIDE)
+        weave(1, WIDE, S)
         for a in (0, 2, 1):
             quantise_slots(a * S, a * S + WIDE)
             early_pass(a)
             quantise_slots(a * S + WIDE, (a + 1) * S)
-            if a == 2:
+            if a == 0:
                 quantise_shared(early_codes, early_quads[:, 4 * EARLY :], early_scale_at, 0, 2 * EARLY)
         for s0, s1 in PIECES:
             if s1 == S:

@@ -55,8 +55,7 @@ def tile_moe_shr_lin_gelu_kernel(tc, xT, w_words, w_scales, b, gate, offs, pos1,
         w_scale = aligned([P, (E + 1) * PASSES * N], U8, "w_scale")
         y = keep.tile([P, S], F32, name="y")
         ys = keep.tile([P, T], F32, name="ys")
-        w_even = [aligned([P, (E + 1) * 2 * N], U8, f"w_codes{a}") for a in (0, 2)]
-        w_odd = aligned([P, (E + 1) * 4 * N], U8, "w_odd")
+        w_codes = [aligned([P, (E + 1) * 4 * N], U8, f"w_codes{v}") for v in range(2)]
         slot_quads = aligned([P, PASSES * 4 * S], BF16, "slot_quads")
         slot_codes = aligned([P, PASSES * S], U32, "slot_codes")
         early_codes = aligned([P, PASSES * EARLY], U32, "early_codes")
@@ -88,14 +87,15 @@ def tile_moe_shr_lin_gelu_kernel(tc, xT, w_words, w_scales, b, gate, offs, pos1,
         x_by_pass = xT.rearrange("(a p j) t -> a p j t", p=P, j=4)
         raw = {}
 
-        def load_row(a, h):
+        def load_row(a, h, cuts=(0, T)):
             if (a, h) == (2, 1):
                 raw[a, h] = slot_quads[:, : 4 * T].bitcast(F32).rearrange("p (e t) -> p e t", e=2)
             elif (a, h) == (LAST, 0):
                 raw[a, h] = raw_last
             else:
                 raw[a, h] = aligned([P, 2, T], F32, f"raw{a}_{h}")
-            nc.sync.dma_start(raw[a, h][:, :, :], x_by_pass[a][:, 2 * h : 2 * h + 2, :])
+            for t0, t1 in zip(cuts, cuts[1:]):
+                nc.sync.dma_start(raw[a, h][:, :, t0:t1], x_by_pass[a][:, 2 * h : 2 * h + 2, t0:t1])
 
         def load_planes(j0, j1):
             nc.sync.dma_start(
@@ -108,15 +108,11 @@ def tile_moe_shr_lin_gelu_kernel(tc, xT, w_words, w_scales, b, gate, offs, pos1,
                     w_scale[32 * q : 32 * q + 4, :].bitcast(I32).rearrange("r (i n) -> r i n", n=N // 4),
                     w_scales.bitcast(I32)[:, :, 4 * q : 4 * q + 4, :].rearrange("e a r n -> r (e a) n"),
                 )
-            for a in (0, 2):
+            for v in range(2):
                 nc.sync.dma_start(
-                    w_even[a // 2][:].bitcast(I32).rearrange("p (e n) -> p e n", e=E + 1),
-                    w_words.bitcast(I32)[:, a, :, :].rearrange("e p n -> p e n"),
+                    w_codes[v][:].bitcast(I32).rearrange("p (i n) -> p i n", n=N // 2),
+                    w_words.bitcast(I32).rearrange("e (u v) p n -> v p (e u) n", v=2)[v],
                 )
-            nc.sync.dma_start(
-                w_odd[:].bitcast(I32).rearrange("p (i n) -> p i n", n=N // 2),
-                w_words.bitcast(I32).rearrange("e (u v) p n -> v p (e u) n", v=2)[1],
-            )
             nc.sync.dma_start(bias[:], b)
             nc.sync.dma_start(pos1_t[:], pos1)
             nc.sync.dma_start(pos2_t[:], pos2)
@@ -177,7 +173,7 @@ def tile_moe_shr_lin_gelu_kernel(tc, xT, w_words, w_scales, b, gate, offs, pos1,
 
         def multiply(sums, e, a, codes, scale_at, width, start, stop):
             i = e * PASSES + a
-            weights, at = (w_odd, i // 2) if a % 2 else (w_even[a // 2], e)
+            weights, at = w_codes[a % 2], i // 2
             nc.tensor.matmul_mx(
                 out=sums,
                 lhsT=weights[:, at * 2 * N : (at + 1) * 2 * N].bitcast(FP4X4),
@@ -220,7 +216,7 @@ def tile_moe_shr_lin_gelu_kernel(tc, xT, w_words, w_scales, b, gate, offs, pos1,
         load_row(0, 1)
         nc.sync.dma_start(offs_t[:], offs)
         load_planes(3, 4)
-        load_row(0, 0)
+        load_row(0, 0, (0, T // 2, T))
         round_row(0, 1, nc.vector.tensor_copy, 0, FIRST_ON_VECTOR)
         round_row(0, 1, nc.scalar.copy, FIRST_ON_VECTOR, T)
         identity = aligned([P, P], F32, "raw0_1")
@@ -236,7 +232,8 @@ def tile_moe_shr_lin_gelu_kernel(tc, xT, w_words, w_scales, b, gate, offs, pos1,
         gather_row(0, 1)
         round_planes(3, 4, nc.scalar.copy)
         gather_plane(3)
-        round_row(0, 0, nc.gpsimd.tensor_copy)
+        round_row(0, 0, nc.gpsimd.tensor_copy, 0, T // 2)
+        round_row(0, 0, nc.gpsimd.tensor_copy, T // 2, T)
         gather_row(0, 0)
         round_planes(2, 3, nc.gpsimd.tensor_copy)
         gather_plane(2)

@@ -59,9 +59,9 @@ def tile_moe_shr_lin_gelu_kernel(tc, xT, w_words, w_scales, b, gate, offs, pos1,
         slot_quads = aligned([P, PASSES * 4 * S], BF16, "slot_quads")
         slot_codes = aligned([P, PASSES * S], U32, "slot_codes")
         early_codes = aligned([P, PASSES * EARLY], U32, "early_codes")
-        planes = slot_quads[:, 2 * 4 * S - 3 * T :][:, : 3 * T + WINDOW]
+        planes = aligned([P, 3 * T + WINDOW], BF16, "planes")
         rows = aligned([P, 2 * ((len(ROWS) - 1) * T + WINDOW)], BF16, "rows")
-        raw_planes = aligned([P, 4 * T], F32, "raw_planes")
+        raw_planes = slot_quads[:, 2 * 4 * S : 3 * 4 * S].bitcast(F32)
         shared_words = aligned([P, 6 * EARLY + 2 * T + 2 * S], U32, "shared_words")
         early_quads = shared_words[:, : 6 * EARLY].bitcast(BF16)
         last_words = shared_words[:, 6 * EARLY :]
@@ -81,7 +81,7 @@ def tile_moe_shr_lin_gelu_kernel(tc, xT, w_words, w_scales, b, gate, offs, pos1,
         nc.gpsimd.memset(warm[:], 0.0)
         nc.scalar.activation(out=ys[:, :8], in_=warm[:], func=GELU)
         nc.vector.memset(rows[:].bitcast(I32)[:, len(ROWS) * T :], 0)
-        nc.vector.memset(planes.bitcast(I32)[:, 2 * T :], 0)
+        nc.vector.memset(planes[:].bitcast(I32)[:, 2 * T :], 0)
         nc.vector.memset(w_scale[:].bitcast(I32), 0)
 
         x_by_pass = xT.rearrange("(a p j) t -> a p j t", p=P, j=4)
@@ -156,7 +156,7 @@ def tile_moe_shr_lin_gelu_kernel(tc, xT, w_words, w_scales, b, gate, offs, pos1,
 
         def round_shared_quads():
             nc.gpsimd.tensor_copy(
-                out=plane_quads.rearrange("p (n j) -> p n j", j=4), in_=raw_planes[:].rearrange("p (j n) -> p n j", j=4)
+                out=plane_quads.rearrange("p (n j) -> p n j", j=4), in_=planes[:, : 4 * T].rearrange("p (j n) -> p n j", j=4)
             )
 
         def quantise_slots(first, last):
@@ -251,7 +251,7 @@ def tile_moe_shr_lin_gelu_kernel(tc, xT, w_words, w_scales, b, gate, offs, pos1,
 
         weave_shared(nc.gpsimd.tensor_copy, U32, early_quads, 1, 3, 0, EARLY)
         round_shared_quads()
-        scales = aligned([P, PASSES * (S + T)], U8, "raw_planes")
+        scales = aligned([P, PASSES * (S + T)], U8, "planes")
         early_scale_at, late_scale_at = PASSES * S, PASSES * (S + EARLY)
         weave(2)
         weave(1, 0, WIDE)

@@ -1,27 +1,24 @@
 from contextlib import ExitStack
 
 import concourse.mybir as mybir
-from concourse.masks import make_identity
 
 K, T, E, C, N = 2048, 640, 10, 128, 128
 S = E * C
 P = 128
 PASSES = 4
-LAST = PASSES - 1
 FLOPS = 2 * K * N * (S + T)
 
 PLANE_PASS = 1
+LAST = 3
 ROWS = [(0, 1), (0, 0), (2, 1), (2, 0), (3, 1), (3, 0)]
 PLANES = [3, 2, 1, 0]
-EARLY_ORDER = (2, 0, 1, 3)
+SLOT_ORDER = (0, 2, 1, 3)
+SHARED_ORDER = (2, 0, 1, 3)
 WINDOW = 1712
 FIRST_ON_VECTOR = 384
-WIDE = 1024
-PIECES = ((0, 512), (512, 1024), (1024, S))
+FIRST_ON_SCALAR = 448
 EARLY = 512
-LATE = T - EARLY
 FETCHED = 256
-BANKS = 8
 BANK = 512
 
 F32 = mybir.dt.float32
@@ -52,24 +49,21 @@ def tile_moe_shr_lin_gelu_kernel(tc, xT, w_words, w_scales, b, gate, offs, pos1,
         bias = keep.tile([P, E + 1], F32, name="bias")
         gates = keep.tile([P, 2 * T], F32, name="gates")
         turned = keep.tile([P, T], F32, name="turned")
+        zeros = keep.tile([P, P], F32, name="zeros")
+        identity = keep.tile([P, P], F32, name="identity")
         w_scale = aligned([P, (E + 1) * PASSES * N], U8, "w_scale")
         y = keep.tile([P, S], F32, name="y")
         ys = keep.tile([P, T], F32, name="ys")
         w_codes = [aligned([P, (E + 1) * 4 * N], U8, f"w_codes{v}") for v in range(2)]
         slot_quads = aligned([P, PASSES * 4 * S], BF16, "slot_quads")
         slot_codes = aligned([P, PASSES * S], U32, "slot_codes")
-        early_codes = aligned([P, PASSES * EARLY], U32, "early_codes")
+        token_codes = aligned([P, PASSES * T], U32, "token_codes")
         planes = aligned([P, 3 * T + WINDOW], BF16, "planes")
         rows = aligned([P, 2 * ((len(ROWS) - 1) * T + WINDOW)], BF16, "rows")
-        raw_planes = slot_quads[:, 2 * 4 * S : 3 * 4 * S].bitcast(F32)
-        shared_words = aligned([P, 6 * EARLY + 2 * T + 2 * S], U32, "shared_words")
-        early_quads = shared_words[:, : 6 * EARLY].bitcast(BF16)
-        last_words = shared_words[:, 6 * EARLY :]
-        gathered = [aligned([P, 2 * S], U32, f"gathered{a}") for a in range(LAST)] + [last_words[:, 2 * T :]]
-        plane_quads = last_words[:, : 2 * T].bitcast(BF16)
-        late_quads = last_words[:, 2 * EARLY : 2 * EARLY + 8 * LATE]
-        raw_last = shared_words[:, 6 * EARLY - T : 6 * EARLY + T].bitcast(F32).rearrange("p (e t) -> p e t", e=2)
-        late_codes = aligned([P, PASSES * LATE], U32, "late_codes")
+        raw_planes = slot_quads[:, 4 * S : 2 * 4 * S].bitcast(F32)
+        token_words = aligned([P, PASSES * 2 * T], U32, "token_words")
+        gathered = [aligned([P, 2 * S], U32, f"gathered{a}") for a in range(PASSES)]
+        raw_last = token_words[:, 3 * T : 5 * T].bitcast(F32).rearrange("p (e t) -> p e t", e=2)
 
         def row_at(a, h):
             return T * (len(ROWS) - 1 - ROWS.index((a, h)))
@@ -77,9 +71,11 @@ def tile_moe_shr_lin_gelu_kernel(tc, xT, w_words, w_scales, b, gate, offs, pos1,
         def plane_at(j):
             return T * (len(PLANES) - 1 - PLANES.index(j))
 
-        warm = keep.tile([P, 8], F32, name="warm")
-        nc.gpsimd.memset(warm[:], 0.0)
-        nc.scalar.activation(out=ys[:, :8], in_=warm[:], func=GELU)
+        nc.gpsimd.memset(zeros[:], 0.0)
+        nc.scalar.activation(out=ys[:, :8], in_=zeros[:, :8], func=GELU)
+        nc.gpsimd.affine_select(
+            out=identity[:], in_=zeros[:], compare_op=mybir.AluOpType.not_equal, fill=1.0, base=0, pattern=[[-1, P]], channel_multiplier=1
+        )
         nc.vector.memset(rows[:].bitcast(I32)[:, len(ROWS) * T :], 0)
         nc.vector.memset(planes[:].bitcast(I32)[:, 2 * T :], 0)
         nc.vector.memset(w_scale[:].bitcast(I32), 0)
@@ -118,6 +114,9 @@ def tile_moe_shr_lin_gelu_kernel(tc, xT, w_words, w_scales, b, gate, offs, pos1,
             nc.sync.dma_start(pos2_t[:], pos2)
             nc.sync.dma_start(gates[:].rearrange("p (g t) -> p g t", g=2), gate.rearrange("g p t -> p g t"))
 
+        def token_quads(first, last):
+            return token_words[:, 2 * first : 2 * last]
+
         def round_row(a, h, copy, t0=0, t1=T):
             at = 2 * row_at(a, h)
             copy(
@@ -125,8 +124,8 @@ def tile_moe_shr_lin_gelu_kernel(tc, xT, w_words, w_scales, b, gate, offs, pos1,
                 in_=raw[a, h][:, :, t0:t1].rearrange("p e t -> p t e"),
             )
 
-        def round_planes(j0, j1, copy):
-            copy(out=planes[:, T * j0 : T * j1], in_=raw_planes[:, T * j0 : T * j1])
+        def round_planes(first, last, copy):
+            copy(out=planes[:, first:last], in_=raw_planes[:, first:last])
 
         def gather_plane(j):
             h, e = divmod(j, 2)
@@ -143,20 +142,24 @@ def tile_moe_shr_lin_gelu_kernel(tc, xT, w_words, w_scales, b, gate, offs, pos1,
             )
 
         def weave(a, s0=0, s1=S):
+            at = S * SLOT_ORDER.index(a)
             nc.scalar.copy(
-                out=slot_quads[:].bitcast(U32)[:, 2 * (S * a + s0) : 2 * (S * a + s1)].rearrange("p (n h) -> p n h", h=2),
+                out=slot_quads[:].bitcast(U32)[:, 2 * (at + s0) : 2 * (at + s1)].rearrange("p (n h) -> p n h", h=2),
                 in_=gathered[a][:, : 2 * S].rearrange("p (h n) -> p n h", h=2)[:, s0:s1, :],
             )
 
-        def weave_shared(copy, dtype, into, i0, i1, t0, t1):
+        def weave_tokens(copy, a, count):
+            at, into = row_at(a, 0), T * SHARED_ORDER.index(a)
             copy(
-                out=into.bitcast(dtype).rearrange("p (a n h) -> p a n h", a=3, h=2)[:, i0:i1],
-                in_=rows[:].bitcast(dtype)[:, : 6 * T].rearrange("p (a h t) -> p a t h", a=3, h=2)[:, i0:i1, t0:t1, :],
+                out=token_quads(into, into + T * count).rearrange("p (a n h) -> p a n h", a=count, h=2),
+                in_=rows[:].bitcast(U32)[:, at : at + 2 * T * count].rearrange("p (a h n) -> p a n h", a=count, h=2),
             )
 
-        def round_shared_quads():
+        def weave_token_planes():
+            into = 2 * T * SHARED_ORDER.index(PLANE_PASS)
             nc.gpsimd.tensor_copy(
-                out=plane_quads.rearrange("p (n j) -> p n j", j=4), in_=planes[:, : 4 * T].rearrange("p (j n) -> p n j", j=4)
+                out=token_words[:, into : into + 2 * T].bitcast(BF16).rearrange("p (n j) -> p n j", j=4),
+                in_=planes[:, : 4 * T].rearrange("p (j n) -> p n j", j=4),
             )
 
         def quantise_slots(first, last):
@@ -164,11 +167,11 @@ def tile_moe_shr_lin_gelu_kernel(tc, xT, w_words, w_scales, b, gate, offs, pos1,
                 out=slot_codes[:, first:last].bitcast(FP8X4), scales=scales[:, first:last], in_=slot_quads[:, 4 * first : 4 * last]
             )
 
-        def quantise_shared(codes, quads, scale_at, first, last):
+        def quantise_tokens(first, last):
             nc.vector.quantize_mx(
-                out=codes[:, first:last].bitcast(FP8X4),
-                scales=scales[:, scale_at + first : scale_at + last],
-                in_=quads,
+                out=token_codes[:, first:last].bitcast(FP8X4),
+                scales=scales[:, PASSES * S + first : PASSES * S + last],
+                in_=token_quads(first, last).bitcast(BF16),
             )
 
         def multiply(sums, e, a, codes, scale_at, width, start, stop):
@@ -184,43 +187,33 @@ def tile_moe_shr_lin_gelu_kernel(tc, xT, w_words, w_scales, b, gate, offs, pos1,
                 stop=stop,
             )
 
-        banks = {}
+        banks = [psum.tile([P, BANK], F32, name=f"bank{i}") for i in range(E // 2 + 2)]
 
-        def expert_pass(e, a):
-            if a == 0:
-                banks[e] = psum.tile([P, BANK], F32, name=f"bank{e % BANKS}")
-            at = a * S + e * C
-            multiply(banks[e][:, :C], e, a, slot_codes[:, at : at + C], at, C, a == 0, a == LAST)
+        def slots_step(first, last):
+            quantise_slots(first, last)
+            done = [(SLOT_ORDER[at // S], at % S // C, at) for at in range(first, last, C)]
+            for a, e, at in sorted(done, key=lambda pass_of: pass_of[0] != LAST):
+                sums = banks[e // 2][:, e % 2 * C : (e % 2 + 1) * C]
+                multiply(sums, e, a, slot_codes[:, at : at + C], at, C, a == SLOT_ORDER[0] and e % 2 == 0, a == LAST and e % 2 == 1)
+            for a, e, at in done:
+                if a == LAST:
+                    sums = banks[e // 2][:, e % 2 * C : (e % 2 + 1) * C]
+                    nc.scalar.activation(out=y[:, e * C : (e + 1) * C], in_=sums, func=GELU, bias=bias[:, e : e + 1])
 
-        def early_pass(a):
-            for e in range(BANKS):
-                expert_pass(e, a)
-
-        def close(s0, s1):
-            group = range(s0 // C, s1 // C)
-            for e in group:
-                expert_pass(e, LAST)
-            for e in group:
-                nc.scalar.activation(out=y[:, e * C : (e + 1) * C], in_=banks[e][:, :C], func=GELU, bias=bias[:, e : e + 1])
-                if e + BANKS < E:
-                    for a in range(LAST):
-                        expert_pass(e + BANKS, a)
-
-        def shared_expert(codes, scale_at, passes, t0, t1, after):
-            width = t1 - t0
-            bank = psum.tile([P, BANK], F32, name=f"bank{after % BANKS}")
-            for i, a in enumerate(passes):
-                multiply(bank[:, :width], E, a, codes[:, i * width : (i + 1) * width], scale_at + i * width, width, i == 0, i == LAST)
-            nc.scalar.activation(out=ys[:, t0:t1], in_=bank[:, :width], func=GELU, bias=bias[:, E : E + 1])
+        def tokens_step(first, last):
+            quantise_tokens(first, last)
+            for i, a in enumerate(SHARED_ORDER):
+                for lot, (t0, t1) in enumerate(((0, EARLY), (EARLY, T))):
+                    if first < i * T + t1 <= last:
+                        at, sums = i * T + t0, banks[E // 2 + lot][:, : t1 - t0]
+                        multiply(sums, E, a, token_codes[:, at : at + t1 - t0], PASSES * S + at, t1 - t0, i == 0, a == LAST)
+                        if a == LAST:
+                            nc.scalar.activation(out=ys[:, t0:t1], in_=sums, func=GELU, bias=bias[:, E : E + 1])
 
         load_row(0, 1)
         nc.sync.dma_start(offs_t[:], offs)
         load_planes(3, 4)
         load_row(0, 0, (0, T // 2, T))
-        round_row(0, 1, nc.vector.tensor_copy, 0, FIRST_ON_VECTOR)
-        round_row(0, 1, nc.scalar.copy, FIRST_ON_VECTOR, T)
-        identity = aligned([P, P], F32, "raw0_1")
-        make_identity(nc, identity[:])
         load_planes(2, 3)
         load_row(2, 1)
         load_row(2, 0)
@@ -229,52 +222,51 @@ def tile_moe_shr_lin_gelu_kernel(tc, xT, w_words, w_scales, b, gate, offs, pos1,
             load_row(a, h)
         preload_weights_and_combine_inputs()
 
+        round_row(0, 1, nc.vector.tensor_copy, 0, FIRST_ON_VECTOR)
+        round_row(0, 1, nc.scalar.copy, FIRST_ON_VECTOR, T)
         gather_row(0, 1)
-        round_planes(3, 4, nc.scalar.copy)
+        round_planes(3 * T, 3 * T + FIRST_ON_SCALAR, nc.scalar.copy)
+        round_planes(3 * T + FIRST_ON_SCALAR, 4 * T, nc.gpsimd.tensor_copy)
         gather_plane(3)
         round_row(0, 0, nc.gpsimd.tensor_copy, 0, T // 2)
         round_row(0, 0, nc.gpsimd.tensor_copy, T // 2, T)
         gather_row(0, 0)
-        round_planes(2, 3, nc.gpsimd.tensor_copy)
+        round_planes(2 * T, 3 * T, nc.gpsimd.tensor_copy)
         gather_plane(2)
         round_row(2, 1, nc.gpsimd.tensor_copy)
         gather_row(2, 1)
         weave(0)
         round_row(2, 0, nc.gpsimd.tensor_copy)
         gather_row(2, 0)
-        round_planes(0, 2, nc.gpsimd.tensor_copy)
+        round_planes(0, 2 * T, nc.gpsimd.tensor_copy)
         gather_plane(1)
         gather_plane(0)
         for h in (1, 0):
             round_row(LAST, h, nc.gpsimd.tensor_copy)
             gather_row(LAST, h)
 
-        weave_shared(nc.gpsimd.tensor_copy, U32, early_quads, 1, 3, 0, EARLY)
-        round_shared_quads()
+        weave_tokens(nc.gpsimd.tensor_copy, 2, 2)
+        weave_token_planes()
         scales = aligned([P, PASSES * (S + T)], U8, "planes")
-        early_scale_at, late_scale_at = PASSES * S, PASSES * (S + EARLY)
         weave(2)
-        weave(1, 0, WIDE)
-        weave(1, WIDE, S)
-        for a in (0, 2, 1):
-            quantise_slots(a * S, a * S + WIDE)
-            early_pass(a)
-            quantise_slots(a * S + WIDE, (a + 1) * S)
-            if a == 0:
-                quantise_shared(early_codes, early_quads[:, 4 * EARLY :], early_scale_at, 0, 2 * EARLY)
-        for s0, s1 in PIECES:
-            if s1 == S:
-                quantise_shared(early_codes, plane_quads[:, : 4 * EARLY], early_scale_at, 2 * EARLY, 3 * EARLY)
-            weave(LAST, s0, s1)
-            quantise_slots(LAST * S + s0, LAST * S + s1)
-            close(s0, s1)
-        weave_shared(nc.scalar.copy, U32, early_quads, 0, 1, 0, EARLY)
-        weave_shared(nc.scalar.copy, U32, late_quads[:, 2 * LATE :], 2, 3, EARLY, T)
-        weave_shared(nc.vector.tensor_copy, I32, late_quads[:, 2 * LATE :], 0, 2, EARLY, T)
-        quantise_shared(early_codes, early_quads[:, : 4 * EARLY], early_scale_at, 3 * EARLY, 4 * EARLY)
-        shared_expert(early_codes, early_scale_at, EARLY_ORDER, 0, EARLY, 2)
-        quantise_shared(late_codes, late_quads.bitcast(BF16), late_scale_at, 0, PASSES * LATE)
-        shared_expert(late_codes, late_scale_at, (1, 3, 2, 0), EARLY, T, E - 2)
+        weave(1, 0, 512)
+        weave(1, 512, S)
+        weave(LAST, 0, 256)
+        weave(LAST, 256, 768)
+        weave(LAST, 768, S)
+        slots_step(0, 1024)
+        slots_step(1024, 2048)
+        tokens_step(0, 1024)
+        slots_step(2048, 3072)
+        slots_step(3072, 4096)
+        weave_tokens(nc.scalar.copy, LAST, 1)
+        tokens_step(1024, 1536)
+        slots_step(4096, 4608)
+        slots_step(4608, 4864)
+        slots_step(4864, 5120)
+        tokens_step(1536, 3 * T)
+        tokens_step(3 * T, 3 * T + EARLY)
+        tokens_step(3 * T + EARLY, 4 * T)
 
         first_choice = aligned([P, T], F32, "first_choice")
         second_choice = aligned([P, T], F32, "raw0_0")
@@ -283,16 +275,16 @@ def tile_moe_shr_lin_gelu_kernel(tc, xT, w_words, w_scales, b, gate, offs, pos1,
         sums = []
         fetched = aligned([P, FETCHED], F32, "raw3_1")
         nc.scalar.activation(out=fetched[:], in_=y[:].indirect(pos2_t[:, : FETCHED // 16]), func=COPY)
-        for i, (t0, t1) in enumerate(((0, 256), (256, EARLY), (EARLY, T))):
+        for i, (t0, t1) in enumerate(stores):
             nc.vector.tensor_tensor(first_choice[:, t0:t1], y[:].indirect(pos1_t[:, t0 // 16 : t1 // 16]), gates[:, t0:t1], MULT)
-            bank = psum.tile([P, BANK], F32, name=f"bank{3 + i}")
+            bank = psum.tile([P, BANK], F32, name=("bank7", "bank0", "bank1")[i])
             for t in range(t0, t1, P):
                 cols = slice(t - t0, t - t0 + P)
                 nc.tensor.matmul(bank[:, cols], ys[:, t : t + P], identity[:], start=True, stop=False, is_transpose=True)
                 nc.tensor.matmul(bank[:, cols], first_choice[:, t : t + P], identity[:], start=False, stop=True, is_transpose=True)
             nc.scalar.copy(out=turned[:, t0:t1], in_=bank[:, : t1 - t0])
         for i, (t0, t1) in enumerate(stores):
-            sums.append(psum.tile([P, BANK], F32, name=("bank0", "bank6", "bank7")[i]))
+            sums.append(psum.tile([P, BANK], F32, name=f"bank{2 + i}"))
             for t in range(t0, t1, P):
                 nc.tensor.transpose(sums[i][:, t - t0 : t - t0 + P], turned[:, t : t + P], identity[:])
         nc.vector.tensor_tensor(second_choice[:, :FETCHED], fetched[:], gates[:, T : T + FETCHED], MULT)

@@ -1,23 +1,24 @@
 from contextlib import ExitStack
 
 import concourse.mybir as mybir
+from concourse.masks import make_identity
 
 K, T, E, C, N = 2048, 640, 10, 128, 128
 S = E * C
 P = 128
 PASSES = 4
+LAST = PASSES - 1
 FLOPS = 2 * K * N * (S + T)
 
 PLANE_PASS = 1
-LAST = 3
 ROWS = [(0, 1), (0, 0), (2, 1), (2, 0), (3, 1), (3, 0)]
 PLANES = [3, 2, 1, 0]
 SLOT_ORDER = (0, 2, 1, 3)
-SHARED_ORDER = (2, 0, 1, 3)
 WINDOW = 1712
 FIRST_ON_VECTOR = 384
-FIRST_ON_SCALAR = 448
+WIDE = 1024
 EARLY = 512
+LATE = T - EARLY
 FETCHED = 256
 BANK = 512
 
@@ -49,21 +50,26 @@ def tile_moe_shr_lin_gelu_kernel(tc, xT, w_words, w_scales, b, gate, offs, pos1,
         bias = keep.tile([P, E + 1], F32, name="bias")
         gates = keep.tile([P, 2 * T], F32, name="gates")
         turned = keep.tile([P, T], F32, name="turned")
-        zeros = keep.tile([P, P], F32, name="zeros")
-        identity = keep.tile([P, P], F32, name="identity")
         w_scale = aligned([P, (E + 1) * PASSES * N], U8, "w_scale")
         y = keep.tile([P, S], F32, name="y")
         ys = keep.tile([P, T], F32, name="ys")
         w_codes = [aligned([P, (E + 1) * 4 * N], U8, f"w_codes{v}") for v in range(2)]
         slot_quads = aligned([P, PASSES * 4 * S], BF16, "slot_quads")
         slot_codes = aligned([P, PASSES * S], U32, "slot_codes")
-        token_codes = aligned([P, PASSES * T], U32, "token_codes")
+        early_codes = aligned([P, 2 * EARLY], U32, "early_codes")
+        plane_codes = slot_codes[:, LAST * S - 2 * C : LAST * S + 2 * C]
+        last_codes = slot_codes[:, LAST * S + 2 * C : LAST * S + 6 * C]
+        late_codes = slot_codes[:, LAST * S + 6 * C :]
         planes = aligned([P, 3 * T + WINDOW], BF16, "planes")
         rows = aligned([P, 2 * ((len(ROWS) - 1) * T + WINDOW)], BF16, "rows")
         raw_planes = slot_quads[:, 4 * S : 2 * 4 * S].bitcast(F32)
-        token_words = aligned([P, PASSES * 2 * T], U32, "token_words")
-        gathered = [aligned([P, 2 * S], U32, f"gathered{a}") for a in range(PASSES)]
-        raw_last = token_words[:, 3 * T : 5 * T].bitcast(F32).rearrange("p (e t) -> p e t", e=2)
+        shared_words = aligned([P, 6 * EARLY + 2 * T + 2 * S], U32, "shared_words")
+        early_quads = shared_words[:, : 6 * EARLY].bitcast(BF16)
+        last_words = shared_words[:, 6 * EARLY :]
+        gathered = [aligned([P, 2 * S], U32, f"gathered{a}") for a in range(LAST)] + [last_words[:, 2 * T :]]
+        plane_quads = last_words[:, : 2 * T].bitcast(BF16)
+        late_quads = last_words[:, 2 * EARLY : 2 * EARLY + 8 * LATE]
+        raw_last = shared_words[:, 6 * EARLY - T : 6 * EARLY + T].bitcast(F32).rearrange("p (e t) -> p e t", e=2)
 
         def row_at(a, h):
             return T * (len(ROWS) - 1 - ROWS.index((a, h)))
@@ -71,11 +77,9 @@ def tile_moe_shr_lin_gelu_kernel(tc, xT, w_words, w_scales, b, gate, offs, pos1,
         def plane_at(j):
             return T * (len(PLANES) - 1 - PLANES.index(j))
 
-        nc.gpsimd.memset(zeros[:], 0.0)
-        nc.scalar.activation(out=ys[:, :8], in_=zeros[:, :8], func=GELU)
-        nc.gpsimd.affine_select(
-            out=identity[:], in_=zeros[:], compare_op=mybir.AluOpType.not_equal, fill=1.0, base=0, pattern=[[-1, P]], channel_multiplier=1
-        )
+        warm = keep.tile([P, 8], F32, name="warm")
+        nc.gpsimd.memset(warm[:], 0.0)
+        nc.scalar.activation(out=ys[:, :8], in_=warm[:], func=GELU)
         nc.vector.memset(rows[:].bitcast(I32)[:, len(ROWS) * T :], 0)
         nc.vector.memset(planes[:].bitcast(I32)[:, 2 * T :], 0)
         nc.vector.memset(w_scale[:].bitcast(I32), 0)
@@ -114,9 +118,6 @@ def tile_moe_shr_lin_gelu_kernel(tc, xT, w_words, w_scales, b, gate, offs, pos1,
             nc.sync.dma_start(pos2_t[:], pos2)
             nc.sync.dma_start(gates[:].rearrange("p (g t) -> p g t", g=2), gate.rearrange("g p t -> p g t"))
 
-        def token_quads(first, last):
-            return token_words[:, 2 * first : 2 * last]
-
         def round_row(a, h, copy, t0=0, t1=T):
             at = 2 * row_at(a, h)
             copy(
@@ -124,8 +125,8 @@ def tile_moe_shr_lin_gelu_kernel(tc, xT, w_words, w_scales, b, gate, offs, pos1,
                 in_=raw[a, h][:, :, t0:t1].rearrange("p e t -> p t e"),
             )
 
-        def round_planes(first, last, copy):
-            copy(out=planes[:, first:last], in_=raw_planes[:, first:last])
+        def round_planes(j0, j1, copy):
+            copy(out=planes[:, T * j0 : T * j1], in_=raw_planes[:, T * j0 : T * j1])
 
         def gather_plane(j):
             h, e = divmod(j, 2)
@@ -148,18 +149,15 @@ def tile_moe_shr_lin_gelu_kernel(tc, xT, w_words, w_scales, b, gate, offs, pos1,
                 in_=gathered[a][:, : 2 * S].rearrange("p (h n) -> p n h", h=2)[:, s0:s1, :],
             )
 
-        def weave_tokens(copy, a, count):
-            at, into = row_at(a, 0), T * SHARED_ORDER.index(a)
+        def weave_shared(copy, dtype, into, i0, i1, t0, t1):
             copy(
-                out=token_quads(into, into + T * count).rearrange("p (a n h) -> p a n h", a=count, h=2),
-                in_=rows[:].bitcast(U32)[:, at : at + 2 * T * count].rearrange("p (a h n) -> p a n h", a=count, h=2),
+                out=into.bitcast(dtype).rearrange("p (a n h) -> p a n h", a=3, h=2)[:, i0:i1],
+                in_=rows[:].bitcast(dtype)[:, : 6 * T].rearrange("p (a h t) -> p a t h", a=3, h=2)[:, i0:i1, t0:t1, :],
             )
 
-        def weave_token_planes():
-            into = 2 * T * SHARED_ORDER.index(PLANE_PASS)
+        def round_shared_quads():
             nc.gpsimd.tensor_copy(
-                out=token_words[:, into : into + 2 * T].bitcast(BF16).rearrange("p (n j) -> p n j", j=4),
-                in_=planes[:, : 4 * T].rearrange("p (j n) -> p n j", j=4),
+                out=plane_quads.rearrange("p (n j) -> p n j", j=4), in_=planes[:, : 4 * T].rearrange("p (j n) -> p n j", j=4)
             )
 
         def quantise_slots(first, last):
@@ -167,12 +165,8 @@ def tile_moe_shr_lin_gelu_kernel(tc, xT, w_words, w_scales, b, gate, offs, pos1,
                 out=slot_codes[:, first:last].bitcast(FP8X4), scales=scales[:, first:last], in_=slot_quads[:, 4 * first : 4 * last]
             )
 
-        def quantise_tokens(first, last):
-            nc.vector.quantize_mx(
-                out=token_codes[:, first:last].bitcast(FP8X4),
-                scales=scales[:, PASSES * S + first : PASSES * S + last],
-                in_=token_quads(first, last).bitcast(BF16),
-            )
+        def quantise_shared(codes, quads, scale_at):
+            nc.vector.quantize_mx(out=codes.bitcast(FP8X4), scales=scales[:, scale_at : scale_at + codes.shape[1]], in_=quads)
 
         def multiply(sums, e, a, codes, scale_at, width, start, stop):
             i = e * PASSES + a
@@ -200,20 +194,21 @@ def tile_moe_shr_lin_gelu_kernel(tc, xT, w_words, w_scales, b, gate, offs, pos1,
                     sums = banks[e // 2][:, e % 2 * C : (e % 2 + 1) * C]
                     nc.scalar.activation(out=y[:, e * C : (e + 1) * C], in_=sums, func=GELU, bias=bias[:, e : e + 1])
 
-        def tokens_step(first, last):
-            quantise_tokens(first, last)
-            for i, a in enumerate(SHARED_ORDER):
-                for lot, (t0, t1) in enumerate(((0, EARLY), (EARLY, T))):
-                    if first < i * T + t1 <= last:
-                        at, sums = i * T + t0, banks[E // 2 + lot][:, : t1 - t0]
-                        multiply(sums, E, a, token_codes[:, at : at + t1 - t0], PASSES * S + at, t1 - t0, i == 0, a == LAST)
-                        if a == LAST:
-                            nc.scalar.activation(out=ys[:, t0:t1], in_=sums, func=GELU, bias=bias[:, E : E + 1])
+        def shared_pass(lot, a, codes, scale_at, start, stop):
+            t0, t1 = ((0, EARLY), (EARLY, T))[lot]
+            sums = banks[E // 2 + lot][:, : t1 - t0]
+            multiply(sums, E, a, codes, scale_at, t1 - t0, start, stop)
+            if stop:
+                nc.scalar.activation(out=ys[:, t0:t1], in_=sums, func=GELU, bias=bias[:, E : E + 1])
 
         load_row(0, 1)
         nc.sync.dma_start(offs_t[:], offs)
         load_planes(3, 4)
         load_row(0, 0, (0, T // 2, T))
+        round_row(0, 1, nc.vector.tensor_copy, 0, FIRST_ON_VECTOR)
+        round_row(0, 1, nc.scalar.copy, FIRST_ON_VECTOR, T)
+        identity = aligned([P, P], F32, "raw0_1")
+        make_identity(nc, identity[:])
         load_planes(2, 3)
         load_row(2, 1)
         load_row(2, 0)
@@ -222,51 +217,54 @@ def tile_moe_shr_lin_gelu_kernel(tc, xT, w_words, w_scales, b, gate, offs, pos1,
             load_row(a, h)
         preload_weights_and_combine_inputs()
 
-        round_row(0, 1, nc.vector.tensor_copy, 0, FIRST_ON_VECTOR)
-        round_row(0, 1, nc.scalar.copy, FIRST_ON_VECTOR, T)
         gather_row(0, 1)
-        round_planes(3 * T, 3 * T + FIRST_ON_SCALAR, nc.scalar.copy)
-        round_planes(3 * T + FIRST_ON_SCALAR, 4 * T, nc.gpsimd.tensor_copy)
+        round_planes(3, 4, nc.scalar.copy)
         gather_plane(3)
         round_row(0, 0, nc.gpsimd.tensor_copy, 0, T // 2)
         round_row(0, 0, nc.gpsimd.tensor_copy, T // 2, T)
         gather_row(0, 0)
-        round_planes(2 * T, 3 * T, nc.gpsimd.tensor_copy)
+        round_planes(2, 3, nc.gpsimd.tensor_copy)
         gather_plane(2)
         round_row(2, 1, nc.gpsimd.tensor_copy)
         gather_row(2, 1)
         weave(0)
         round_row(2, 0, nc.gpsimd.tensor_copy)
         gather_row(2, 0)
-        round_planes(0, 2 * T, nc.gpsimd.tensor_copy)
+        round_planes(0, 2, nc.gpsimd.tensor_copy)
         gather_plane(1)
         gather_plane(0)
         for h in (1, 0):
             round_row(LAST, h, nc.gpsimd.tensor_copy)
             gather_row(LAST, h)
 
-        weave_tokens(nc.gpsimd.tensor_copy, 2, 2)
-        weave_token_planes()
+        weave_shared(nc.gpsimd.tensor_copy, U32, early_quads, 1, 3, 0, EARLY)
+        round_shared_quads()
         scales = aligned([P, PASSES * (S + T)], U8, "planes")
+        early_scale_at, late_scale_at = PASSES * S, PASSES * (S + EARLY)
         weave(2)
         weave(1, 0, 512)
         weave(1, 512, S)
         weave(LAST, 0, 256)
         weave(LAST, 256, 768)
         weave(LAST, 768, S)
-        slots_step(0, 1024)
-        slots_step(1024, 2048)
-        tokens_step(0, 1024)
-        slots_step(2048, 3072)
-        slots_step(3072, 4096)
-        weave_tokens(nc.scalar.copy, LAST, 1)
-        tokens_step(1024, 1536)
-        slots_step(4096, 4608)
-        slots_step(4608, 4864)
-        slots_step(4864, 5120)
-        tokens_step(1536, 3 * T)
-        tokens_step(3 * T, 3 * T + EARLY)
-        tokens_step(3 * T + EARLY, 4 * T)
+        weave_shared(nc.scalar.copy, U32, early_quads, 0, 1, 0, EARLY)
+        weave_shared(nc.scalar.copy, U32, late_quads[:, 2 * LATE :], 2, 3, EARLY, T)
+        slots_step(0, WIDE)
+        quantise_shared(early_codes[:, : 2 * EARLY], early_quads[:, 4 * EARLY :], early_scale_at)
+        for i, a in enumerate((2, 0)):
+            shared_pass(0, a, early_codes[:, i * EARLY : (i + 1) * EARLY], early_scale_at + i * EARLY, i == 0, False)
+        for first in range(WIDE, 4 * WIDE, WIDE):
+            slots_step(first, first + WIDE)
+        slots_step(4 * WIDE, 4 * WIDE + 512)
+        slots_step(4 * WIDE + 512, 5 * WIDE)
+        weave_shared(nc.vector.tensor_copy, I32, late_quads[:, 2 * LATE :], 0, 2, EARLY, T)
+        quantise_shared(plane_codes, plane_quads[:, : 4 * EARLY], early_scale_at + 2 * EARLY)
+        shared_pass(0, PLANE_PASS, plane_codes, early_scale_at + 2 * EARLY, False, False)
+        quantise_shared(last_codes, early_quads[:, : 4 * EARLY], early_scale_at + 3 * EARLY)
+        shared_pass(0, LAST, last_codes, early_scale_at + 3 * EARLY, False, True)
+        quantise_shared(late_codes, late_quads.bitcast(BF16), late_scale_at)
+        for i, a in enumerate((1, 3, 2, 0)):
+            shared_pass(1, a, late_codes[:, i * LATE : (i + 1) * LATE], late_scale_at + i * LATE, i == 0, i == LAST)
 
         first_choice = aligned([P, T], F32, "first_choice")
         second_choice = aligned([P, T], F32, "raw0_0")
@@ -275,7 +273,7 @@ def tile_moe_shr_lin_gelu_kernel(tc, xT, w_words, w_scales, b, gate, offs, pos1,
         sums = []
         fetched = aligned([P, FETCHED], F32, "raw3_1")
         nc.scalar.activation(out=fetched[:], in_=y[:].indirect(pos2_t[:, : FETCHED // 16]), func=COPY)
-        for i, (t0, t1) in enumerate(stores):
+        for i, (t0, t1) in enumerate(((0, 256), (256, EARLY), (EARLY, T))):
             nc.vector.tensor_tensor(first_choice[:, t0:t1], y[:].indirect(pos1_t[:, t0 // 16 : t1 // 16]), gates[:, t0:t1], MULT)
             bank = psum.tile([P, BANK], F32, name=("bank7", "bank0", "bank1")[i])
             for t in range(t0, t1, P):

@@ -19,6 +19,7 @@ FIRST_ON_VECTOR = 384
 WIDE = 1024
 EARLY = 512
 LATE = T - EARLY
+RUN = 4
 FETCHED = 256
 BANK = 512
 
@@ -63,10 +64,10 @@ def tile_moe_shr_lin_gelu_kernel(tc, xT, w_words, w_scales, b, gate, offs, pos1,
         planes = aligned([P, 3 * T + WINDOW], BF16, "planes")
         rows = aligned([P, 2 * ((len(ROWS) - 1) * T + WINDOW)], BF16, "rows")
         raw_planes = slot_quads[:, 4 * S : 2 * 4 * S].bitcast(F32)
-        shared_words = aligned([P, 6 * EARLY + 2 * T + 2 * S], U32, "shared_words")
+        shared_words = aligned([P, 6 * EARLY + 2 * T + 6 * LATE], U32, "shared_words")
         early_quads = shared_words[:, : 6 * EARLY].bitcast(BF16)
         last_words = shared_words[:, 6 * EARLY :]
-        gathered = [aligned([P, 2 * S], U32, f"gathered{a}") for a in range(LAST)] + [last_words[:, 2 * T :]]
+        gathered = [aligned([P, 2 * S], U32, f"gathered{a}") for a in range(PASSES)]
         plane_quads = last_words[:, : 2 * T].bitcast(BF16)
         late_quads = last_words[:, 2 * EARLY : 2 * EARLY + 8 * LATE]
         raw_last = shared_words[:, 6 * EARLY - T : 6 * EARLY + T].bitcast(F32).rearrange("p (e t) -> p e t", e=2)
@@ -118,11 +119,11 @@ def tile_moe_shr_lin_gelu_kernel(tc, xT, w_words, w_scales, b, gate, offs, pos1,
             nc.sync.dma_start(pos2_t[:], pos2)
             nc.sync.dma_start(gates[:].rearrange("p (g t) -> p g t", g=2), gate.rearrange("g p t -> p g t"))
 
-        def round_row(a, h, copy, t0=0, t1=T):
+        def round_row(a, h, copy, t0=0, t1=T, run=1):
             at = 2 * row_at(a, h)
             copy(
-                out=rows[:, at : at + 2 * T].rearrange("p (t e) -> p t e", e=2)[:, t0:t1, :],
-                in_=raw[a, h][:, :, t0:t1].rearrange("p e t -> p t e"),
+                out=rows[:, at + 2 * t0 : at + 2 * t1].rearrange("p (c i e) -> p c e i", e=2, i=run),
+                in_=raw[a, h][:, :, t0:t1].rearrange("p e (c i) -> p c e i", i=run),
             )
 
         def round_planes(j0, j1, copy):
@@ -149,15 +150,16 @@ def tile_moe_shr_lin_gelu_kernel(tc, xT, w_words, w_scales, b, gate, offs, pos1,
                 in_=gathered[a][:, : 2 * S].rearrange("p (h n) -> p n h", h=2)[:, s0:s1, :],
             )
 
-        def weave_shared(copy, dtype, into, i0, i1, t0, t1):
+        def weave_shared(copy, dtype, into, i0, i1, t0, t1, run=1):
             copy(
-                out=into.bitcast(dtype).rearrange("p (a n h) -> p a n h", a=3, h=2)[:, i0:i1],
-                in_=rows[:].bitcast(dtype)[:, : 6 * T].rearrange("p (a h t) -> p a t h", a=3, h=2)[:, i0:i1, t0:t1, :],
+                out=into.bitcast(dtype).rearrange("p (a c i h) -> p a c h i", a=3, h=2, i=run)[:, i0:i1],
+                in_=rows[:].bitcast(dtype)[:, : 6 * T].rearrange("p (a h c i) -> p a c h i", a=3, h=2, i=run)[:, i0:i1, t0 // run : t1 // run],
             )
 
         def round_shared_quads():
             nc.gpsimd.tensor_copy(
-                out=plane_quads.rearrange("p (n j) -> p n j", j=4), in_=planes[:, : 4 * T].rearrange("p (j n) -> p n j", j=4)
+                out=plane_quads.rearrange("p (c i j) -> p c j i", j=4, i=2),
+                in_=planes[:, : 4 * T].rearrange("p (j c i) -> p c j i", j=4, i=2),
             )
 
         def quantise_slots(first, last):
@@ -220,24 +222,25 @@ def tile_moe_shr_lin_gelu_kernel(tc, xT, w_words, w_scales, b, gate, offs, pos1,
         gather_row(0, 1)
         round_planes(3, 4, nc.scalar.copy)
         gather_plane(3)
-        round_row(0, 0, nc.gpsimd.tensor_copy, 0, T // 2)
-        round_row(0, 0, nc.gpsimd.tensor_copy, T // 2, T)
+        round_row(0, 0, nc.gpsimd.tensor_copy, 0, T // 2, RUN)
+        round_row(0, 0, nc.gpsimd.tensor_copy, T // 2, T, RUN)
         gather_row(0, 0)
         round_planes(2, 3, nc.gpsimd.tensor_copy)
         gather_plane(2)
-        round_row(2, 1, nc.gpsimd.tensor_copy)
+        round_row(2, 1, nc.gpsimd.tensor_copy, run=RUN)
         gather_row(2, 1)
         weave(0)
-        round_row(2, 0, nc.gpsimd.tensor_copy)
+        round_row(2, 0, nc.gpsimd.tensor_copy, run=RUN)
         gather_row(2, 0)
         round_planes(0, 2, nc.gpsimd.tensor_copy)
         gather_plane(1)
         gather_plane(0)
         for h in (1, 0):
-            round_row(LAST, h, nc.gpsimd.tensor_copy)
+            round_row(LAST, h, nc.gpsimd.tensor_copy, run=RUN)
             gather_row(LAST, h)
 
-        weave_shared(nc.gpsimd.tensor_copy, U32, early_quads, 1, 3, 0, EARLY)
+        weave_shared(nc.gpsimd.tensor_copy, U32, early_quads, 1, 3, 0, EARLY, 2)
+        weave_shared(nc.gpsimd.tensor_copy, U32, late_quads[:, 2 * LATE :], 0, 3, EARLY, T, 2)
         round_shared_quads()
         scales = aligned([P, PASSES * (S + T)], U8, "planes")
         early_scale_at, late_scale_at = PASSES * S, PASSES * (S + EARLY)
@@ -248,7 +251,6 @@ def tile_moe_shr_lin_gelu_kernel(tc, xT, w_words, w_scales, b, gate, offs, pos1,
         weave(LAST, 256, 768)
         weave(LAST, 768, S)
         weave_shared(nc.scalar.copy, U32, early_quads, 0, 1, 0, EARLY)
-        weave_shared(nc.scalar.copy, U32, late_quads[:, 2 * LATE :], 2, 3, EARLY, T)
         slots_step(0, WIDE)
         quantise_shared(early_codes[:, : 2 * EARLY], early_quads[:, 4 * EARLY :], early_scale_at)
         for i, a in enumerate((2, 0)):
@@ -257,7 +259,6 @@ def tile_moe_shr_lin_gelu_kernel(tc, xT, w_words, w_scales, b, gate, offs, pos1,
             slots_step(first, first + WIDE)
         slots_step(4 * WIDE, 4 * WIDE + 512)
         slots_step(4 * WIDE + 512, 5 * WIDE)
-        weave_shared(nc.vector.tensor_copy, I32, late_quads[:, 2 * LATE :], 0, 2, EARLY, T)
         quantise_shared(plane_codes, plane_quads[:, : 4 * EARLY], early_scale_at + 2 * EARLY)
         shared_pass(0, PLANE_PASS, plane_codes, early_scale_at + 2 * EARLY, False, False)
         quantise_shared(last_codes, early_quads[:, : 4 * EARLY], early_scale_at + 3 * EARLY)

from contextlib import ExitStack

import concourse.mybir as mybir
from concourse.masks import make_identity

K, T, E, C, N = 2048, 640, 10, 128, 128
S = E * C
P = 128
PASSES = 4
LAST = PASSES - 1
FLOPS = 2 * K * N * (S + T)

PLANE_PASS = 1
ROWS = [(0, 1), (0, 0), (2, 1), (2, 0), (3, 1), (3, 0)]
PLANES = [3, 2, 1, 0]
SLOT_ORDER = (0, 2, 1, 3)
WINDOW = 1712
FIRST_ON_VECTOR = 384
WIDE = 1024
EARLY = 512
LATE = T - EARLY
RUN = 4
FETCHED = 256
BANK = 512

F32 = mybir.dt.float32
BF16 = mybir.dt.bfloat16
U32 = mybir.dt.uint32
I32 = mybir.dt.int32
U16 = mybir.dt.uint16
U8 = mybir.dt.uint8
FP8X4 = mybir.dt.float8_e4m3fn_x4
FP4X4 = mybir.dt.float4_e2m1fn_x4
GELU = mybir.ActivationFunctionType.Gelu_apprx_tanh
COPY = mybir.ActivationFunctionType.Copy
MULT = mybir.AluOpType.mult


def tile_moe_shr_lin_gelu_kernel(tc, xT, w_words, w_scales, b, gate, offs, pos1, pos2, out):
    nc = tc.nc
    with ExitStack() as ctx:
        keep = ctx.enter_context(tc.tile_pool(name="keep", bufs=1))
        psum = ctx.enter_context(tc.psum_pool(name="psum", bufs=1))

        def aligned(shape, dtype, name):
            return keep.tile(shape, dtype, name=name, align_bytes=64)

        offs_t = keep.tile([P, S // 16], U16, name="offs_t")
        pos1_t = keep.tile([P, T // 16], U16, name="pos1_t")
        pos2_t = keep.tile([P, T // 16], U16, name="pos2_t")
        bias = keep.tile([P, E + 1], F32, name="bias")
        gates = keep.tile([P, 2 * T], F32, name="gates")
        turned = keep.tile([P, T], F32, name="turned")
        w_scale = aligned([P, (E + 1) * PASSES * N], U8, "w_scale")
        y = keep.tile([P, S], F32, name="y")
        ys = keep.tile([P, T], F32, name="ys")
        w_codes = [aligned([P, (E + 1) * 4 * N], U8, f"w_codes{v}") for v in range(2)]
        slot_quads = aligned([P, PASSES * 4 * S], BF16, "slot_quads")
        slot_codes = aligned([P, PASSES * S], U32, "slot_codes")
        early_codes = aligned([P, 2 * EARLY], U32, "early_codes")
        plane_codes = slot_codes[:, LAST * S - 2 * C : LAST * S + 2 * C]
        last_codes = slot_codes[:, LAST * S + 2 * C : LAST * S + 6 * C]
        late_codes = slot_codes[:, LAST * S + 6 * C :]
        planes = aligned([P, 3 * T + WINDOW], BF16, "planes")
        rows = aligned([P, 2 * ((len(ROWS) - 1) * T + WINDOW)], BF16, "rows")
        raw_planes = slot_quads[:, 4 * S : 2 * 4 * S].bitcast(F32)
        shared_words = aligned([P, 6 * EARLY + 2 * T + 6 * LATE], U32, "shared_words")
        early_quads = shared_words[:, : 6 * EARLY].bitcast(BF16)
        last_words = shared_words[:, 6 * EARLY :]
        gathered = [aligned([P, 2 * S], U32, f"gathered{a}") for a in range(PASSES)]
        plane_quads = last_words[:, : 2 * T].bitcast(BF16)
        late_quads = last_words[:, 2 * EARLY : 2 * EARLY + 8 * LATE]
        raw_last = shared_words[:, 6 * EARLY - T : 6 * EARLY + T].bitcast(F32).rearrange("p (e t) -> p e t", e=2)

        def row_at(a, h):
            return T * (len(ROWS) - 1 - ROWS.index((a, h)))

        def plane_at(j):
            return T * (len(PLANES) - 1 - PLANES.index(j))

        warm = keep.tile([P, 8], F32, name="warm")
        nc.gpsimd.memset(warm[:], 0.0)
        nc.scalar.activation(out=ys[:, :8], in_=warm[:], func=GELU)
        nc.vector.memset(rows[:].bitcast(I32)[:, len(ROWS) * T :], 0)
        nc.vector.memset(planes[:].bitcast(I32)[:, 2 * T :], 0)
        nc.vector.memset(w_scale[:].bitcast(I32), 0)

        x_by_pass = xT.rearrange("(a p j) t -> a p j t", p=P, j=4)
        raw = {}

        def load_row(a, h, cuts=(0, T)):
            if (a, h) == (2, 1):
                raw[a, h] = slot_quads[:, : 4 * T].bitcast(F32).rearrange("p (e t) -> p e t", e=2)
            elif (a, h) == (LAST, 0):
                raw[a, h] = raw_last
            else:
                raw[a, h] = aligned([P, 2, T], F32, f"raw{a}_{h}")
            for t0, t1 in zip(cuts, cuts[1:]):
                nc.sync.dma_start(raw[a, h][:, :, t0:t1], x_by_pass[a][:, 2 * h : 2 * h + 2, t0:t1])

        def load_planes(j0, j1):
            nc.sync.dma_start(
                raw_planes[:, T * j0 : T * j1], x_by_pass[PLANE_PASS][:, j0:j1, :].rearrange("p j t -> p (j t)")
            )

        def preload_weights_and_combine_inputs():
            for q in range(4):
                nc.sync.dma_start(
                    w_scale[32 * q : 32 * q + 4, :].bitcast(I32).rearrange("r (i n) -> r i n", n=N // 4),
                    w_scales.bitcast(I32)[:, :, 4 * q : 4 * q + 4, :].rearrange("e a r n -> r (e a) n"),
                )
            for v in range(2):
                nc.sync.dma_start(
                    w_codes[v][:].bitcast(I32).rearrange("p (i n) -> p i n", n=N // 2),
                    w_words.bitcast(I32).rearrange("e (u v) p n -> v p (e u) n", v=2)[v],
                )
            nc.sync.dma_start(bias[:], b)
            nc.sync.dma_start(pos1_t[:], pos1)
            nc.sync.dma_start(pos2_t[:], pos2)
            nc.sync.dma_start(gates[:].rearrange("p (g t) -> p g t", g=2), gate.rearrange("g p t -> p g t"))

        def round_row(a, h, copy, t0=0, t1=T, run=1):
            at = 2 * row_at(a, h)
            copy(
                out=rows[:, at + 2 * t0 : at + 2 * t1].rearrange("p (c i e) -> p c e i", e=2, i=run),
                in_=raw[a, h][:, :, t0:t1].rearrange("p e (c i) -> p c e i", i=run),
            )

        def round_planes(j0, j1, copy):
            copy(out=planes[:, T * j0 : T * j1], in_=raw_planes[:, T * j0 : T * j1])

        def gather_plane(j):
            h, e = divmod(j, 2)
            nc.scalar.activation(
                out=gathered[PLANE_PASS][:, :].bitcast(BF16)[:, 2 * S * h : 2 * S * (h + 1)].rearrange("p (n e) -> p n e", e=2)[:, :, e],
                in_=planes[:, plane_at(j) : plane_at(j) + WINDOW].indirect(offs_t[:]),
                func=COPY,
            )

        def gather_row(a, h):
            at = row_at(a, h)
            nc.vector.tensor_copy(
                gathered[a][:, S * h : S * (h + 1)], rows[:].bitcast(U32)[:, at : at + WINDOW].indirect(offs_t[:])
            )

        def weave(a, s0=0, s1=S):
            at = S * SLOT_ORDER.index(a)
            nc.scalar.copy(
                out=slot_quads[:].bitcast(U32)[:, 2 * (at + s0) : 2 * (at + s1)].rearrange("p (n h) -> p n h", h=2),
                in_=gathered[a][:, : 2 * S].rearrange("p (h n) -> p n h", h=2)[:, s0:s1, :],
            )

        def weave_shared(copy, dtype, into, i0, i1, t0, t1, run=1):
            copy(
                out=into.bitcast(dtype).rearrange("p (a c i h) -> p a c h i", a=3, h=2, i=run)[:, i0:i1],
                in_=rows[:].bitcast(dtype)[:, : 6 * T].rearrange("p (a h c i) -> p a c h i", a=3, h=2, i=run)[:, i0:i1, t0 // run : t1 // run],
            )

        def round_shared_quads():
            nc.gpsimd.tensor_copy(
                out=plane_quads.rearrange("p (c i j) -> p c j i", j=4, i=2),
                in_=planes[:, : 4 * T].rearrange("p (j c i) -> p c j i", j=4, i=2),
            )

        def quantise_slots(first, last):
            nc.vector.quantize_mx(
                out=slot_codes[:, first:last].bitcast(FP8X4), scales=scales[:, first:last], in_=slot_quads[:, 4 * first : 4 * last]
            )

        def quantise_shared(codes, quads, scale_at):
            nc.vector.quantize_mx(out=codes.bitcast(FP8X4), scales=scales[:, scale_at : scale_at + codes.shape[1]], in_=quads)

        def multiply(sums, e, a, codes, scale_at, width, start, stop):
            i = e * PASSES + a
            weights, at = w_codes[a % 2], i // 2
            nc.tensor.matmul_mx(
                out=sums,
                lhsT=weights[:, at * 2 * N : (at + 1) * 2 * N].bitcast(FP4X4),
                lhsT_scale=w_scale[:, i * N : (i + 1) * N],
                rhs=codes.bitcast(FP8X4),
                rhs_scale=scales[:, scale_at : scale_at + width],
                start=start,
                stop=stop,
            )

        banks = [psum.tile([P, BANK], F32, name=f"bank{i}") for i in range(E // 2 + 2)]

        def slots_step(first, last):
            quantise_slots(first, last)
            done = [(SLOT_ORDER[at // S], at % S // C, at) for at in range(first, last, C)]
            for a, e, at in sorted(done, key=lambda pass_of: pass_of[0] != LAST):
                sums = banks[e // 2][:, e % 2 * C : (e % 2 + 1) * C]
                multiply(sums, e, a, slot_codes[:, at : at + C], at, C, a == SLOT_ORDER[0] and e % 2 == 0, a == LAST and e % 2 == 1)
            for a, e, at in done:
                if a == LAST:
                    sums = banks[e // 2][:, e % 2 * C : (e % 2 + 1) * C]
                    nc.scalar.activation(out=y[:, e * C : (e + 1) * C], in_=sums, func=GELU, bias=bias[:, e : e + 1])

        def shared_pass(lot, a, codes, scale_at, start, stop):
            t0, t1 = ((0, EARLY), (EARLY, T))[lot]
            sums = banks[E // 2 + lot][:, : t1 - t0]
            multiply(sums, E, a, codes, scale_at, t1 - t0, start, stop)
            if stop:
                nc.scalar.activation(out=ys[:, t0:t1], in_=sums, func=GELU, bias=bias[:, E : E + 1])

        load_row(0, 1)
        nc.sync.dma_start(offs_t[:], offs)
        load_planes(3, 4)
        load_row(0, 0, (0, T // 2, T))
        round_row(0, 1, nc.vector.tensor_copy, 0, FIRST_ON_VECTOR)
        round_row(0, 1, nc.scalar.copy, FIRST_ON_VECTOR, T)
        identity = aligned([P, P], F32, "raw0_1")
        make_identity(nc, identity[:])
        load_planes(2, 3)
        load_row(2, 1)
        load_row(2, 0)
        load_planes(0, 2)
        for a, h in ROWS[4:]:
            load_row(a, h)
        preload_weights_and_combine_inputs()

        gather_row(0, 1)
        round_planes(3, 4, nc.scalar.copy)
        gather_plane(3)
        round_row(0, 0, nc.gpsimd.tensor_copy, 0, T // 2, RUN)
        round_row(0, 0, nc.gpsimd.tensor_copy, T // 2, T, RUN)
        gather_row(0, 0)
        round_planes(2, 3, nc.gpsimd.tensor_copy)
        gather_plane(2)
        round_row(2, 1, nc.gpsimd.tensor_copy, run=RUN)
        gather_row(2, 1)
        weave(0)
        round_row(2, 0, nc.gpsimd.tensor_copy, run=RUN)
        gather_row(2, 0)
        round_planes(0, 2, nc.gpsimd.tensor_copy)
        gather_plane(1)
        gather_plane(0)
        for h in (1, 0):
            round_row(LAST, h, nc.gpsimd.tensor_copy, run=RUN)
            gather_row(LAST, h)

        weave_shared(nc.gpsimd.tensor_copy, U32, early_quads, 1, 3, 0, EARLY, 2)
        weave_shared(nc.gpsimd.tensor_copy, U32, late_quads[:, 2 * LATE :], 0, 3, EARLY, T, 2)
        round_shared_quads()
        scales = aligned([P, PASSES * (S + T)], U8, "planes")
        early_scale_at, late_scale_at = PASSES * S, PASSES * (S + EARLY)
        weave(2)
        weave(1, 0, 512)
        weave(1, 512, S)
        weave(LAST, 0, 256)
        weave(LAST, 256, 768)
        weave(LAST, 768, S)
        weave_shared(nc.scalar.copy, U32, early_quads, 0, 1, 0, EARLY)
        slots_step(0, WIDE)
        quantise_shared(early_codes[:, : 2 * EARLY], early_quads[:, 4 * EARLY :], early_scale_at)
        for i, a in enumerate((2, 0)):
            shared_pass(0, a, early_codes[:, i * EARLY : (i + 1) * EARLY], early_scale_at + i * EARLY, i == 0, False)
        for first in range(WIDE, 4 * WIDE, WIDE):
            slots_step(first, first + WIDE)
        slots_step(4 * WIDE, 4 * WIDE + 512)
        slots_step(4 * WIDE + 512, 5 * WIDE)
        quantise_shared(plane_codes, plane_quads[:, : 4 * EARLY], early_scale_at + 2 * EARLY)
        shared_pass(0, PLANE_PASS, plane_codes, early_scale_at + 2 * EARLY, False, False)
        quantise_shared(last_codes, early_quads[:, : 4 * EARLY], early_scale_at + 3 * EARLY)
        shared_pass(0, LAST, last_codes, early_scale_at + 3 * EARLY, False, True)
        quantise_shared(late_codes, late_quads.bitcast(BF16), late_scale_at)
        for i, a in enumerate((1, 3, 2, 0)):
            shared_pass(1, a, late_codes[:, i * LATE : (i + 1) * LATE], late_scale_at + i * LATE, i == 0, i == LAST)

        first_choice = aligned([P, T], F32, "first_choice")
        second_choice = aligned([P, T], F32, "raw0_0")
        total = aligned([P, T], F32, "raw2_0")
        stores = ((0, 256), (256, EARLY), (EARLY, T))
        sums = []
        fetched = aligned([P, FETCHED], F32, "raw3_1")
        nc.scalar.activation(out=fetched[:], in_=y[:].indirect(pos2_t[:, : FETCHED // 16]), func=COPY)
        for i, (t0, t1) in enumerate(((0, 256), (256, EARLY), (EARLY, T))):
            nc.vector.tensor_tensor(first_choice[:, t0:t1], y[:].indirect(pos1_t[:, t0 // 16 : t1 // 16]), gates[:, t0:t1], MULT)
            bank = psum.tile([P, BANK], F32, name=("bank7", "bank0", "bank1")[i])
            for t in range(t0, t1, P):
                cols = slice(t - t0, t - t0 + P)
                nc.tensor.matmul(bank[:, cols], ys[:, t : t + P], identity[:], start=True, stop=False, is_transpose=True)
                nc.tensor.matmul(bank[:, cols], first_choice[:, t : t + P], identity[:], start=False, stop=True, is_transpose=True)
            nc.scalar.copy(out=turned[:, t0:t1], in_=bank[:, : t1 - t0])
        for i, (t0, t1) in enumerate(stores):
            sums.append(psum.tile([P, BANK], F32, name=f"bank{2 + i}"))
            for t in range(t0, t1, P):
                nc.tensor.transpose(sums[i][:, t - t0 : t - t0 + P], turned[:, t : t + P], identity[:])
        nc.vector.tensor_tensor(second_choice[:, :FETCHED], fetched[:], gates[:, T : T + FETCHED], MULT)
        nc.vector.tensor_tensor(second_choice[:, FETCHED:], y[:].indirect(pos2_t[:, FETCHED // 16 :]), gates[:, T + FETCHED :], MULT)
        for i, (t0, t1) in enumerate(stores):
            nc.vector.tensor_add(total[:, t0:t1], sums[i][:, : t1 - t0], second_choice[:, t0:t1])
            nc.sync.dma_start(out[:, t0:t1], total[:, t0:t1])
